import numpy as np
import ml_dtypes


def mxq(x, axis, fmt="e4m3"):
    dtype, down = {"e4m3": (ml_dtypes.float8_e4m3fn, 7), "e5m2": (ml_dtypes.float8_e5m2, 14)}[fmt]
    v = np.moveaxis(np.asarray(x, np.float32).astype(ml_dtypes.bfloat16).astype(np.float64), axis, -1)
    blocks = v.reshape(v.shape[:-1] + (-1, 32))
    amax = np.abs(blocks).max(-1, keepdims=True)
    byte = np.maximum(np.where(amax > 0, np.frexp(amax)[1] - 1 + 127, 0) - down, 1)
    scale = np.exp2(byte - 127.0)
    codes = (blocks / scale).astype(np.float32).astype(dtype).astype(np.float64)
    return np.moveaxis((codes * scale).reshape(v.shape), -1, axis)


WIDE = False


def mx_kscale(k):
    if not WIDE:
        return np.ones(k)
    levels = np.array([10, -10, 5, -5, 0])
    if k % 512:
        return np.exp2(np.random.permutation(np.resize(levels, k // 32))).repeat(32)
    a = np.empty((k // 512, 16))
    for p in range(k // 512):
        a[p, :8] = np.random.permutation(np.resize(levels, 8))
        for g in range(8):
            far = levels[np.abs(levels - a[p, g]) >= 10]
            a[p, g + 8] = far[np.random.randint(len(far))]
    return np.exp2(a.ravel()).repeat(32)


def f64(x):
    return np.asarray(x).astype(np.float64)


def striped(idx):
    return np.tile(idx.reshape(-1, 16).T, (8, 1)).astype(np.uint16)


def unstriped(offs):
    return offs[:16].T.reshape(-1).astype(np.int64)


def pack_weight(w):
    k, n = w.shape
    w = f64(np.asarray(w, np.float32).astype(ml_dtypes.bfloat16)).reshape(k // 32, 32, n)
    amax = np.abs(w).max(1)
    byte = np.clip(np.where(amax > 0, np.frexp(amax)[1] - 1 + 127 - 7, 1), 1, 254)
    scaled = (w * np.exp2(127.0 - byte)[:, None, :]).reshape(k, n).astype(np.float32)
    words = np.ascontiguousarray(scaled.reshape(k // 512, 128, 4, n).transpose(0, 1, 3, 2)).astype(ml_dtypes.float8_e4m3fn).view(np.uint8)
    return words, np.ascontiguousarray(byte.astype(np.uint8).reshape(k // 512, 16, n))


def unpack_weight(words, scales):
    g, p, n, _ = words.shape
    vals = np.ascontiguousarray(words).view(ml_dtypes.float8_e4m3fn).astype(np.float64) * np.repeat(np.exp2(scales.astype(np.float64) - 127.0), 8, axis=1)[..., None]
    return vals.transpose(0, 1, 3, 2).reshape(g * 512, n)


def relu(v):
    return np.maximum(v, 0.0)


K, T, S, H, R, G, W = 1024, 2048, 512, 512, 512, 256, 512
P = 2 ** 7


def setup_inputs():
    n = np.random.standard_normal
    s = mx_kscale(K)[:, None]
    u = mx_kscale(H)
    packed_xT = pack_weight(n((K, T)) * s)
    return {
        "x_words": packed_xT[0],
        "x_scales": packed_xT[1],
        "w1": (n((K, H)) / np.sqrt(K) / s * u).astype(np.float32),
        "kn1": (n((H, G)) / np.sqrt(H) / u[:, None]).astype(np.float32),
        "frac1": (np.tile(np.random.uniform(0.0, 1.0, R), (P, 1))).astype(np.float32),
        "kn2": (n((H, W)) / np.sqrt(H) / u[:, None]).astype(np.float32),
        "frac2": (np.tile(np.random.uniform(0.0, 1.0, R), (P, 1))).astype(np.float32),
        "true": (n((S, R))).astype(np.float32),
        "offs": striped(np.random.permutation(T)[:S]),
        "left1": striped(np.random.permutation(np.concatenate([np.arange(G), np.random.randint(0, G, R - G)]))),
        "right1": striped(np.random.permutation(np.concatenate([np.arange(G), np.random.randint(0, G, R - G)]))),
        "left2": striped(np.random.randint(0, W, R)),
        "right2": striped(np.random.randint(0, W, R)),
    }


def reference(x_words, x_scales, w1, kn1, frac1, kn2, frac2, true, offs, left1, right1, left2, right2):
    xq = unpack_weight(x_words, x_scales)[:, unstriped(offs)]
    h = relu(mxq(f64(w1), 0, "e4m3").T @ xq)
    hq = mxq(h, 0, "e4m3")
    kn1q = mxq(f64(kn1), 0, "e4m3")
    y1 = hq.T @ kn1q
    gl1 = y1[:, unstriped(left1)]
    kn2q = mxq(f64(kn2), 0, "e4m3")
    y2 = hq.T @ kn2q
    gl2 = y2[:, unstriped(left2)]
    fc = gl1 + f64(frac1)[:1] * (y1[:, unstriped(right1)] - gl1) + gl2 + f64(frac2)[:1] * (y2[:, unstriped(right2)] - gl2)
    return np.abs(f64(true) - fc)

@@ -1,0 +1,236 @@
+from contextlib import ExitStack
+
+import concourse.mybir as mybir
+from concourse.masks import make_identity
+
+K, T, S, H, R, G, W = 1024, 2048, 512, 512, 512, 256, 512
+FLOPS = 2 * K * H * S + 2 * H * S * (G + W)
+
+F32 = mybir.dt.float32
+BF16 = mybir.dt.bfloat16
+U32 = mybir.dt.uint32
+I32 = mybir.dt.int32
+U16 = mybir.dt.uint16
+U8 = mybir.dt.uint8
+FP8X4 = mybir.dt.float8_e4m3fn_x4
+ACT = mybir.ActivationFunctionType
+ALU = mybir.AluOpType
+
+P = 128
+PACK = 4
+K_PASS = P * PACK
+PASSES = K // K_PASS
+BLOCKS = S // P
+CHUNKS = R // P
+HALF = S // 2
+WINDOW = R + 16
+LATE = 2
+
+
+def tile_picked_ynhits_err_p_kernel(
+    tc, x_words, x_scales, w1, kn1, frac1, kn2, frac2, true, offs, left1, right1, left2, right2, out
+):
+    nc = tc.nc
+    with ExitStack() as ctx:
+        keep = ctx.enter_context(tc.tile_pool(name="keep", bufs=1))
+        psum = ctx.enter_context(tc.psum_pool(name="psum", bufs=1))
+
+        def held(shape, dtype, name):
+            return keep.tile(shape, dtype, name=name, tag=name, align_bytes=64)
+
+        def load_list(src, name):
+            lst = held([P, R // 16], U16, name)
+            nc.sync.dma_start(lst[:], src)
+            return lst
+
+        def load_rows(src, width, name):
+            raw = held([P, PACK, width], F32, name)
+            nc.sync.dma_start(raw[:], src.rearrange("(p j) n -> p j n", j=PACK))
+            return raw
+
+        def quantize(grouped, width, name):
+            codes = held([P, width], U32, name + "_codes")
+            scales = held([P, width], U8, name + "_scales")
+            nc.vector.quantize_mx(out=codes[:].bitcast(FP8X4), scales=scales[:], in_=grouped[:])
+            return codes, scales
+
+        x_scale_rows = held([P, T], U8, "x_scale_rows")
+        nc.gpsimd.memset(x_scale_rows[:].bitcast(I32), 0)
+        identity = held([P, P], F32, "identity")
+        make_identity(nc, identity[:])
+
+        offs_t = load_list(offs, "offs_t")
+        w1_raw = [load_rows(w1[:K_PASS, :], H, "w1_raw0")]
+        for q in range(4):
+            nc.sync.dma_start(
+                x_scale_rows[32 * q : 32 * q + 4 * PASSES, :].bitcast(I32),
+                x_scales[:, 4 * q : 4 * q + 4, :].bitcast(I32),
+            )
+        w1_raw.append(load_rows(w1[K_PASS:, :], H, "w1_raw1"))
+        x_table = []
+        for o in range(PASSES):
+            words = held([P, T], U32, "x_table%d" % o)
+            nc.sync.dma_start(words[:].bitcast(I32), x_words[o].rearrange("p n t -> p (n t)").bitcast(I32))
+            x_table.append(words)
+        kn1_raw = load_rows(kn1, G, "kn1_raw")
+        right1_t = load_list(right1, "right1_t")
+        frac1_t = held([P, R], F32, "frac1_t")
+        nc.sync.dma_start(frac1_t[:], frac1)
+        left1_t = load_list(left1, "left1_t")
+        kn2_raw = load_rows(kn2, W, "kn2_raw")
+        left2_t = load_list(left2, "left2_t")
+        right2_t = load_list(right2, "right2_t")
+        frac2_t = held([P, R], F32, "frac2_t")
+        nc.sync.dma_start(frac2_t[:], frac2)
+        true_t = held([P, BLOCKS, R], F32, "true_t")
+        nc.sync.dma_start(true_t[:], true.rearrange("(b p) r -> p b r", p=P))
+
+        knots1 = [held([P, WINDOW], F32, "knots1_%d" % b) for b in range(BLOCKS)]
+        knots2 = [held([P, WINDOW], F32, "knots2_%d" % b) for b in range(BLOCKS)]
+        for b in range(BLOCKS):
+            nc.vector.memset(knots1[b][:, G:], 0.0)
+            nc.vector.memset(knots2[b][:, W:], 0.0)
+
+        x_scale = held([P, S], U8, "x_scale")
+        nc.vector.tensor_copy(x_scale[:], x_scale_rows[:].indirect(offs_t[:]))
+
+        w1_q = []
+        for o in range(PASSES):
+            grouped = held([P, PACK * H], BF16, "w1_grouped%d" % o)
+            dst = grouped[:].rearrange("p (t m j) -> p m j t", t=PACK, j=PACK)
+            src = w1_raw[o][:].rearrange("p j (m t) -> p m j t", t=PACK)
+            if o == 0:
+                nc.scalar.activation(dst, src, ACT.Copy)
+            else:
+                nc.vector.tensor_copy(dst, src)
+            w1_q.append(quantize(grouped, H, "w1_%d" % o))
+
+        x_codes = [[None, None] for o in range(PASSES)]
+        for o in range(PASSES):
+            for half in range(2):
+                picked = held([P, HALF], U32, "x_codes%d_%d" % (o, half))
+                cols = slice(half * HALF // 16, (half + 1) * HALF // 16)
+                nc.vector.tensor_copy(picked[:], x_table[o][:].indirect(offs_t[:, cols]))
+                x_codes[o][half] = picked
+
+        def interleave(raw, width, name, engine_copy):
+            grouped = held([P, PACK * width], BF16, name)
+            engine_copy(
+                grouped[:].rearrange("p (c i j) -> p c j i", i=PACK, j=PACK),
+                raw[:].rearrange("p j (c i) -> p c j i", i=PACK),
+            )
+            return grouped
+
+        kn1_q = quantize(interleave(kn1_raw, G, "kn1_grouped", nc.vector.tensor_copy), G, "kn1")
+
+        def knots(h_q, kn_q, width, window):
+            acc = psum.tile([P, W], F32, name="work_bank", tag="work_bank", bufs=4)
+            nc.tensor.matmul_mx(
+                out=acc[:, :width],
+                lhsT=h_q[0][:].bitcast(FP8X4),
+                lhsT_scale=h_q[1][:],
+                rhs=kn_q[0][:].bitcast(FP8X4),
+                rhs_scale=kn_q[1][:],
+                start=True,
+                stop=True,
+            )
+            nc.scalar.activation(window[:, :width], acc[:, :width], ACT.Copy, scale=-1.0)
+
+        h_q = []
+        for b in range(BLOCKS):
+            half, first = divmod(b * P, HALF)
+            acc = psum.tile([P, PACK, P], F32, name="block_bank", tag="block_bank", bufs=BLOCKS)
+            for o in range(PASSES):
+                for t in range(PACK):
+                    nc.tensor.matmul_mx(
+                        out=acc[:, t, :],
+                        lhsT=w1_q[o][0][:, t * P : (t + 1) * P].bitcast(FP8X4),
+                        lhsT_scale=w1_q[o][1][:, t * P : (t + 1) * P],
+                        rhs=x_codes[o][half][:, first : first + P].bitcast(FP8X4),
+                        rhs_scale=x_scale[4 * o :, b * P : (b + 1) * P],
+                        start=(o == 0 and t == 0),
+                        stop=(o == PASSES - 1 and t == PACK - 1),
+                    )
+            hidden = held([P, PACK * P], BF16, "hidden%d" % b)
+            nc.scalar.activation(
+                hidden[:].rearrange("p (n t) -> p n t", t=PACK), acc[:].rearrange("p t n -> p n t"), ACT.Relu
+            )
+            h_q.append(quantize(hidden, P, "h%d" % b))
+            knots(h_q[b], kn1_q, G, knots1[b])
+
+        rest1 = held([P, R], F32, "rest1")
+        nc.vector.tensor_scalar(rest1[:], frac1_t[:], -1.0, 1.0, op0=ALU.mult, op1=ALU.add)
+
+        def add_turned(bank, term, start, stop):
+            for c in range(CHUNKS):
+                cols = slice(c * P, (c + 1) * P)
+                nc.tensor.matmul(
+                    bank[:, cols], term[:, cols], identity[:], is_transpose=True,
+                    start=(start and c == 0), stop=(stop and c == CHUNKS - 1),
+                )
+
+        def weighted(window, lst, weight, name):
+            term = held([P, R], F32, name)
+            nc.vector.tensor_tensor(term[:], window[:].indirect(lst[:]), weight[:], ALU.mult)
+            return term
+
+        sums = []
+        for b in range(BLOCKS):
+            bank = psum.tile([P, R], F32, name="block_bank", tag="block_bank", bufs=BLOCKS)
+            add_turned(bank, weighted(knots1[b], right1_t, frac1_t, "right1_term%d" % b), True, False)
+            add_turned(bank, weighted(knots1[b], left1_t, rest1, "left1_term%d" % b), False, False)
+            sums.append(bank)
+
+        kn2_q = quantize(
+            interleave(kn2_raw, W, "kn2_grouped", lambda dst, src: nc.scalar.activation(dst, src, ACT.Copy)), W, "kn2"
+        )
+        for b in range(BLOCKS):
+            knots(h_q[b], kn2_q, W, knots2[b])
+        rest2 = held([P, R], F32, "kn2_codes")
+        nc.scalar.activation(rest2[:], frac2_t[:], ACT.Copy, scale=-1.0, bias=1.0)
+        for b in range(BLOCKS):
+            add_turned(sums[b], true_t[:, b, :], False, False)
+
+        def turn_back(b, func):
+            turned = held([P, R], F32, "turned%d" % b)
+            nc.scalar.activation(turned[:], sums[b][:], func)
+            back = psum.tile([P, R], F32, name="work_bank", tag="work_bank", bufs=4)
+            for c in range(CHUNKS):
+                cols = slice(c * P, (c + 1) * P)
+                nc.tensor.transpose(back[:, cols], turned[:, cols], identity[:])
+            return back
+
+        partial = {}
+        for b in range(BLOCKS):
+            late = b >= BLOCKS - LATE
+            add_turned(sums[b], weighted(knots2[b], right2_t, frac2_t, "right2_term%d" % b), False, late)
+            if late:
+                partial[b] = turn_back(b, ACT.Copy)
+
+        for b in range(BLOCKS - LATE):
+            add_turned(sums[b], weighted(knots2[b], left2_t, rest2, "left2_term%d" % b), False, True)
+            back = turn_back(b, ACT.Abs)
+            result = held([P, R], F32, "result%d" % b)
+            nc.scalar.copy(result[:], back[:])
+            nc.sync.dma_start(out[b * P : (b + 1) * P, :], result[:])
+
+        def gather_left(b, cols, name):
+            term = held([P, cols.stop - cols.start], F32, name)
+            lst = left2_t[:, cols.start // 16 : cols.stop // 16]
+            nc.vector.tensor_tensor(term[:], knots2[b][:].indirect(lst), rest2[:, cols], ALU.mult)
+            return term
+
+        def finish(b, cols, term, total_name, result_name):
+            total = held([P, cols.stop - cols.start], F32, total_name)
+            nc.vector.tensor_tensor(total[:], partial[b][:, cols], term[:], ALU.add)
+            result = held([P, cols.stop - cols.start], F32, result_name)
+            nc.scalar.activation(result[:], total[:], ACT.Abs)
+            nc.sync.dma_start(out[b * P : (b + 1) * P, cols], result[:])
+
+        whole, low, high = slice(0, R), slice(0, R // 2), slice(R // 2, R)
+        term2 = gather_left(2, whole, "left2_term2")
+        term3_low = gather_left(3, low, "left2_term3_low")
+        finish(2, whole, term2, "total2", "turned1")
+        term3_high = gather_left(3, high, "left2_term3_high")
+        finish(3, low, term3_low, "total3_low", "result3_low")
+        finish(3, high, term3_high, "total3_high", "result3_high")

@@ -24,7 +24,7 @@ BLOCKS = S // P
 CHUNKS = R // P
 HALF = S // 2
 WINDOW = R + 16
-LATE = 2
+LAST = BLOCKS - 1
 
 
 def tile_picked_ynhits_err_p_kernel(
@@ -97,8 +97,8 @@ def tile_picked_ynhits_err_p_kernel(
         w1_q = []
         for o in range(PASSES):
             grouped = held([P, PACK * H], BF16, "w1_grouped%d" % o)
-            dst = grouped[:].rearrange("p (t m j) -> p m j t", t=PACK, j=PACK)
-            src = w1_raw[o][:].rearrange("p j (m t) -> p m j t", t=PACK)
+            dst = grouped[:].rearrange("p (t m j) -> p m t j", t=PACK, j=PACK)
+            src = w1_raw[o][:].rearrange("p j (m t) -> p m t j", t=PACK)
             if o == 0:
                 nc.scalar.activation(dst, src, ACT.Copy)
             else:
@@ -121,9 +121,9 @@ def tile_picked_ynhits_err_p_kernel(
             )
             return grouped
 
-        kn1_q = quantize(interleave(kn1_raw, G, "kn1_grouped", nc.vector.tensor_copy), G, "kn1")
+        kn1_grouped = interleave(kn1_raw, G, "kn1_grouped", nc.vector.tensor_copy)
 
-        def knots(h_q, kn_q, width, window):
+        def knots(h_q, kn_q, width, window, on_vector=False):
             acc = psum.tile([P, W], F32, name="work_bank", tag="work_bank", bufs=4)
             nc.tensor.matmul_mx(
                 out=acc[:, :width],
@@ -134,7 +134,10 @@ def tile_picked_ynhits_err_p_kernel(
                 start=True,
                 stop=True,
             )
-            nc.scalar.activation(window[:, :width], acc[:, :width], ACT.Copy, scale=-1.0)
+            if on_vector:
+                nc.vector.tensor_scalar_mul(window[:, :width], acc[:, :width], -1.0)
+            else:
+                nc.scalar.activation(window[:, :width], acc[:, :width], ACT.Copy, scale=-1.0)
 
         h_q = []
         for b in range(BLOCKS):
@@ -156,10 +159,20 @@ def tile_picked_ynhits_err_p_kernel(
                 hidden[:].rearrange("p (n t) -> p n t", t=PACK), acc[:].rearrange("p t n -> p n t"), ACT.Relu
             )
             h_q.append(quantize(hidden, P, "h%d" % b))
-            knots(h_q[b], kn1_q, G, knots1[b])
+            if b == 0:
+                kn1_q = quantize(kn1_grouped, G, "kn1")
+            knots(h_q[b], kn1_q, G, knots1[b], on_vector=(b == 0))
 
         rest1 = held([P, R], F32, "rest1")
         nc.vector.tensor_scalar(rest1[:], frac1_t[:], -1.0, 1.0, op0=ALU.mult, op1=ALU.add)
+
+        kn2_q = quantize(
+            interleave(kn2_raw, W, "kn2_grouped", lambda dst, src: nc.scalar.activation(dst, src, ACT.Copy)), W, "kn2"
+        )
+        for b in range(BLOCKS):
+            knots(h_q[b], kn2_q, W, knots2[b])
+        rest2 = held([P, R], F32, "rest2")
+        nc.scalar.activation(rest2[:], frac2_t[:], ACT.Copy, scale=-1.0, bias=1.0)
 
         def add_turned(bank, term, start, stop):
             for c in range(CHUNKS):
@@ -179,17 +192,9 @@ def tile_picked_ynhits_err_p_kernel(
             bank = psum.tile([P, R], F32, name="block_bank", tag="block_bank", bufs=BLOCKS)
             add_turned(bank, weighted(knots1[b], right1_t, frac1_t, "right1_term%d" % b), True, False)
             add_turned(bank, weighted(knots1[b], left1_t, rest1, "left1_term%d" % b), False, False)
+            add_turned(bank, true_t[:, b, :], False, b == LAST)
             sums.append(bank)
 
-        kn2_q = quantize(
-            interleave(kn2_raw, W, "kn2_grouped", lambda dst, src: nc.scalar.activation(dst, src, ACT.Copy)), W, "kn2"
-        )
-        for b in range(BLOCKS):
-            knots(h_q[b], kn2_q, W, knots2[b])
-        rest2 = held([P, R], F32, "kn2_codes")
-        nc.scalar.activation(rest2[:], frac2_t[:], ACT.Copy, scale=-1.0, bias=1.0)
-        for b in range(BLOCKS):
-            add_turned(sums[b], true_t[:, b, :], False, False)
 
         def turn_back(b, func):
             turned = held([P, R], F32, "turned%d" % b)
@@ -200,37 +205,29 @@ def tile_picked_ynhits_err_p_kernel(
                 nc.tensor.transpose(back[:, cols], turned[:, cols], identity[:])
             return back
 
-        partial = {}
-        for b in range(BLOCKS):
-            late = b >= BLOCKS - LATE
-            add_turned(sums[b], weighted(knots2[b], right2_t, frac2_t, "right2_term%d" % b), False, late)
-            if late:
-                partial[b] = turn_back(b, ACT.Copy)
+        partial = turn_back(LAST, ACT.Copy)
 
-        for b in range(BLOCKS - LATE):
+        for b in range(LAST):
+            add_turned(sums[b], weighted(knots2[b], right2_t, frac2_t, "right2_term%d" % b), False, False)
             add_turned(sums[b], weighted(knots2[b], left2_t, rest2, "left2_term%d" % b), False, True)
             back = turn_back(b, ACT.Abs)
             result = held([P, R], F32, "result%d" % b)
             nc.scalar.copy(result[:], back[:])
             nc.sync.dma_start(out[b * P : (b + 1) * P, :], result[:])
 
-        def gather_left(b, cols, name):
-            term = held([P, cols.stop - cols.start], F32, name)
+        halves = [slice(0, R // 2), slice(R // 2, R)]
+        right_term = weighted(knots2[LAST], right2_t, frac2_t, "right2_term%d" % LAST)
+        left_terms = []
+        for i, cols in enumerate(halves):
+            term = held([P, R // 2], F32, "left2_half%d" % i)
             lst = left2_t[:, cols.start // 16 : cols.stop // 16]
-            nc.vector.tensor_tensor(term[:], knots2[b][:].indirect(lst), rest2[:, cols], ALU.mult)
-            return term
-
-        def finish(b, cols, term, total_name, result_name):
-            total = held([P, cols.stop - cols.start], F32, total_name)
-            nc.vector.tensor_tensor(total[:], partial[b][:, cols], term[:], ALU.add)
-            result = held([P, cols.stop - cols.start], F32, result_name)
-            nc.scalar.activation(result[:], total[:], ACT.Abs)
-            nc.sync.dma_start(out[b * P : (b + 1) * P, cols], result[:])
-
-        whole, low, high = slice(0, R), slice(0, R // 2), slice(R // 2, R)
-        term2 = gather_left(2, whole, "left2_term2")
-        term3_low = gather_left(3, low, "left2_term3_low")
-        finish(2, whole, term2, "total2", "turned1")
-        term3_high = gather_left(3, high, "left2_term3_high")
-        finish(3, low, term3_low, "total3_low", "result3_low")
-        finish(3, high, term3_high, "total3_high", "result3_high")
+            nc.vector.tensor_tensor(term[:], knots2[LAST][:].indirect(lst), rest2[:, cols], ALU.mult)
+            left_terms.append(term)
+        with_right = held([P, R], F32, "with_right")
+        nc.vector.tensor_tensor(with_right[:], partial[:], right_term[:], ALU.add)
+        result = held([P, R], F32, "turned%d" % (LAST - 1))
+        for i, cols in enumerate(halves):
+            total = held([P, R // 2], F32, "total%d" % i)
+            nc.vector.tensor_tensor(total[:], with_right[:, cols], left_terms[i][:], ALU.add)
+            nc.scalar.activation(result[:, cols], total[:], ACT.Abs)
+            nc.sync.dma_start(out[LAST * P :, cols], result[:, cols])

@@ -25,6 +25,7 @@ CHUNKS = R // P
 HALF = S // 2
 WINDOW = R + 16
 LAST = BLOCKS - 1
+AFTER_KN2 = 4
 
 
 def tile_picked_ynhits_err_p_kernel(
@@ -166,9 +167,8 @@ def tile_picked_ynhits_err_p_kernel(
         rest1 = held([P, R], F32, "rest1")
         nc.vector.tensor_scalar(rest1[:], frac1_t[:], -1.0, 1.0, op0=ALU.mult, op1=ALU.add)
 
-        kn2_q = quantize(
-            interleave(kn2_raw, W, "kn2_grouped", lambda dst, src: nc.scalar.activation(dst, src, ACT.Copy)), W, "kn2"
-        )
+        kn2_grouped = interleave(kn2_raw, W, "kn2_grouped", lambda dst, src: nc.scalar.activation(dst, src, ACT.Copy))
+        kn2_q = quantize(kn2_grouped, W, "kn2")
         for b in range(BLOCKS):
             knots(h_q[b], kn2_q, W, knots2[b])
         rest2 = held([P, R], F32, "rest2")
@@ -182,17 +182,21 @@ def tile_picked_ynhits_err_p_kernel(
                     start=(start and c == 0), stop=(stop and c == CHUNKS - 1),
                 )
 
-        def weighted(window, lst, weight, name):
-            term = held([P, R], F32, name)
-            nc.vector.tensor_tensor(term[:], window[:].indirect(lst[:]), weight[:], ALU.mult)
+        def weighted(window, lst, weight, term):
+            nc.vector.tensor_tensor(term, window[:].indirect(lst[:]), weight[:], ALU.mult)
             return term
 
+        def term_tile(name):
+            return held([P, R], F32, name)[:]
+
+        after_kn2 = held([P, AFTER_KN2, R], F32, "kn2_grouped")
+        rate1_terms = [term_tile("rate1_term%d" % i) for i in range(2 * BLOCKS - AFTER_KN2)]
+        rate1_terms.extend(after_kn2[:, i, :] for i in range(AFTER_KN2))
         sums = []
         for b in range(BLOCKS):
             bank = psum.tile([P, R], F32, name="block_bank", tag="block_bank", bufs=BLOCKS)
-            add_turned(bank, weighted(knots1[b], right1_t, frac1_t, "right1_term%d" % b), True, False)
-            add_turned(bank, weighted(knots1[b], left1_t, rest1, "left1_term%d" % b), False, False)
-            add_turned(bank, true_t[:, b, :], False, b == LAST)
+            add_turned(bank, weighted(knots1[b], right1_t, frac1_t, rate1_terms[2 * b]), True, False)
+            add_turned(bank, weighted(knots1[b], left1_t, rest1, rate1_terms[2 * b + 1]), False, False)
             sums.append(bank)
 
 
@@ -205,18 +209,20 @@ def tile_picked_ynhits_err_p_kernel(
                 nc.tensor.transpose(back[:, cols], turned[:, cols], identity[:])
             return back
 
+        add_turned(sums[LAST], true_t[:, LAST, :], False, True)
         partial = turn_back(LAST, ACT.Copy)
 
         for b in range(LAST):
-            add_turned(sums[b], weighted(knots2[b], right2_t, frac2_t, "right2_term%d" % b), False, False)
-            add_turned(sums[b], weighted(knots2[b], left2_t, rest2, "left2_term%d" % b), False, True)
+            add_turned(sums[b], true_t[:, b, :], False, False)
+            add_turned(sums[b], weighted(knots2[b], right2_t, frac2_t, term_tile("right2_term%d" % b)), False, False)
+            add_turned(sums[b], weighted(knots2[b], left2_t, rest2, term_tile("left2_term%d" % b)), False, True)
             back = turn_back(b, ACT.Abs)
             result = held([P, R], F32, "result%d" % b)
             nc.scalar.copy(result[:], back[:])
             nc.sync.dma_start(out[b * P : (b + 1) * P, :], result[:])
 
         halves = [slice(0, R // 2), slice(R // 2, R)]
-        right_term = weighted(knots2[LAST], right2_t, frac2_t, "right2_term%d" % LAST)
+        right_term = weighted(knots2[LAST], right2_t, frac2_t, term_tile("right2_term%d" % LAST))
         left_terms = []
         for i, cols in enumerate(halves):
             term = held([P, R // 2], F32, "left2_half%d" % i)
@@ -224,7 +230,7 @@ def tile_picked_ynhits_err_p_kernel(
             nc.vector.tensor_tensor(term[:], knots2[LAST][:].indirect(lst), rest2[:, cols], ALU.mult)
             left_terms.append(term)
         with_right = held([P, R], F32, "with_right")
-        nc.vector.tensor_tensor(with_right[:], partial[:], right_term[:], ALU.add)
+        nc.vector.tensor_tensor(with_right[:], partial[:], right_term, ALU.add)
         result = held([P, R], F32, "turned%d" % (LAST - 1))
         for i, cols in enumerate(halves):
             total = held([P, R // 2], F32, "total%d" % i)

@@ -25,7 +25,6 @@ CHUNKS = R // P
 HALF = S // 2
 WINDOW = R + 16
 LAST = BLOCKS - 1
-AFTER_KN2 = 4
 
 
 def tile_picked_ynhits_err_p_kernel(
@@ -60,29 +59,34 @@ def tile_picked_ynhits_err_p_kernel(
         identity = held([P, P], F32, "identity")
         make_identity(nc, identity[:])
 
+        def load_words(o):
+            words = held([P, T], U32, "x_table%d" % o)
+            nc.sync.dma_start(words[:].bitcast(I32), x_words[o].rearrange("p n t -> p (n t)").bitcast(I32))
+            return words
+
+        def load_fraction(frac, name):
+            cols = held([P, PACK], F32, name)
+            nc.sync.dma_start(cols[:], frac[0].rearrange("(p c) -> p c", c=PACK))
+            return cols
+
         offs_t = load_list(offs, "offs_t")
         w1_raw = [load_rows(w1[:K_PASS, :], H, "w1_raw0")]
+        frac1_cols = load_fraction(frac1, "frac1_cols")
+        frac2_cols = load_fraction(frac2, "frac2_cols")
         for q in range(4):
             nc.sync.dma_start(
                 x_scale_rows[32 * q : 32 * q + 4 * PASSES, :].bitcast(I32),
                 x_scales[:, 4 * q : 4 * q + 4, :].bitcast(I32),
             )
         w1_raw.append(load_rows(w1[K_PASS:, :], H, "w1_raw1"))
-        x_table = []
-        for o in range(PASSES):
-            words = held([P, T], U32, "x_table%d" % o)
-            nc.sync.dma_start(words[:].bitcast(I32), x_words[o].rearrange("p n t -> p (n t)").bitcast(I32))
-            x_table.append(words)
+        x_table = [load_words(0)]
+        x_table.append(load_words(1))
         kn1_raw = load_rows(kn1, G, "kn1_raw")
         right1_t = load_list(right1, "right1_t")
-        frac1_t = held([P, R], F32, "frac1_t")
-        nc.sync.dma_start(frac1_t[:], frac1)
         left1_t = load_list(left1, "left1_t")
         kn2_raw = load_rows(kn2, W, "kn2_raw")
-        left2_t = load_list(left2, "left2_t")
         right2_t = load_list(right2, "right2_t")
-        frac2_t = held([P, R], F32, "frac2_t")
-        nc.sync.dma_start(frac2_t[:], frac2)
+        left2_t = load_list(left2, "left2_t")
         true_t = held([P, BLOCKS, R], F32, "true_t")
         nc.sync.dma_start(true_t[:], true.rearrange("(b p) r -> p b r", p=P))
 
@@ -106,6 +110,23 @@ def tile_picked_ynhits_err_p_kernel(
                 nc.vector.tensor_copy(dst, src)
             w1_q.append(quantize(grouped, H, "w1_%d" % o))
 
+        def work_bank(shape):
+            return psum.tile(shape, F32, name="work_bank", tag="work_bank", bufs=4)
+
+        def spread(cols, name):
+            bank = work_bank([P, PACK, P])
+            for c in range(PACK):
+                nc.tensor.transpose(bank[:, c, :], cols[:, c : c + 1].to_broadcast([P, P]), identity[:])
+            rows = bank[:].rearrange("p c n -> p n c")
+            part = held([P, R], F32, name + "_part")
+            rest = held([P, R], F32, name + "_rest")
+            nc.scalar.activation(part[:].rearrange("p (n c) -> p n c", c=PACK), rows, ACT.Copy)
+            nc.scalar.activation(rest[:].rearrange("p (n c) -> p n c", c=PACK), rows, ACT.Copy, scale=-1.0, bias=1.0)
+            return part, rest
+
+        part1, rest1 = spread(frac1_cols, "frac1")
+        part2, rest2 = spread(frac2_cols, "frac2")
+
         x_codes = [[None, None] for o in range(PASSES)]
         for o in range(PASSES):
             for half in range(2):
@@ -125,7 +146,7 @@ def tile_picked_ynhits_err_p_kernel(
         kn1_grouped = interleave(kn1_raw, G, "kn1_grouped", nc.vector.tensor_copy)
 
         def knots(h_q, kn_q, width, window, on_vector=False):
-            acc = psum.tile([P, W], F32, name="work_bank", tag="work_bank", bufs=4)
+            acc = work_bank([P, W])
             nc.tensor.matmul_mx(
                 out=acc[:, :width],
                 lhsT=h_q[0][:].bitcast(FP8X4),
@@ -164,76 +185,111 @@ def tile_picked_ynhits_err_p_kernel(
                 kn1_q = quantize(kn1_grouped, G, "kn1")
             knots(h_q[b], kn1_q, G, knots1[b], on_vector=(b == 0))
 
-        rest1 = held([P, R], F32, "rest1")
-        nc.vector.tensor_scalar(rest1[:], frac1_t[:], -1.0, 1.0, op0=ALU.mult, op1=ALU.add)
-
         kn2_grouped = interleave(kn2_raw, W, "kn2_grouped", lambda dst, src: nc.scalar.activation(dst, src, ACT.Copy))
         kn2_q = quantize(kn2_grouped, W, "kn2")
         for b in range(BLOCKS):
             knots(h_q[b], kn2_q, W, knots2[b])
-        rest2 = held([P, R], F32, "rest2")
-        nc.scalar.activation(rest2[:], frac2_t[:], ACT.Copy, scale=-1.0, bias=1.0)
 
         def add_turned(bank, term, start, stop):
-            for c in range(CHUNKS):
+            chunks = term.shape[1] // P
+            for c in range(chunks):
                 cols = slice(c * P, (c + 1) * P)
                 nc.tensor.matmul(
                     bank[:, cols], term[:, cols], identity[:], is_transpose=True,
-                    start=(start and c == 0), stop=(stop and c == CHUNKS - 1),
+                    start=(start and c == 0), stop=(stop and c == chunks - 1),
                 )
 
         def weighted(window, lst, weight, term):
-            nc.vector.tensor_tensor(term, window[:].indirect(lst[:]), weight[:], ALU.mult)
+            nc.vector.tensor_tensor(term, window[:].indirect(lst), weight, ALU.mult)
+            return term
+
+        def fetched(window, lst, plain):
+            nc.scalar.activation(plain, window[:].indirect(lst), ACT.Copy)
+            return plain
+
+        def times(plain, weight, term):
+            nc.vector.tensor_tensor(term, plain, weight, ALU.mult)
             return term
 
         def term_tile(name):
             return held([P, R], F32, name)[:]
 
-        after_kn2 = held([P, AFTER_KN2, R], F32, "kn2_grouped")
-        rate1_terms = [term_tile("rate1_term%d" % i) for i in range(2 * BLOCKS - AFTER_KN2)]
-        rate1_terms.extend(after_kn2[:, i, :] for i in range(AFTER_KN2))
-        sums = []
-        for b in range(BLOCKS):
-            bank = psum.tile([P, R], F32, name="block_bank", tag="block_bank", bufs=BLOCKS)
-            add_turned(bank, weighted(knots1[b], right1_t, frac1_t, rate1_terms[2 * b]), True, False)
-            add_turned(bank, weighted(knots1[b], left1_t, rest1, rate1_terms[2 * b + 1]), False, False)
-            sums.append(bank)
+        def sum_bank():
+            return psum.tile([P, R], F32, name="block_bank", tag="block_bank", bufs=BLOCKS)
 
-
-        def turn_back(b, func):
-            turned = held([P, R], F32, "turned%d" % b)
-            nc.scalar.activation(turned[:], sums[b][:], func)
-            back = psum.tile([P, R], F32, name="work_bank", tag="work_bank", bufs=4)
-            for c in range(CHUNKS):
+        def turn_back(total, width, func, name):
+            turned = held([P, width], F32, name)
+            nc.scalar.activation(turned[:], total, func)
+            back = work_bank([P, R])
+            for c in range(width // P):
                 cols = slice(c * P, (c + 1) * P)
                 nc.tensor.transpose(back[:, cols], turned[:, cols], identity[:])
             return back
 
-        add_turned(sums[LAST], true_t[:, LAST, :], False, True)
-        partial = turn_back(LAST, ACT.Copy)
-
-        for b in range(LAST):
-            add_turned(sums[b], true_t[:, b, :], False, False)
-            add_turned(sums[b], weighted(knots2[b], right2_t, frac2_t, term_tile("right2_term%d" % b)), False, False)
-            add_turned(sums[b], weighted(knots2[b], left2_t, rest2, term_tile("left2_term%d" % b)), False, True)
-            back = turn_back(b, ACT.Abs)
+        def finish(b, back):
             result = held([P, R], F32, "result%d" % b)
             nc.scalar.copy(result[:], back[:])
             nc.sync.dma_start(out[b * P : (b + 1) * P, :], result[:])
 
         halves = [slice(0, R // 2), slice(R // 2, R)]
-        right_term = weighted(knots2[LAST], right2_t, frac2_t, term_tile("right2_term%d" % LAST))
-        left_terms = []
-        for i, cols in enumerate(halves):
-            term = held([P, R // 2], F32, "left2_half%d" % i)
+        sums = [sum_bank(), sum_bank(), None, sum_bank()]
+        half_sums = [sum_bank()]
+
+        def add_halves(term, start, stop):
+            for i, cols in enumerate(halves):
+                add_turned(half_sums[i], term[:, cols], start, stop)
+
+        def left2_half(b, cols, term):
             lst = left2_t[:, cols.start // 16 : cols.stop // 16]
-            nc.vector.tensor_tensor(term[:], knots2[LAST][:].indirect(lst), rest2[:, cols], ALU.mult)
-            left_terms.append(term)
-        with_right = held([P, R], F32, "with_right")
-        nc.vector.tensor_tensor(with_right[:], partial[:], right_term, ALU.add)
-        result = held([P, R], F32, "turned%d" % (LAST - 1))
+            return weighted(knots2[b], lst, rest2[:, cols], term)
+
+        add_turned(sums[0], weighted(knots1[0], right1_t[:], part1[:], term_tile("right1_term0")), True, False)
+        add_turned(sums[0], weighted(knots1[0], left1_t[:], rest1[:], term_tile("left1_term0")), False, False)
+        add_turned(sums[1], weighted(knots1[1], right1_t[:], part1[:], term_tile("right1_term1")), True, False)
+        add_turned(sums[1], weighted(knots1[1], left1_t[:], rest1[:], term_tile("kn2_grouped")), False, False)
+
+        plain = fetched(knots1[3], right1_t[:], term_tile("kn2_raw"))
+        add_turned(sums[3], times(plain, part1[:], term_tile("right1_term3")), True, False)
+        plains3 = held([P, 2, R], F32, "kn2_codes")
+        fetched(knots1[3], left1_t[:], plains3[:, 0, :])
+        fetched(knots2[3], right2_t[:], plains3[:, 1, :])
+
+        add_turned(sums[0], true_t[:, 0, :], False, False)
+        add_turned(sums[0], weighted(knots2[0], right2_t[:], part2[:], term_tile("right2_term0")), False, False)
+        add_turned(sums[1], true_t[:, 1, :], False, False)
+        add_turned(sums[0], weighted(knots2[0], left2_t[:], rest2[:], term_tile("left2_term0")), False, True)
+        add_turned(sums[3], true_t[:, 3, :], False, False)
+        add_turned(sums[1], weighted(knots2[1], right2_t[:], part2[:], term_tile("right2_term1")), False, False)
+        back0 = turn_back(sums[0][:], R, ACT.Abs, "turned0")
+        right1_plain2 = fetched(knots1[2], right1_t[:], term_tile("left2_term0"))
+        finish(0, back0)
+        add_turned(sums[1], weighted(knots2[1], left2_t[:], rest2[:], term_tile("left2_term1")), False, True)
+        half_sums.append(sum_bank())
+        add_halves(true_t[:, 2, :], True, False)
+        add_halves(weighted(knots2[2], right2_t[:], part2[:], term_tile("right2_term2")), False, False)
+        back1 = turn_back(sums[1][:], R, ACT.Abs, "turned1")
+        left1_plain2 = fetched(knots1[2], left1_t[:], term_tile("left2_term1"))
+        finish(1, back1)
+        add_turned(sums[3], times(plains3[:, 0, :], rest1[:], term_tile("left1_term3")), False, False)
+        add_turned(sums[3], times(plains3[:, 1, :], part2[:], term_tile("right2_term3")), False, True)
+        add_halves(times(right1_plain2, part1[:], term_tile("right1_term2")), False, False)
+        partial = turn_back(sums[3][:], R, ACT.Copy, "turned3")
+        last_low = held([P, R // 2], F32, "last_low")
+        left2_half(LAST, halves[0], last_low[:])
+        add_halves(times(left1_plain2, rest1[:], term_tile("left1_term2")), False, False)
+
+        last_terms = held([P, 3, R // 2], F32, "left2_term1")
+        backs = []
         for i, cols in enumerate(halves):
+            add_turned(half_sums[i], left2_half(2, cols, last_terms[:, i, :]), False, True)
+            backs.append(turn_back(half_sums[i][:, : R // 2], R // 2, ACT.Abs, "turned2_%d" % i))
+        left2_half(LAST, halves[1], last_terms[:, 2, :])
+        for i, cols in enumerate(halves):
+            result2 = held([P, R // 2], F32, "result2_%d" % i)
+            nc.scalar.copy(result2[:], backs[i][:, : R // 2])
+            nc.sync.dma_start(out[2 * P : 3 * P, cols], result2[:])
             total = held([P, R // 2], F32, "total%d" % i)
-            nc.vector.tensor_tensor(total[:], with_right[:, cols], left_terms[i][:], ALU.add)
-            nc.scalar.activation(result[:, cols], total[:], ACT.Abs)
-            nc.sync.dma_start(out[LAST * P :, cols], result[:, cols])
+            nc.vector.tensor_tensor(total[:], partial[:, cols], [last_low[:], last_terms[:, 2, :]][i], ALU.add)
+            result3 = held([P, R // 2], F32, "turned2_%d" % i)
+            nc.scalar.activation(result3[:], total[:], ACT.Abs)
+            nc.sync.dma_start(out[LAST * P :, cols], result3[:])

@@ -56,6 +56,8 @@ def tile_picked_ynhits_err_p_kernel(
 
         x_scale_rows = held([P, T], U8, "x_scale_rows")
         nc.gpsimd.memset(x_scale_rows[:].bitcast(I32), 0)
+        frac_rows = held([P, P], F32, "frac_rows")
+        nc.gpsimd.memset(frac_rows[:], 0.0)
         identity = held([P, P], F32, "identity")
         make_identity(nc, identity[:])
 
@@ -64,20 +66,15 @@ def tile_picked_ynhits_err_p_kernel(
             nc.sync.dma_start(words[:].bitcast(I32), x_words[o].rearrange("p n t -> p (n t)").bitcast(I32))
             return words
 
-        def load_fraction(frac, name):
-            cols = held([P, PACK], F32, name)
-            nc.sync.dma_start(cols[:], frac[0].rearrange("(p c) -> p c", c=PACK))
-            return cols
-
         offs_t = load_list(offs, "offs_t")
         w1_raw = [load_rows(w1[:K_PASS, :], H, "w1_raw0")]
-        frac1_cols = load_fraction(frac1, "frac1_cols")
-        frac2_cols = load_fraction(frac2, "frac2_cols")
         for q in range(4):
             nc.sync.dma_start(
                 x_scale_rows[32 * q : 32 * q + 4 * PASSES, :].bitcast(I32),
                 x_scales[:, 4 * q : 4 * q + 4, :].bitcast(I32),
             )
+        for i, frac in enumerate((frac1, frac2)):
+            nc.sync.dma_start(frac_rows[i * CHUNKS : (i + 1) * CHUNKS, :], frac[0].rearrange("(c n) -> c n", n=P))
         w1_raw.append(load_rows(w1[K_PASS:, :], H, "w1_raw1"))
         x_table = [load_words(0)]
         x_table.append(load_words(1))
@@ -113,19 +110,24 @@ def tile_picked_ynhits_err_p_kernel(
         def work_bank(shape):
             return psum.tile(shape, F32, name="work_bank", tag="work_bank", bufs=4)
 
-        def spread(cols, name):
-            bank = work_bank([P, PACK, P])
-            for c in range(PACK):
-                nc.tensor.transpose(bank[:, c, :], cols[:, c : c + 1].to_broadcast([P, P]), identity[:])
-            rows = bank[:].rearrange("p c n -> p n c")
+        bank = work_bank([P, P])
+        nc.tensor.transpose(bank[:], frac_rows[:], identity[:])
+        frac_cols = held([P, 2 * CHUNKS], F32, "frac_cols")
+        nc.scalar.copy(frac_cols[:], bank[:, : 2 * CHUNKS])
+
+        def spread(first, name):
+            bank = work_bank([P, R])
+            for c in range(CHUNKS):
+                column = frac_cols[:, first + c : first + c + 1]
+                nc.tensor.transpose(bank[:, c * P : (c + 1) * P], column.to_broadcast([P, P]), identity[:])
             part = held([P, R], F32, name + "_part")
             rest = held([P, R], F32, name + "_rest")
-            nc.scalar.activation(part[:].rearrange("p (n c) -> p n c", c=PACK), rows, ACT.Copy)
-            nc.scalar.activation(rest[:].rearrange("p (n c) -> p n c", c=PACK), rows, ACT.Copy, scale=-1.0, bias=1.0)
+            nc.scalar.copy(part[:], bank[:])
+            nc.scalar.activation(rest[:], bank[:], ACT.Copy, scale=-1.0, bias=1.0)
             return part, rest
 
-        part1, rest1 = spread(frac1_cols, "frac1")
-        part2, rest2 = spread(frac2_cols, "frac2")
+        part1, rest1 = spread(0, "frac1")
+        part2, rest2 = spread(CHUNKS, "frac2")
 
         x_codes = [[None, None] for o in range(PASSES)]
         for o in range(PASSES):
@@ -161,8 +163,7 @@ def tile_picked_ynhits_err_p_kernel(
             else:
                 nc.scalar.activation(window[:, :width], acc[:, :width], ACT.Copy, scale=-1.0)
 
-        h_q = []
-        for b in range(BLOCKS):
+        def hidden_block(b):
             half, first = divmod(b * P, HALF)
             acc = psum.tile([P, PACK, P], F32, name="block_bank", tag="block_bank", bufs=BLOCKS)
             for o in range(PASSES):
@@ -180,15 +181,7 @@ def tile_picked_ynhits_err_p_kernel(
             nc.scalar.activation(
                 hidden[:].rearrange("p (n t) -> p n t", t=PACK), acc[:].rearrange("p t n -> p n t"), ACT.Relu
             )
-            h_q.append(quantize(hidden, P, "h%d" % b))
-            if b == 0:
-                kn1_q = quantize(kn1_grouped, G, "kn1")
-            knots(h_q[b], kn1_q, G, knots1[b], on_vector=(b == 0))
-
-        kn2_grouped = interleave(kn2_raw, W, "kn2_grouped", lambda dst, src: nc.scalar.activation(dst, src, ACT.Copy))
-        kn2_q = quantize(kn2_grouped, W, "kn2")
-        for b in range(BLOCKS):
-            knots(h_q[b], kn2_q, W, knots2[b])
+            return hidden
 
         def add_turned(bank, term, start, stop):
             chunks = term.shape[1] // P
@@ -214,26 +207,29 @@ def tile_picked_ynhits_err_p_kernel(
         def term_tile(name):
             return held([P, R], F32, name)[:]
 
+        def ring_tile():
+            return keep.tile([P, R], F32, name="ring", tag="ring", bufs=3, align_bytes=64)[:]
+
         def sum_bank():
             return psum.tile([P, R], F32, name="block_bank", tag="block_bank", bufs=BLOCKS)
 
-        def turn_back(total, width, func, name):
+        def turn_out(total, width, func, name):
             turned = held([P, width], F32, name)
             nc.scalar.activation(turned[:], total, func)
-            back = work_bank([P, R])
+            return turned
+
+        def turn_in(turned, width, back):
             for c in range(width // P):
                 cols = slice(c * P, (c + 1) * P)
                 nc.tensor.transpose(back[:, cols], turned[:, cols], identity[:])
             return back
 
-        def finish(b, back):
-            result = held([P, R], F32, "result%d" % b)
+        def finish(b, back, name):
+            result = held([P, R], F32, name)
             nc.scalar.copy(result[:], back[:])
             nc.sync.dma_start(out[b * P : (b + 1) * P, :], result[:])
 
         halves = [slice(0, R // 2), slice(R // 2, R)]
-        sums = [sum_bank(), sum_bank(), None, sum_bank()]
-        half_sums = [sum_bank()]
 
         def add_halves(term, start, stop):
             for i, cols in enumerate(halves):
@@ -243,53 +239,78 @@ def tile_picked_ynhits_err_p_kernel(
             lst = left2_t[:, cols.start // 16 : cols.stop // 16]
             return weighted(knots2[b], lst, rest2[:, cols], term)
 
+        hidden = [hidden_block(b) for b in range(BLOCKS)]
+        h_q = [quantize(hidden[0], P, "h0")]
+        kn1_q = quantize(kn1_grouped, G, "kn1")
+        h_q.append(quantize(hidden[1], P, "h1"))
+        knots(h_q[0], kn1_q, G, knots1[0], on_vector=True)
+        knots(h_q[1], kn1_q, G, knots1[1])
+        h_q.append(quantize(hidden[2], P, "h2"))
+        knots(h_q[2], kn1_q, G, knots1[2])
+        sums = [sum_bank(), sum_bank(), None, sum_bank()]
+        half_sums = [sum_bank()]
         add_turned(sums[0], weighted(knots1[0], right1_t[:], part1[:], term_tile("right1_term0")), True, False)
+        h_q.append(quantize(hidden[3], P, "h3"))
+        kn2_grouped = interleave(kn2_raw, W, "kn2_grouped", lambda dst, src: nc.scalar.activation(dst, src, ACT.Copy))
+        knots(h_q[3], kn1_q, G, knots1[3])
         add_turned(sums[0], weighted(knots1[0], left1_t[:], rest1[:], term_tile("left1_term0")), False, False)
         add_turned(sums[1], weighted(knots1[1], right1_t[:], part1[:], term_tile("right1_term1")), True, False)
-        add_turned(sums[1], weighted(knots1[1], left1_t[:], rest1[:], term_tile("kn2_grouped")), False, False)
-
+        kn2_q = quantize(kn2_grouped, W, "kn2")
         plain = fetched(knots1[3], right1_t[:], term_tile("kn2_raw"))
+        for b in (0, 1, 3, 2):
+            knots(h_q[b], kn2_q, W, knots2[b])
+        after_kn2 = held([P, 2, R], F32, "kn2_grouped")
+        add_turned(sums[1], weighted(knots1[1], left1_t[:], rest1[:], after_kn2[:, 0, :]), False, False)
+        left1_term2 = weighted(knots1[2], left1_t[:], rest1[:], after_kn2[:, 1, :])
         add_turned(sums[3], times(plain, part1[:], term_tile("right1_term3")), True, False)
-        plains3 = held([P, 2, R], F32, "kn2_codes")
-        fetched(knots1[3], left1_t[:], plains3[:, 0, :])
-        fetched(knots2[3], right2_t[:], plains3[:, 1, :])
+        plains = held([P, 3, R], F32, "kn2_codes")
+        left1_plain3 = fetched(knots1[3], left1_t[:], plains[:, 0, :])
+        left2_plain3 = fetched(knots2[3], left2_t[:], plains[:, 1, :])
+        right1_plain2 = fetched(knots1[2], right1_t[:], plains[:, 2, :])
 
+        half_sums.append(work_bank([P, R]))
         add_turned(sums[0], true_t[:, 0, :], False, False)
-        add_turned(sums[0], weighted(knots2[0], right2_t[:], part2[:], term_tile("right2_term0")), False, False)
         add_turned(sums[1], true_t[:, 1, :], False, False)
-        add_turned(sums[0], weighted(knots2[0], left2_t[:], rest2[:], term_tile("left2_term0")), False, True)
         add_turned(sums[3], true_t[:, 3, :], False, False)
-        add_turned(sums[1], weighted(knots2[1], right2_t[:], part2[:], term_tile("right2_term1")), False, False)
-        back0 = turn_back(sums[0][:], R, ACT.Abs, "turned0")
-        right1_plain2 = fetched(knots1[2], right1_t[:], term_tile("left2_term0"))
-        finish(0, back0)
-        add_turned(sums[1], weighted(knots2[1], left2_t[:], rest2[:], term_tile("left2_term1")), False, True)
-        half_sums.append(sum_bank())
         add_halves(true_t[:, 2, :], True, False)
-        add_halves(weighted(knots2[2], right2_t[:], part2[:], term_tile("right2_term2")), False, False)
-        back1 = turn_back(sums[1][:], R, ACT.Abs, "turned1")
-        left1_plain2 = fetched(knots1[2], left1_t[:], term_tile("left2_term1"))
-        finish(1, back1)
-        add_turned(sums[3], times(plains3[:, 0, :], rest1[:], term_tile("left1_term3")), False, False)
-        add_turned(sums[3], times(plains3[:, 1, :], part2[:], term_tile("right2_term3")), False, True)
-        add_halves(times(right1_plain2, part1[:], term_tile("right1_term2")), False, False)
-        partial = turn_back(sums[3][:], R, ACT.Copy, "turned3")
-        last_low = held([P, R // 2], F32, "last_low")
-        left2_half(LAST, halves[0], last_low[:])
-        add_halves(times(left1_plain2, rest1[:], term_tile("left1_term2")), False, False)
+        add_halves(left1_term2, False, False)
+        add_turned(sums[0], weighted(knots2[0], right2_t[:], part2[:], ring_tile()), False, False)
+        add_turned(sums[0], weighted(knots2[0], left2_t[:], rest2[:], ring_tile()), False, True)
+        add_turned(sums[3], left2_plain3, False, False)
+        add_turned(sums[3], times(left1_plain3, rest1[:], ring_tile()), False, True)
+        add_turned(sums[1], weighted(knots2[1], right2_t[:], part2[:], ring_tile()), False, False)
+        turned0 = turn_out(sums[0][:], R, ACT.Abs, "turned0")
+        back0 = turn_in(turned0, R, work_bank([P, R]))
+        turned3 = turn_out(sums[3][:], R, ACT.Copy, "turned3")
+        partial = turn_in(turned3, R, work_bank([P, R]))
+        finish(0, back0, "result0")
+        add_turned(sums[1], weighted(knots2[1], left2_t[:], rest2[:], ring_tile()), False, True)
+        add_halves(weighted(knots2[2], right2_t[:], part2[:], ring_tile()), False, False)
+        turned1 = turn_out(sums[1][:], R, ACT.Abs, "turned1")
+        back1 = turn_in(turned1, R, sum_bank())
+        add_halves(times(right1_plain2, part1[:], ring_tile()), False, False)
+        finish(1, back1, "result1")
 
-        last_terms = held([P, 3, R // 2], F32, "left2_term1")
-        backs = []
+        turned2 = []
+        last_term = ring_tile()
         for i, cols in enumerate(halves):
-            add_turned(half_sums[i], left2_half(2, cols, last_terms[:, i, :]), False, True)
-            backs.append(turn_back(half_sums[i][:, : R // 2], R // 2, ACT.Abs, "turned2_%d" % i))
-        left2_half(LAST, halves[1], last_terms[:, 2, :])
+            add_turned(half_sums[i], left2_half(2, cols, last_term[:, cols]), False, True)
+            turned2.append(turn_out(half_sums[i][:, : R // 2], R // 2, ACT.Abs, "turned2_%d" % i))
+        backs = [turn_in(turned, R // 2, sum_bank()) for turned in turned2]
+        gaps = ring_tile()
+        steps = held([P, R], F32, "steps")
+        for cols in halves:
+            lst = right2_t[:, cols.start // 16 : cols.stop // 16]
+            nc.vector.tensor_tensor(gaps[:, cols], knots2[LAST][:].indirect(lst), left2_plain3[:, cols], ALU.subtract)
+        for cols in halves:
+            times(gaps[:, cols], part2[:, cols], steps[:, cols])
         for i, cols in enumerate(halves):
             result2 = held([P, R // 2], F32, "result2_%d" % i)
             nc.scalar.copy(result2[:], backs[i][:, : R // 2])
             nc.sync.dma_start(out[2 * P : 3 * P, cols], result2[:])
+        result3 = held([P, R], F32, "turned2_1")
+        for i, cols in enumerate(halves):
             total = held([P, R // 2], F32, "total%d" % i)
-            nc.vector.tensor_tensor(total[:], partial[:, cols], [last_low[:], last_terms[:, 2, :]][i], ALU.add)
-            result3 = held([P, R // 2], F32, "turned2_%d" % i)
-            nc.scalar.activation(result3[:], total[:], ACT.Abs)
-            nc.sync.dma_start(out[LAST * P :, cols], result3[:])
+            nc.vector.tensor_tensor(total[:], partial[:, cols], steps[:, cols], ALU.add)
+            nc.scalar.activation(result3[:, cols], total[:], ACT.Abs)
+            nc.sync.dma_start(out[LAST * P :, cols], result3[:, cols])

@@ -24,7 +24,7 @@ BLOCKS = S // P
 CHUNKS = R // P
 HALF = S // 2
 WINDOW = R + 16
-LAST = BLOCKS - 1
+HALVES = (slice(0, R // 2), slice(R // 2, R))
 
 
 def tile_picked_ynhits_err_p_kernel(
@@ -38,6 +38,15 @@ def tile_picked_ynhits_err_p_kernel(
         def held(shape, dtype, name):
             return keep.tile(shape, dtype, name=name, tag=name, align_bytes=64)
 
+        def row(name):
+            return held([P, R], F32, name)[:]
+
+        def bank(name):
+            return psum.tile([P, R], F32, name=name, tag=name, bufs=1)
+
+        def work_bank():
+            return psum.tile([P, R], F32, name="work_bank", tag="work_bank", bufs=4)
+
         def load_list(src, name):
             lst = held([P, R // 16], U16, name)
             nc.sync.dma_start(lst[:], src)
@@ -47,6 +56,11 @@ def tile_picked_ynhits_err_p_kernel(
             raw = held([P, PACK, width], F32, name)
             nc.sync.dma_start(raw[:], src.rearrange("(p j) n -> p j n", j=PACK))
             return raw
+
+        def load_words(o):
+            words = held([P, T], U32, "x_table%d" % o)
+            nc.sync.dma_start(words[:].bitcast(I32), x_words[o].rearrange("p n t -> p (n t)").bitcast(I32))
+            return words
 
         def quantize(grouped, width, name):
             codes = held([P, width], U32, name + "_codes")
@@ -61,11 +75,6 @@ def tile_picked_ynhits_err_p_kernel(
         identity = held([P, P], F32, "identity")
         make_identity(nc, identity[:])
 
-        def load_words(o):
-            words = held([P, T], U32, "x_table%d" % o)
-            nc.sync.dma_start(words[:].bitcast(I32), x_words[o].rearrange("p n t -> p (n t)").bitcast(I32))
-            return words
-
         offs_t = load_list(offs, "offs_t")
         w1_raw = [load_rows(w1[:K_PASS, :], H, "w1_raw0")]
         for q in range(4):
@@ -76,8 +85,7 @@ def tile_picked_ynhits_err_p_kernel(
         for i, frac in enumerate((frac1, frac2)):
             nc.sync.dma_start(frac_rows[i * CHUNKS : (i + 1) * CHUNKS, :], frac[0].rearrange("(c n) -> c n", n=P))
         w1_raw.append(load_rows(w1[K_PASS:, :], H, "w1_raw1"))
-        x_table = [load_words(0)]
-        x_table.append(load_words(1))
+        x_table = [load_words(o) for o in range(PASSES)]
         kn1_raw = load_rows(kn1, G, "kn1_raw")
         right1_t = load_list(right1, "right1_t")
         left1_t = load_list(left1, "left1_t")
@@ -107,23 +115,20 @@ def tile_picked_ynhits_err_p_kernel(
                 nc.vector.tensor_copy(dst, src)
             w1_q.append(quantize(grouped, H, "w1_%d" % o))
 
-        def work_bank(shape):
-            return psum.tile(shape, F32, name="work_bank", tag="work_bank", bufs=4)
-
-        bank = work_bank([P, P])
-        nc.tensor.transpose(bank[:], frac_rows[:], identity[:])
+        turned_rows = work_bank()
+        nc.tensor.transpose(turned_rows[:, :P], frac_rows[:], identity[:])
         frac_cols = held([P, 2 * CHUNKS], F32, "frac_cols")
-        nc.scalar.copy(frac_cols[:], bank[:, : 2 * CHUNKS])
+        nc.scalar.copy(frac_cols[:], turned_rows[:, : 2 * CHUNKS])
 
         def spread(first, name):
-            bank = work_bank([P, R])
+            spread_rows = work_bank()
             for c in range(CHUNKS):
                 column = frac_cols[:, first + c : first + c + 1]
-                nc.tensor.transpose(bank[:, c * P : (c + 1) * P], column.to_broadcast([P, P]), identity[:])
-            part = held([P, R], F32, name + "_part")
-            rest = held([P, R], F32, name + "_rest")
-            nc.scalar.copy(part[:], bank[:])
-            nc.scalar.activation(rest[:], bank[:], ACT.Copy, scale=-1.0, bias=1.0)
+                nc.tensor.transpose(spread_rows[:, c * P : (c + 1) * P], column.to_broadcast([P, P]), identity[:])
+            part = row(name + "_part")
+            rest = row(name + "_rest")
+            nc.scalar.copy(part, spread_rows[:])
+            nc.scalar.activation(rest, spread_rows[:], ACT.Copy, scale=-1.0, bias=1.0)
             return part, rest
 
         part1, rest1 = spread(0, "frac1")
@@ -145,10 +150,26 @@ def tile_picked_ynhits_err_p_kernel(
             )
             return grouped
 
-        kn1_grouped = interleave(kn1_raw, G, "kn1_grouped", nc.vector.tensor_copy)
+        def hidden_block(b, acc):
+            half, first = divmod(b * P, HALF)
+            for o in range(PASSES):
+                for t in range(PACK):
+                    nc.tensor.matmul_mx(
+                        out=acc[:, t * P : (t + 1) * P],
+                        lhsT=w1_q[o][0][:, t * P : (t + 1) * P].bitcast(FP8X4),
+                        lhsT_scale=w1_q[o][1][:, t * P : (t + 1) * P],
+                        rhs=x_codes[o][half][:, first : first + P].bitcast(FP8X4),
+                        rhs_scale=x_scale[4 * o :, b * P : (b + 1) * P],
+                        start=(o == 0 and t == 0),
+                        stop=(o == PASSES - 1 and t == PACK - 1),
+                    )
+            hidden = held([P, PACK * P], BF16, "hidden%d" % b)
+            nc.scalar.activation(
+                hidden[:].rearrange("p (n t) -> p n t", t=PACK), acc[:].rearrange("p (t n) -> p n t", t=PACK), ACT.Relu
+            )
+            return hidden
 
-        def knots(h_q, kn_q, width, window, on_vector=False):
-            acc = work_bank([P, W])
+        def knots(h_q, kn_q, width, window, acc, on_vector=False):
             nc.tensor.matmul_mx(
                 out=acc[:, :width],
                 lhsT=h_q[0][:].bitcast(FP8X4),
@@ -163,34 +184,21 @@ def tile_picked_ynhits_err_p_kernel(
             else:
                 nc.scalar.activation(window[:, :width], acc[:, :width], ACT.Copy, scale=-1.0)
 
-        def hidden_block(b):
-            half, first = divmod(b * P, HALF)
-            acc = psum.tile([P, PACK, P], F32, name="block_bank", tag="block_bank", bufs=BLOCKS)
-            for o in range(PASSES):
-                for t in range(PACK):
-                    nc.tensor.matmul_mx(
-                        out=acc[:, t, :],
-                        lhsT=w1_q[o][0][:, t * P : (t + 1) * P].bitcast(FP8X4),
-                        lhsT_scale=w1_q[o][1][:, t * P : (t + 1) * P],
-                        rhs=x_codes[o][half][:, first : first + P].bitcast(FP8X4),
-                        rhs_scale=x_scale[4 * o :, b * P : (b + 1) * P],
-                        start=(o == 0 and t == 0),
-                        stop=(o == PASSES - 1 and t == PACK - 1),
-                    )
-            hidden = held([P, PACK * P], BF16, "hidden%d" % b)
-            nc.scalar.activation(
-                hidden[:].rearrange("p (n t) -> p n t", t=PACK), acc[:].rearrange("p t n -> p n t"), ACT.Relu
-            )
-            return hidden
-
-        def add_turned(bank, term, start, stop):
+        def add_turned(total, term, start=False, stop=False):
             chunks = term.shape[1] // P
             for c in range(chunks):
                 cols = slice(c * P, (c + 1) * P)
                 nc.tensor.matmul(
-                    bank[:, cols], term[:, cols], identity[:], is_transpose=True,
+                    total[:, cols], term[:, cols], identity[:], is_transpose=True,
                     start=(start and c == 0), stop=(stop and c == chunks - 1),
                 )
+
+        def add_halves(term, start=False):
+            for total, cols in zip(sums2, HALVES):
+                add_turned(total, term[:, cols], start=start)
+
+        def part_of(lst, cols):
+            return lst[:, cols.start // 16 : cols.stop // 16]
 
         def weighted(window, lst, weight, term):
             nc.vector.tensor_tensor(term, window[:].indirect(lst), weight, ALU.mult)
@@ -204,18 +212,9 @@ def tile_picked_ynhits_err_p_kernel(
             nc.vector.tensor_tensor(term, plain, weight, ALU.mult)
             return term
 
-        def term_tile(name):
-            return held([P, R], F32, name)[:]
-
-        def ring_tile():
-            return keep.tile([P, R], F32, name="ring", tag="ring", bufs=3, align_bytes=64)[:]
-
-        def sum_bank():
-            return psum.tile([P, R], F32, name="block_bank", tag="block_bank", bufs=BLOCKS)
-
         def turn_out(total, width, func, name):
             turned = held([P, width], F32, name)
-            nc.scalar.activation(turned[:], total, func)
+            nc.scalar.activation(turned[:], total[:, :width], func)
             return turned
 
         def turn_in(turned, width, back):
@@ -224,93 +223,86 @@ def tile_picked_ynhits_err_p_kernel(
                 nc.tensor.transpose(back[:, cols], turned[:, cols], identity[:])
             return back
 
-        def finish(b, back, name):
-            result = held([P, R], F32, name)
-            nc.scalar.copy(result[:], back[:])
-            nc.sync.dma_start(out[b * P : (b + 1) * P, :], result[:])
+        def store(b, back, cols, name):
+            width = cols.stop - cols.start
+            result = held([P, width], F32, name)
+            nc.scalar.copy(result[:], back[:, :width])
+            nc.sync.dma_start(out[b * P : (b + 1) * P, cols], result[:])
 
-        halves = [slice(0, R // 2), slice(R // 2, R)]
-
-        def add_halves(term, start, stop):
-            for i, cols in enumerate(halves):
-                add_turned(half_sums[i], term[:, cols], start, stop)
-
-        def left2_half(b, cols, term):
-            lst = left2_t[:, cols.start // 16 : cols.stop // 16]
-            return weighted(knots2[b], lst, rest2[:, cols], term)
-
-        hidden = [hidden_block(b) for b in range(BLOCKS)]
-        h_q = [quantize(hidden[0], P, "h0")]
+        whole = slice(0, R)
+        kn1_grouped = interleave(kn1_raw, G, "kn1_grouped", nc.vector.tensor_copy)
+        hidden = {b: hidden_block(b, bank("bank%d" % b)) for b in (0, 1, 3)}
+        h_q = {0: quantize(hidden[0], P, "h0")}
         kn1_q = quantize(kn1_grouped, G, "kn1")
-        h_q.append(quantize(hidden[1], P, "h1"))
-        knots(h_q[0], kn1_q, G, knots1[0], on_vector=True)
-        knots(h_q[1], kn1_q, G, knots1[1])
-        h_q.append(quantize(hidden[2], P, "h2"))
-        knots(h_q[2], kn1_q, G, knots1[2])
-        sums = [sum_bank(), sum_bank(), None, sum_bank()]
-        half_sums = [sum_bank()]
-        add_turned(sums[0], weighted(knots1[0], right1_t[:], part1[:], term_tile("right1_term0")), True, False)
-        h_q.append(quantize(hidden[3], P, "h3"))
+        h_q[1] = quantize(hidden[1], P, "h1")
+        knots(h_q[0], kn1_q, G, knots1[0], work_bank(), on_vector=True)
+        knots(h_q[1], kn1_q, G, knots1[1], work_bank())
+        h_q[3] = quantize(hidden[3], P, "h3")
+        knots(h_q[3], kn1_q, G, knots1[3], work_bank())
+
+        sums = {b: bank("bank%d" % b) for b in (0, 1, 3)}
+        add_turned(sums[0], weighted(knots1[0], right1_t[:], part1, row("right1_term0")), start=True)
         kn2_grouped = interleave(kn2_raw, W, "kn2_grouped", lambda dst, src: nc.scalar.activation(dst, src, ACT.Copy))
-        knots(h_q[3], kn1_q, G, knots1[3])
-        add_turned(sums[0], weighted(knots1[0], left1_t[:], rest1[:], term_tile("left1_term0")), False, False)
-        add_turned(sums[1], weighted(knots1[1], right1_t[:], part1[:], term_tile("right1_term1")), True, False)
+        add_turned(sums[0], weighted(knots1[0], left1_t[:], rest1, row("left1_term0")))
+        right1_term1 = weighted(knots1[1], right1_t[:], part1, row("right1_term1"))
         kn2_q = quantize(kn2_grouped, W, "kn2")
-        plain = fetched(knots1[3], right1_t[:], term_tile("kn2_raw"))
-        for b in (0, 1, 3, 2):
-            knots(h_q[b], kn2_q, W, knots2[b])
-        after_kn2 = held([P, 2, R], F32, "kn2_grouped")
-        add_turned(sums[1], weighted(knots1[1], left1_t[:], rest1[:], after_kn2[:, 0, :]), False, False)
-        left1_term2 = weighted(knots1[2], left1_t[:], rest1[:], after_kn2[:, 1, :])
-        add_turned(sums[3], times(plain, part1[:], term_tile("right1_term3")), True, False)
-        plains = held([P, 3, R], F32, "kn2_codes")
-        left1_plain3 = fetched(knots1[3], left1_t[:], plains[:, 0, :])
-        left2_plain3 = fetched(knots2[3], left2_t[:], plains[:, 1, :])
-        right1_plain2 = fetched(knots1[2], right1_t[:], plains[:, 2, :])
+        right1_plain3 = fetched(knots1[3], right1_t[:], row("kn2_raw"))
+        knots(h_q[0], kn2_q, W, knots2[0], work_bank())
+        knots(h_q[3], kn2_q, W, knots2[3], work_bank())
+        knots(h_q[1], kn2_q, W, knots2[1], bank("bank2"))
+        left2_plain3 = fetched(knots2[3], left2_t[:], row("left2_plain3"))
+        add_turned(sums[1], right1_term1, start=True)
+        add_turned(sums[1], weighted(knots1[1], left1_t[:], rest1, row("kn2_grouped")))
+        hidden[2] = hidden_block(2, bank("bank2"))
+        left1_plain3 = fetched(knots1[3], left1_t[:], row("x_codes1_1"))
+        add_turned(sums[0], true_t[:, 0, :])
+        add_turned(sums[1], true_t[:, 1, :])
+        add_turned(sums[3], true_t[:, 3, :], start=True)
+        add_turned(sums[3], times(right1_plain3, part1, row("right1_term3")))
+        add_turned(sums[0], weighted(knots2[0], right2_t[:], part2, row("right2_term0")))
+        add_turned(sums[3], left2_plain3)
+        add_turned(sums[0], weighted(knots2[0], left2_t[:], rest2, row("left2_term0")), stop=True)
+        turned0 = turn_out(sums[0], R, ACT.Abs, "turned0")
+        add_turned(sums[1], weighted(knots2[1], right2_t[:], part2, row("right2_term1")))
+        h_q[2] = quantize(hidden[2], P, "h2")
+        knots(h_q[2], kn1_q, G, knots1[2], work_bank())
+        knots(h_q[2], kn2_q, W, knots2[2], work_bank())
+        right1_plain2 = fetched(knots1[2], right1_t[:], row("right1_plain2"))
+        add_turned(sums[3], times(left1_plain3, rest1, row("left1_term3")), stop=True)
+        back0 = turn_in(turned0, R, work_bank())
+        turned3 = turn_out(sums[3], R, ACT.Copy, "turned3")
+        store(0, back0, whole, "result0")
+        sums2 = [bank("bank2"), work_bank()]
+        add_halves(true_t[:, 2, :], start=True)
+        after_h2 = held([P, 2, R], F32, "hidden2")
+        add_turned(sums[1], weighted(knots2[1], left2_t[:], rest2, after_h2[:, 0, :]), stop=True)
+        turned1 = turn_out(sums[1], R, ACT.Abs, "turned1")
+        add_halves(weighted(knots1[2], left1_t[:], rest1, after_h2[:, 1, :]))
+        partial = turn_in(turned3, R, work_bank())
+        add_halves(weighted(knots2[2], right2_t[:], part2, row("right2_term2")))
+        store(1, turn_in(turned1, R, bank("bank0")), whole, "result1")
+        add_halves(times(right1_plain2, part1, row("right1_term2")))
 
-        half_sums.append(work_bank([P, R]))
-        add_turned(sums[0], true_t[:, 0, :], False, False)
-        add_turned(sums[1], true_t[:, 1, :], False, False)
-        add_turned(sums[3], true_t[:, 3, :], False, False)
-        add_halves(true_t[:, 2, :], True, False)
-        add_halves(left1_term2, False, False)
-        add_turned(sums[0], weighted(knots2[0], right2_t[:], part2[:], ring_tile()), False, False)
-        add_turned(sums[0], weighted(knots2[0], left2_t[:], rest2[:], ring_tile()), False, True)
-        add_turned(sums[3], left2_plain3, False, False)
-        add_turned(sums[3], times(left1_plain3, rest1[:], ring_tile()), False, True)
-        add_turned(sums[1], weighted(knots2[1], right2_t[:], part2[:], ring_tile()), False, False)
-        turned0 = turn_out(sums[0][:], R, ACT.Abs, "turned0")
-        back0 = turn_in(turned0, R, work_bank([P, R]))
-        turned3 = turn_out(sums[3][:], R, ACT.Copy, "turned3")
-        partial = turn_in(turned3, R, work_bank([P, R]))
-        finish(0, back0, "result0")
-        add_turned(sums[1], weighted(knots2[1], left2_t[:], rest2[:], ring_tile()), False, True)
-        add_halves(weighted(knots2[2], right2_t[:], part2[:], ring_tile()), False, False)
-        turned1 = turn_out(sums[1][:], R, ACT.Abs, "turned1")
-        back1 = turn_in(turned1, R, sum_bank())
-        add_halves(times(right1_plain2, part1[:], ring_tile()), False, False)
-        finish(1, back1, "result1")
-
+        last_term = row("right1_plain2")
         turned2 = []
-        last_term = ring_tile()
-        for i, cols in enumerate(halves):
-            add_turned(half_sums[i], left2_half(2, cols, last_term[:, cols]), False, True)
-            turned2.append(turn_out(half_sums[i][:, : R // 2], R // 2, ACT.Abs, "turned2_%d" % i))
-        backs = [turn_in(turned, R // 2, sum_bank()) for turned in turned2]
-        gaps = ring_tile()
-        steps = held([P, R], F32, "steps")
-        for cols in halves:
-            lst = right2_t[:, cols.start // 16 : cols.stop // 16]
-            nc.vector.tensor_tensor(gaps[:, cols], knots2[LAST][:].indirect(lst), left2_plain3[:, cols], ALU.subtract)
-        for cols in halves:
+        for i, cols in enumerate(HALVES):
+            term = weighted(knots2[2], part_of(left2_t, cols), rest2[:, cols], last_term[:, cols])
+            add_turned(sums2[i], term, stop=True)
+            turned2.append(turn_out(sums2[i], R // 2, ACT.Abs, "turned2_%d" % i))
+        backs2 = [turn_in(turned2[i], R // 2, bank("bank%d" % (3, 1)[i])) for i in range(2)]
+
+        gaps = row("right2_term2")
+        steps = row("steps")
+        for cols in HALVES:
+            window = knots2[3][:].indirect(part_of(right2_t, cols))
+            nc.vector.tensor_tensor(gaps[:, cols], window, left2_plain3[:, cols], ALU.subtract)
+        for cols in HALVES:
             times(gaps[:, cols], part2[:, cols], steps[:, cols])
-        for i, cols in enumerate(halves):
-            result2 = held([P, R // 2], F32, "result2_%d" % i)
-            nc.scalar.copy(result2[:], backs[i][:, : R // 2])
-            nc.sync.dma_start(out[2 * P : 3 * P, cols], result2[:])
-        result3 = held([P, R], F32, "turned2_1")
-        for i, cols in enumerate(halves):
+        for i, cols in enumerate(HALVES):
+            store(2, backs2[i], cols, "result2_%d" % i)
+        result3 = row("turned2_1")
+        for i, cols in enumerate(HALVES):
             total = held([P, R // 2], F32, "total%d" % i)
             nc.vector.tensor_tensor(total[:], partial[:, cols], steps[:, cols], ALU.add)
             nc.scalar.activation(result3[:, cols], total[:], ACT.Abs)
-            nc.sync.dma_start(out[LAST * P :, cols], result3[:, cols])
+            nc.sync.dma_start(out[3 * P :, cols], result3[:, cols])

@@ -231,67 +231,66 @@ def tile_picked_ynhits_err_p_kernel(
 
         whole = slice(0, R)
         kn1_grouped = interleave(kn1_raw, G, "kn1_grouped", nc.vector.tensor_copy)
-        hidden = {b: hidden_block(b, bank("bank%d" % b)) for b in (0, 1, 3)}
-        h_q = {0: quantize(hidden[0], P, "h0")}
+        hidden = [hidden_block(b, bank("bank%d" % b)) for b in range(BLOCKS)]
+        h_q = [quantize(hidden[0], P, "h0")]
         kn1_q = quantize(kn1_grouped, G, "kn1")
-        h_q[1] = quantize(hidden[1], P, "h1")
+        h_q.append(quantize(hidden[1], P, "h1"))
         knots(h_q[0], kn1_q, G, knots1[0], work_bank(), on_vector=True)
         knots(h_q[1], kn1_q, G, knots1[1], work_bank())
-        h_q[3] = quantize(hidden[3], P, "h3")
-        knots(h_q[3], kn1_q, G, knots1[3], work_bank())
+        h_q.append(quantize(hidden[2], P, "h2"))
+        knots(h_q[2], kn1_q, G, knots1[2], work_bank())
 
         sums = {b: bank("bank%d" % b) for b in (0, 1, 3)}
         add_turned(sums[0], weighted(knots1[0], right1_t[:], part1, row("right1_term0")), start=True)
+        h_q.append(quantize(hidden[3], P, "h3"))
         kn2_grouped = interleave(kn2_raw, W, "kn2_grouped", lambda dst, src: nc.scalar.activation(dst, src, ACT.Copy))
+        knots(h_q[3], kn1_q, G, knots1[3], work_bank())
         add_turned(sums[0], weighted(knots1[0], left1_t[:], rest1, row("left1_term0")))
-        right1_term1 = weighted(knots1[1], right1_t[:], part1, row("right1_term1"))
+        add_turned(sums[1], weighted(knots1[1], right1_t[:], part1, row("right1_term1")), start=True)
         kn2_q = quantize(kn2_grouped, W, "kn2")
         right1_plain3 = fetched(knots1[3], right1_t[:], row("kn2_raw"))
-        knots(h_q[0], kn2_q, W, knots2[0], work_bank())
-        knots(h_q[3], kn2_q, W, knots2[3], work_bank())
-        knots(h_q[1], kn2_q, W, knots2[1], bank("bank2"))
-        left2_plain3 = fetched(knots2[3], left2_t[:], row("left2_plain3"))
-        add_turned(sums[1], right1_term1, start=True)
-        add_turned(sums[1], weighted(knots1[1], left1_t[:], rest1, row("kn2_grouped")))
-        hidden[2] = hidden_block(2, bank("bank2"))
-        left1_plain3 = fetched(knots1[3], left1_t[:], row("x_codes1_1"))
+        for b in (0, 1, 2, 3):
+            knots(h_q[b], kn2_q, W, knots2[b], work_bank())
+        plains = held([P, 3, R], F32, "kn2_codes")
+        left2_plain1 = fetched(knots2[1], left2_t[:], plains[:, 0, :])
+        left1_plain3 = fetched(knots1[3], left1_t[:], plains[:, 1, :])
+        left2_plain3 = fetched(knots2[3], left2_t[:], row("kn2_scales"))
+        after_kn2 = held([P, 2, R], F32, "kn2_grouped")
+        add_turned(sums[1], weighted(knots1[1], left1_t[:], rest1, after_kn2[:, 0, :]))
         add_turned(sums[0], true_t[:, 0, :])
+        sums2 = [bank("bank2"), work_bank()]
+        add_halves(weighted(knots1[2], right1_t[:], part1, after_kn2[:, 1, :]), start=True)
+        add_turned(sums[3], times(right1_plain3, part1, row("right1_term3")), start=True)
         add_turned(sums[1], true_t[:, 1, :])
-        add_turned(sums[3], true_t[:, 3, :], start=True)
-        add_turned(sums[3], times(right1_plain3, part1, row("right1_term3")))
         add_turned(sums[0], weighted(knots2[0], right2_t[:], part2, row("right2_term0")))
-        add_turned(sums[3], left2_plain3)
+        add_turned(sums[3], true_t[:, 3, :])
         add_turned(sums[0], weighted(knots2[0], left2_t[:], rest2, row("left2_term0")), stop=True)
         turned0 = turn_out(sums[0], R, ACT.Abs, "turned0")
+        left1_plain2 = fetched(knots1[2], left1_t[:], row("left2_term0"))
+        add_halves(true_t[:, 2, :])
         add_turned(sums[1], weighted(knots2[1], right2_t[:], part2, row("right2_term1")))
-        h_q[2] = quantize(hidden[2], P, "h2")
-        knots(h_q[2], kn1_q, G, knots1[2], work_bank())
-        knots(h_q[2], kn2_q, W, knots2[2], work_bank())
-        right1_plain2 = fetched(knots1[2], right1_t[:], row("right1_plain2"))
-        add_turned(sums[3], times(left1_plain3, rest1, row("left1_term3")), stop=True)
-        back0 = turn_in(turned0, R, work_bank())
-        turned3 = turn_out(sums[3], R, ACT.Copy, "turned3")
-        store(0, back0, whole, "result0")
-        sums2 = [bank("bank2"), work_bank()]
-        add_halves(true_t[:, 2, :], start=True)
-        after_h2 = held([P, 2, R], F32, "hidden2")
-        add_turned(sums[1], weighted(knots2[1], left2_t[:], rest2, after_h2[:, 0, :]), stop=True)
+        add_turned(sums[3], left2_plain3)
+        add_turned(sums[1], times(left2_plain1, rest2, row("left2_term1")), stop=True)
         turned1 = turn_out(sums[1], R, ACT.Abs, "turned1")
-        add_halves(weighted(knots1[2], left1_t[:], rest1, after_h2[:, 1, :]))
+        back0 = turn_in(turned0, R, work_bank())
+        add_turned(sums[3], times(left1_plain3, rest1, row("left1_term3")), stop=True)
+        turned3 = turn_out(sums[3], R, ACT.Copy, "turned3")
+        store(0, back0, whole, "left1_term3")
+        late_terms = held([P, 2, R], F32, "kn2_codes")
+        add_halves(weighted(knots2[2], right2_t[:], part2, late_terms[:, 0, :]))
+        back1 = turn_in(turned1, R, bank("bank0"))
+        store(1, back1, whole, "result1")
         partial = turn_in(turned3, R, work_bank())
-        add_halves(weighted(knots2[2], right2_t[:], part2, row("right2_term2")))
-        store(1, turn_in(turned1, R, bank("bank0")), whole, "result1")
-        add_halves(times(right1_plain2, part1, row("right1_term2")))
+        add_halves(weighted(knots2[2], left2_t[:], rest2, late_terms[:, 1, :]))
 
-        last_term = row("right1_plain2")
+        last_term = row("left1_term2")
         turned2 = []
         for i, cols in enumerate(HALVES):
-            term = weighted(knots2[2], part_of(left2_t, cols), rest2[:, cols], last_term[:, cols])
-            add_turned(sums2[i], term, stop=True)
+            add_turned(sums2[i], times(left1_plain2[:, cols], rest1[:, cols], last_term[:, cols]), stop=True)
             turned2.append(turn_out(sums2[i], R // 2, ACT.Abs, "turned2_%d" % i))
-        backs2 = [turn_in(turned2[i], R // 2, bank("bank%d" % (3, 1)[i])) for i in range(2)]
+        backs2 = [turn_in(turned2[0], R // 2, bank("bank1")), turn_in(turned2[1], R // 2, work_bank())]
 
-        gaps = row("right2_term2")
+        gaps = row("turned1")
         steps = row("steps")
         for cols in HALVES:
             window = knots2[3][:].indirect(part_of(right2_t, cols))

@@ -247,40 +247,39 @@ def tile_picked_ynhits_err_p_kernel(
         knots(h_q[3], kn1_q, G, knots1[3], work_bank())
         add_turned(sums[0], weighted(knots1[0], left1_t[:], rest1, row("left1_term0")))
         add_turned(sums[1], weighted(knots1[1], right1_t[:], part1, row("right1_term1")), start=True)
+        add_turned(sums[1], weighted(knots1[1], left1_t[:], rest1, row("left1_term1")))
         kn2_q = quantize(kn2_grouped, W, "kn2")
-        right1_plain3 = fetched(knots1[3], right1_t[:], row("kn2_raw"))
-        for b in (0, 1, 2, 3):
+        plains3 = held([P, 2, R], F32, "kn2_raw")
+        right1_plain3 = fetched(knots1[3], right1_t[:], plains3[:, 0, :])
+        left1_plain3 = fetched(knots1[3], left1_t[:], plains3[:, 1, :])
+        for b in range(BLOCKS):
             knots(h_q[b], kn2_q, W, knots2[b], work_bank())
-        plains = held([P, 3, R], F32, "kn2_codes")
-        left2_plain1 = fetched(knots2[1], left2_t[:], plains[:, 0, :])
-        left1_plain3 = fetched(knots1[3], left1_t[:], plains[:, 1, :])
+        left2_plain1 = fetched(knots2[1], left2_t[:], row("kn2_codes"))
         left2_plain3 = fetched(knots2[3], left2_t[:], row("kn2_scales"))
-        after_kn2 = held([P, 2, R], F32, "kn2_grouped")
-        add_turned(sums[1], weighted(knots1[1], left1_t[:], rest1, after_kn2[:, 0, :]))
-        add_turned(sums[0], true_t[:, 0, :])
         sums2 = [bank("bank2"), work_bank()]
-        add_halves(weighted(knots1[2], right1_t[:], part1, after_kn2[:, 1, :]), start=True)
+        add_halves(weighted(knots1[2], right1_t[:], part1, row("kn2_grouped")), start=True)
         add_turned(sums[3], times(right1_plain3, part1, row("right1_term3")), start=True)
-        add_turned(sums[1], true_t[:, 1, :])
+        add_turned(sums[3], times(left1_plain3, rest1, row("left1_term3")))
+        add_turned(sums[0], true_t[:, 0, :])
         add_turned(sums[0], weighted(knots2[0], right2_t[:], part2, row("right2_term0")))
+        add_turned(sums[1], true_t[:, 1, :])
         add_turned(sums[3], true_t[:, 3, :])
         add_turned(sums[0], weighted(knots2[0], left2_t[:], rest2, row("left2_term0")), stop=True)
         turned0 = turn_out(sums[0], R, ACT.Abs, "turned0")
         left1_plain2 = fetched(knots1[2], left1_t[:], row("left2_term0"))
-        add_halves(true_t[:, 2, :])
+        add_turned(sums[3], left2_plain3, stop=True)
+        turned3 = turn_out(sums[3], R, ACT.Copy, "turned3")
         add_turned(sums[1], weighted(knots2[1], right2_t[:], part2, row("right2_term1")))
-        add_turned(sums[3], left2_plain3)
+        back0 = turn_in(turned0, R, work_bank())
         add_turned(sums[1], times(left2_plain1, rest2, row("left2_term1")), stop=True)
         turned1 = turn_out(sums[1], R, ACT.Abs, "turned1")
-        back0 = turn_in(turned0, R, work_bank())
-        add_turned(sums[3], times(left1_plain3, rest1, row("left1_term3")), stop=True)
-        turned3 = turn_out(sums[3], R, ACT.Copy, "turned3")
-        store(0, back0, whole, "left1_term3")
-        late_terms = held([P, 2, R], F32, "kn2_codes")
+        store(0, back0, whole, "left2_term1")
+        add_halves(true_t[:, 2, :])
+        late_terms = held([P, 2, R], F32, "right2_term0")
         add_halves(weighted(knots2[2], right2_t[:], part2, late_terms[:, 0, :]))
+        partial = turn_in(turned3, R, work_bank())
         back1 = turn_in(turned1, R, bank("bank0"))
         store(1, back1, whole, "result1")
-        partial = turn_in(turned3, R, work_bank())
         add_halves(weighted(knots2[2], left2_t[:], rest2, late_terms[:, 1, :]))
 
         last_term = row("left1_term2")

@@ -45,7 +45,7 @@ def tile_picked_ynhits_err_p_kernel(
             return psum.tile([P, R], F32, name=name, tag=name, bufs=1)
 
         def work_bank():
-            return psum.tile([P, R], F32, name="work_bank", tag="work_bank", bufs=4)
+            return psum.tile([P, R], F32, name="work_bank", tag="work_bank", bufs=3)
 
         def load_list(src, name):
             lst = held([P, R // 16], U16, name)
@@ -184,6 +184,18 @@ def tile_picked_ynhits_err_p_kernel(
             else:
                 nc.scalar.activation(window[:, :width], acc[:, :width], ACT.Copy, scale=-1.0)
 
+        def warm_up(widths, acc):
+            for width in widths:
+                nc.tensor.matmul_mx(
+                    out=acc[:, :width],
+                    lhsT=h_q[2][0][:].bitcast(FP8X4),
+                    lhsT_scale=h_q[2][1][:],
+                    rhs=w1_q[0][0][:, :width].bitcast(FP8X4),
+                    rhs_scale=w1_q[0][1][:, :width],
+                    start=True,
+                    stop=True,
+                )
+
         def add_turned(total, term, start=False, stop=False):
             chunks = term.shape[1] // P
             for c in range(chunks):
@@ -253,7 +265,7 @@ def tile_picked_ynhits_err_p_kernel(
         right1_plain3 = fetched(knots1[3], right1_t[:], plains3[:, 0, :])
         left1_plain3 = fetched(knots1[3], left1_t[:], plains3[:, 1, :])
         for b in range(BLOCKS):
-            knots(h_q[b], kn2_q, W, knots2[b], work_bank())
+            knots(h_q[b], kn2_q, W, knots2[b], bank("spare") if b == 3 else work_bank())
         left2_plain1 = fetched(knots2[1], left2_t[:], row("kn2_codes"))
         left2_plain3 = fetched(knots2[3], left2_t[:], row("kn2_scales"))
         sums2 = [bank("bank2"), work_bank()]
@@ -264,6 +276,7 @@ def tile_picked_ynhits_err_p_kernel(
         add_turned(sums[0], weighted(knots2[0], right2_t[:], part2, row("right2_term0")))
         add_turned(sums[1], true_t[:, 1, :])
         add_turned(sums[3], true_t[:, 3, :])
+        warm_up((W, G), bank("spare"))
         add_turned(sums[0], weighted(knots2[0], left2_t[:], rest2, row("left2_term0")), stop=True)
         turned0 = turn_out(sums[0], R, ACT.Abs, "turned0")
         left1_plain2 = fetched(knots1[2], left1_t[:], row("left2_term0"))
@@ -275,6 +288,7 @@ def tile_picked_ynhits_err_p_kernel(
         turned1 = turn_out(sums[1], R, ACT.Abs, "turned1")
         store(0, back0, whole, "left2_term1")
         add_halves(true_t[:, 2, :])
+        warm_up((W, W), bank("bank0"))
         late_terms = held([P, 2, R], F32, "right2_term0")
         add_halves(weighted(knots2[2], right2_t[:], part2, late_terms[:, 0, :]))
         partial = turn_in(turned3, R, work_bank())
@@ -287,9 +301,9 @@ def tile_picked_ynhits_err_p_kernel(
         for i, cols in enumerate(HALVES):
             add_turned(sums2[i], times(left1_plain2[:, cols], rest1[:, cols], last_term[:, cols]), stop=True)
             turned2.append(turn_out(sums2[i], R // 2, ACT.Abs, "turned2_%d" % i))
-        backs2 = [turn_in(turned2[0], R // 2, bank("bank1")), turn_in(turned2[1], R // 2, work_bank())]
+        backs2 = [turn_in(turned2[0], R // 2, bank("bank1")), turn_in(turned2[1], R // 2, bank("spare"))]
 
-        gaps = row("turned1")
+        gaps = row("turned0")
         steps = row("steps")
         for cols in HALVES:
             window = knots2[3][:].indirect(part_of(right2_t, cols))

@@ -44,9 +44,6 @@ def tile_picked_ynhits_err_p_kernel(
         def bank(name):
             return psum.tile([P, R], F32, name=name, tag=name, bufs=1)
 
-        def work_bank():
-            return psum.tile([P, R], F32, name="work_bank", tag="work_bank", bufs=3)
-
         def load_list(src, name):
             lst = held([P, R // 16], U16, name)
             nc.sync.dma_start(lst[:], src)
@@ -89,11 +86,13 @@ def tile_picked_ynhits_err_p_kernel(
         kn1_raw = load_rows(kn1, G, "kn1_raw")
         right1_t = load_list(right1, "right1_t")
         left1_t = load_list(left1, "left1_t")
-        kn2_raw = load_rows(kn2, W, "kn2_raw")
+        kn2_raw = [load_rows(kn2[:, cols], W // 2, "kn2_raw%d" % i) for i, cols in enumerate(HALVES)]
         right2_t = load_list(right2, "right2_t")
         left2_t = load_list(left2, "left2_t")
-        true_t = held([P, BLOCKS, R], F32, "true_t")
-        nc.sync.dma_start(true_t[:], true.rearrange("(b p) r -> p b r", p=P))
+        true_t = {}
+        for b in (1, 2, 3, 0):
+            true_t[b] = row("true%d" % b)
+            nc.sync.dma_start(true_t[b], true[b * P : (b + 1) * P, :])
 
         knots1 = [held([P, WINDOW], F32, "knots1_%d" % b) for b in range(BLOCKS)]
         knots2 = [held([P, WINDOW], F32, "knots2_%d" % b) for b in range(BLOCKS)]
@@ -115,13 +114,14 @@ def tile_picked_ynhits_err_p_kernel(
                 nc.vector.tensor_copy(dst, src)
             w1_q.append(quantize(grouped, H, "w1_%d" % o))
 
-        turned_rows = work_bank()
+        turned_rows = bank("diff_a")
         nc.tensor.transpose(turned_rows[:, :P], frac_rows[:], identity[:])
         frac_cols = held([P, 2 * CHUNKS], F32, "frac_cols")
         nc.scalar.copy(frac_cols[:], turned_rows[:, : 2 * CHUNKS])
+        minus_frac1 = held([P, CHUNKS], F32, "minus_frac1")
+        nc.scalar.activation(minus_frac1[:], turned_rows[:, :CHUNKS], ACT.Copy, scale=-1.0)
 
-        def spread(first, name):
-            spread_rows = work_bank()
+        def spread(first, name, spread_rows):
             for c in range(CHUNKS):
                 column = frac_cols[:, first + c : first + c + 1]
                 nc.tensor.transpose(spread_rows[:, c * P : (c + 1) * P], column.to_broadcast([P, P]), identity[:])
@@ -131,8 +131,8 @@ def tile_picked_ynhits_err_p_kernel(
             nc.scalar.activation(rest, spread_rows[:], ACT.Copy, scale=-1.0, bias=1.0)
             return part, rest
 
-        part1, rest1 = spread(0, "frac1")
-        part2, rest2 = spread(CHUNKS, "frac2")
+        part1, rest1 = spread(0, "frac1", bank("sum0"))
+        part2, rest2 = spread(CHUNKS, "frac2", bank("sum1"))
 
         x_codes = [[None, None] for o in range(PASSES)]
         for o in range(PASSES):
@@ -142,13 +142,11 @@ def tile_picked_ynhits_err_p_kernel(
                 nc.vector.tensor_copy(picked[:], x_table[o][:].indirect(offs_t[:, cols]))
                 x_codes[o][half] = picked
 
-        def interleave(raw, width, name, engine_copy):
-            grouped = held([P, PACK * width], BF16, name)
-            engine_copy(
-                grouped[:].rearrange("p (c i j) -> p c j i", i=PACK, j=PACK),
+        def interleave(raw, grouped):
+            nc.vector.tensor_copy(
+                grouped.rearrange("p (c i j) -> p c j i", i=PACK, j=PACK),
                 raw[:].rearrange("p j (c i) -> p c j i", i=PACK),
             )
-            return grouped
 
         def hidden_block(b, acc):
             half, first = divmod(b * P, HALF)
@@ -169,45 +167,35 @@ def tile_picked_ynhits_err_p_kernel(
             )
             return hidden
 
-        def knots(h_q, kn_q, width, window, acc, on_vector=False):
+        def product(stationary, moving, acc):
+            width = acc.shape[1]
             nc.tensor.matmul_mx(
-                out=acc[:, :width],
-                lhsT=h_q[0][:].bitcast(FP8X4),
-                lhsT_scale=h_q[1][:],
-                rhs=kn_q[0][:].bitcast(FP8X4),
-                rhs_scale=kn_q[1][:],
+                out=acc,
+                lhsT=stationary[0][:].bitcast(FP8X4),
+                lhsT_scale=stationary[1][:],
+                rhs=moving[0][:, :width].bitcast(FP8X4),
+                rhs_scale=moving[1][:, :width],
                 start=True,
                 stop=True,
             )
-            if on_vector:
-                nc.vector.tensor_scalar_mul(window[:, :width], acc[:, :width], -1.0)
-            else:
-                nc.scalar.activation(window[:, :width], acc[:, :width], ACT.Copy, scale=-1.0)
 
-        def warm_up(widths, acc):
-            for width in widths:
-                nc.tensor.matmul_mx(
-                    out=acc[:, :width],
-                    lhsT=h_q[2][0][:].bitcast(FP8X4),
-                    lhsT_scale=h_q[2][1][:],
-                    rhs=w1_q[0][0][:, :width].bitcast(FP8X4),
-                    rhs_scale=w1_q[0][1][:, :width],
-                    start=True,
-                    stop=True,
-                )
+        def warm_up(acc):
+            product(h_q[0], w1_q[0], acc)
+
+        def knots_out(acc, window):
+            nc.scalar.activation(window[:, : acc.shape[1]], acc, ACT.Copy, scale=-1.0)
+
+        def knots(b, kn_q, window, acc):
+            product(h_q[b], kn_q, acc)
+            knots_out(acc, window)
 
         def add_turned(total, term, start=False, stop=False):
-            chunks = term.shape[1] // P
-            for c in range(chunks):
+            for c in range(CHUNKS):
                 cols = slice(c * P, (c + 1) * P)
                 nc.tensor.matmul(
                     total[:, cols], term[:, cols], identity[:], is_transpose=True,
-                    start=(start and c == 0), stop=(stop and c == chunks - 1),
+                    start=(start and c == 0), stop=(stop and c == CHUNKS - 1),
                 )
-
-        def add_halves(term, start=False):
-            for total, cols in zip(sums2, HALVES):
-                add_turned(total, term[:, cols], start=start)
 
         def part_of(lst, cols):
             return lst[:, cols.start // 16 : cols.stop // 16]
@@ -216,105 +204,117 @@ def tile_picked_ynhits_err_p_kernel(
             nc.vector.tensor_tensor(term, window[:].indirect(lst), weight, ALU.mult)
             return term
 
-        def fetched(window, lst, plain):
-            nc.scalar.activation(plain, window[:].indirect(lst), ACT.Copy)
+        def fetched(window, lst, plain, sign):
+            nc.scalar.activation(plain, window[:].indirect(lst), ACT.Copy, scale=sign)
             return plain
 
-        def times(plain, weight, term):
-            nc.vector.tensor_tensor(term, plain, weight, ALU.mult)
-            return term
-
-        def turn_out(total, width, func, name):
-            turned = held([P, width], F32, name)
-            nc.scalar.activation(turned[:], total[:, :width], func)
+        def turn_out(total, name):
+            turned = row(name)
+            nc.scalar.copy(turned, total[:])
             return turned
 
-        def turn_in(turned, width, back):
-            for c in range(width // P):
+        def interpolate(diff, turned, name):
+            whole = row(name)
+            for c in range(CHUNKS):
+                cols = slice(c * P, (c + 1) * P)
+                nc.vector.scalar_tensor_tensor(
+                    whole[:, cols], diff[:, cols], minus_frac1[:, c : c + 1], turned[:, cols], ALU.mult, ALU.add
+                )
+            return whole
+
+        def turn_in(turned, back):
+            for c in range(CHUNKS):
                 cols = slice(c * P, (c + 1) * P)
                 nc.tensor.transpose(back[:, cols], turned[:, cols], identity[:])
             return back
 
-        def store(b, back, cols, name):
-            width = cols.stop - cols.start
-            result = held([P, width], F32, name)
-            nc.scalar.copy(result[:], back[:, :width])
-            nc.sync.dma_start(out[b * P : (b + 1) * P, cols], result[:])
+        def store(b, back):
+            result = row("result%d" % b)
+            nc.scalar.activation(result, back[:], ACT.Abs)
+            nc.sync.dma_start(out[b * P : (b + 1) * P, :], result)
 
-        whole = slice(0, R)
-        kn1_grouped = interleave(kn1_raw, G, "kn1_grouped", nc.vector.tensor_copy)
-        hidden = [hidden_block(b, bank("bank%d" % b)) for b in range(BLOCKS)]
-        h_q = [quantize(hidden[0], P, "h0")]
+        kn1_grouped = held([P, PACK * G], BF16, "kn1_grouped")
+        interleave(kn1_raw, kn1_grouped[:])
+        hidden = {b: hidden_block(b, bank(name)) for b, name in ((1, "diff_b"), (0, "sum2"), (2, "sum3"))}
         kn1_q = quantize(kn1_grouped, G, "kn1")
-        h_q.append(quantize(hidden[1], P, "h1"))
-        knots(h_q[0], kn1_q, G, knots1[0], work_bank(), on_vector=True)
-        knots(h_q[1], kn1_q, G, knots1[1], work_bank())
-        h_q.append(quantize(hidden[2], P, "h2"))
-        knots(h_q[2], kn1_q, G, knots1[2], work_bank())
-
-        sums = {b: bank("bank%d" % b) for b in (0, 1, 3)}
-        add_turned(sums[0], weighted(knots1[0], right1_t[:], part1, row("right1_term0")), start=True)
-        h_q.append(quantize(hidden[3], P, "h3"))
-        kn2_grouped = interleave(kn2_raw, W, "kn2_grouped", lambda dst, src: nc.scalar.activation(dst, src, ACT.Copy))
-        knots(h_q[3], kn1_q, G, knots1[3], work_bank())
-        add_turned(sums[0], weighted(knots1[0], left1_t[:], rest1, row("left1_term0")))
-        add_turned(sums[1], weighted(knots1[1], right1_t[:], part1, row("right1_term1")), start=True)
-        add_turned(sums[1], weighted(knots1[1], left1_t[:], rest1, row("left1_term1")))
+        h_q = {b: quantize(hidden[b], P, "h%d" % b) for b in (1, 0)}
+        kn2_grouped = held([P, PACK * W], BF16, "hidden0")
+        interleave(kn2_raw[0], kn2_grouped[:, : PACK * W // 2])
+        h_q[2] = quantize(hidden[2], P, "h2")
+        interleave(kn2_raw[1], kn2_grouped[:, PACK * W // 2 :])
         kn2_q = quantize(kn2_grouped, W, "kn2")
-        plains3 = held([P, 2, R], F32, "kn2_raw")
-        right1_plain3 = fetched(knots1[3], right1_t[:], plains3[:, 0, :])
-        left1_plain3 = fetched(knots1[3], left1_t[:], plains3[:, 1, :])
-        for b in range(BLOCKS):
-            knots(h_q[b], kn2_q, W, knots2[b], bank("spare") if b == 3 else work_bank())
-        left2_plain1 = fetched(knots2[1], left2_t[:], row("kn2_codes"))
-        left2_plain3 = fetched(knots2[3], left2_t[:], row("kn2_scales"))
-        sums2 = [bank("bank2"), work_bank()]
-        add_halves(weighted(knots1[2], right1_t[:], part1, row("kn2_grouped")), start=True)
-        add_turned(sums[3], times(right1_plain3, part1, row("right1_term3")), start=True)
-        add_turned(sums[3], times(left1_plain3, rest1, row("left1_term3")))
-        add_turned(sums[0], true_t[:, 0, :])
-        add_turned(sums[0], weighted(knots2[0], right2_t[:], part2, row("right2_term0")))
-        add_turned(sums[1], true_t[:, 1, :])
-        add_turned(sums[3], true_t[:, 3, :])
-        warm_up((W, G), bank("spare"))
-        add_turned(sums[0], weighted(knots2[0], left2_t[:], rest2, row("left2_term0")), stop=True)
-        turned0 = turn_out(sums[0], R, ACT.Abs, "turned0")
-        left1_plain2 = fetched(knots1[2], left1_t[:], row("left2_term0"))
-        add_turned(sums[3], left2_plain3, stop=True)
-        turned3 = turn_out(sums[3], R, ACT.Copy, "turned3")
-        add_turned(sums[1], weighted(knots2[1], right2_t[:], part2, row("right2_term1")))
-        back0 = turn_in(turned0, R, work_bank())
-        add_turned(sums[1], times(left2_plain1, rest2, row("left2_term1")), stop=True)
-        turned1 = turn_out(sums[1], R, ACT.Abs, "turned1")
-        store(0, back0, whole, "left2_term1")
-        add_halves(true_t[:, 2, :])
-        warm_up((W, W), bank("bank0"))
-        late_terms = held([P, 2, R], F32, "right2_term0")
-        add_halves(weighted(knots2[2], right2_t[:], part2, late_terms[:, 0, :]))
-        partial = turn_in(turned3, R, work_bank())
-        back1 = turn_in(turned1, R, bank("bank0"))
-        store(1, back1, whole, "result1")
-        add_halves(weighted(knots2[2], left2_t[:], rest2, late_terms[:, 1, :]))
+        knots(1, kn1_q, knots1[1], bank("work_a")[:, :G])
+        left1_1 = fetched(knots1[1], left1_t[:], row("left1_1"), 1.0)
+        knots(0, kn1_q, knots1[0], bank("work_b")[:, :G])
+        right1_1 = fetched(knots1[1], right1_t[:], row("right1_1"), -1.0)
+        early2 = bank("diff_b")[:, :G]
+        product(h_q[2], kn1_q, early2)
 
-        last_term = row("left1_term2")
-        turned2 = []
-        for i, cols in enumerate(HALVES):
-            add_turned(sums2[i], times(left1_plain2[:, cols], rest1[:, cols], last_term[:, cols]), stop=True)
-            turned2.append(turn_out(sums2[i], R // 2, ACT.Abs, "turned2_%d" % i))
-        backs2 = [turn_in(turned2[0], R // 2, bank("bank1")), turn_in(turned2[1], R // 2, bank("spare"))]
+        sums = [bank("sum%d" % b) for b in range(BLOCKS)]
+        add_turned(sums[1], true_t[1], start=True)
+        add_turned(sums[2], true_t[2], start=True)
+        add_turned(sums[1], left1_1)
+        knots(1, kn2_q, knots2[1], bank("diff_a")[:])
+        knots_out(early2, knots1[2])
+        left1_2 = fetched(knots1[2], left1_t[:], row("h1_codes"), 1.0)
+        knots(2, kn2_q, knots2[2], bank("work_a")[:])
+        right1_2 = fetched(knots1[2], right1_t[:], row("h2_codes"), -1.0)
+        add_turned(sums[3], true_t[3], start=True)
+        terms0 = held([P, 2, R], F32, "hidden0")
+        add_turned(sums[0], weighted(knots1[0], right1_t[:], part1, terms0[:, 0, :]), start=True)
+        weighted(knots1[0], left1_t[:], rest1, terms0[:, 1, :])
+        diff1 = bank("diff_a")
+        add_turned(diff1, left1_1, start=True)
+        add_turned(diff1, right1_1, stop=True)
+        add_turned(sums[0], true_t[0])
+        add_turned(sums[1], weighted(knots2[1], left2_t[:], rest2, row("left2_1")))
+        right2_1 = weighted(knots2[1], right2_t[:], part2, row("right2_1"))
+        left2_2 = weighted(knots2[2], left2_t[:], rest2, row("left2_2"))
+        h_q[3] = quantize(hidden_block(3, bank("work_a")), P, "h3")
+        add_turned(sums[1], right2_1, stop=True)
+        turned1 = turn_out(sums[1], "turned1")
+        diff2 = bank("diff_b")
+        add_turned(sums[2], left1_2)
+        add_turned(diff2, left1_2, start=True)
+        knots(3, kn2_q, knots2[3], bank("work_b")[:])
+        shared = bank("work_a")
+        warm_up(shared[:, G:])
+        knots(3, kn1_q, knots1[3], shared[:, :G])
+        left1_3 = fetched(knots1[3], left1_t[:], row("left1_3"), 1.0)
+        right1_3 = fetched(knots1[3], right1_t[:], row("right1_3"), -1.0)
+        add_turned(diff2, right1_2, stop=True)
+        add_turned(sums[2], left2_2)
+        add_turned(sums[2], weighted(knots2[2], right2_t[:], part2, row("hidden3")), stop=True)
+        turned2 = turn_out(sums[2], "turned2")
+        whole1 = interpolate(diff1, turned1, "whole1")
+        shared = bank("diff_a")
+        warm_up(shared[:])
+        knots(0, kn2_q, knots2[0], shared[:])
+        store(1, turn_in(whole1, bank("sum1")))
+        diff3 = bank("work_b")
+        add_turned(sums[3], left1_3)
+        add_turned(diff3, left1_3, start=True)
+        add_turned(sums[3], weighted(knots2[3], left2_t[:], rest2, row("left2_3")))
+        right2_3 = weighted(knots2[3], right2_t[:], part2, row("right2_3"))
+        add_turned(diff3, right1_3, stop=True)
+        back2 = bank("sum2")
+        warm_up(back2[:])
+        warm_up(back2[:])
+        add_turned(sums[3], right2_3, stop=True)
+        turned3 = turn_out(sums[3], "turned3")
+        store(2, turn_in(interpolate(diff2, turned2, "whole2"), back2))
+        add_turned(sums[0], terms0[:, 1, :])
+        add_turned(sums[0], weighted(knots2[0], left2_t[:], rest2, row("left2_0")), stop=True)
+        turned0 = turn_out(sums[0], "turned0")
+        store(3, turn_in(interpolate(diff3, turned3, "whole3"), bank("sum3")))
+        partial = turn_in(turned0, bank("sum0"))
 
-        gaps = row("turned0")
-        steps = row("steps")
+        last_term = row("turned3")
         for cols in HALVES:
-            window = knots2[3][:].indirect(part_of(right2_t, cols))
-            nc.vector.tensor_tensor(gaps[:, cols], window, left2_plain3[:, cols], ALU.subtract)
-        for cols in HALVES:
-            times(gaps[:, cols], part2[:, cols], steps[:, cols])
-        for i, cols in enumerate(HALVES):
-            store(2, backs2[i], cols, "result2_%d" % i)
-        result3 = row("turned2_1")
+            weighted(knots2[0], part_of(right2_t, cols), part2[:, cols], last_term[:, cols])
         for i, cols in enumerate(HALVES):
             total = held([P, R // 2], F32, "total%d" % i)
-            nc.vector.tensor_tensor(total[:], partial[:, cols], steps[:, cols], ALU.add)
-            nc.scalar.activation(result3[:, cols], total[:], ACT.Abs)
-            nc.sync.dma_start(out[3 * P :, cols], result3[:, cols])
+            nc.vector.tensor_tensor(total[:], partial[:, cols], last_term[:, cols], ALU.add)
+            result = held([P, R // 2], F32, "result0_%d" % i)
+            nc.scalar.activation(result[:], total[:], ACT.Abs)
+            nc.sync.dma_start(out[:P, cols], result[:])

@@ -86,11 +86,11 @@ def tile_picked_ynhits_err_p_kernel(
         kn1_raw = load_rows(kn1, G, "kn1_raw")
         right1_t = load_list(right1, "right1_t")
         left1_t = load_list(left1, "left1_t")
-        kn2_raw = [load_rows(kn2[:, cols], W // 2, "kn2_raw%d" % i) for i, cols in enumerate(HALVES)]
+        kn2_raw = load_rows(kn2, W, "kn2_raw")
         right2_t = load_list(right2, "right2_t")
         left2_t = load_list(left2, "left2_t")
         true_t = {}
-        for b in (1, 2, 3, 0):
+        for b in (0, 1, 3, 2):
             true_t[b] = row("true%d" % b)
             nc.sync.dma_start(true_t[b], true[b * P : (b + 1) * P, :])
 
@@ -114,12 +114,12 @@ def tile_picked_ynhits_err_p_kernel(
                 nc.vector.tensor_copy(dst, src)
             w1_q.append(quantize(grouped, H, "w1_%d" % o))
 
-        turned_rows = bank("diff_a")
+        turned_rows = bank("work_c")
         nc.tensor.transpose(turned_rows[:, :P], frac_rows[:], identity[:])
         frac_cols = held([P, 2 * CHUNKS], F32, "frac_cols")
         nc.scalar.copy(frac_cols[:], turned_rows[:, : 2 * CHUNKS])
-        minus_frac1 = held([P, CHUNKS], F32, "minus_frac1")
-        nc.scalar.activation(minus_frac1[:], turned_rows[:, :CHUNKS], ACT.Copy, scale=-1.0)
+        minus_frac = held([P, 2 * CHUNKS], F32, "minus_frac")
+        nc.scalar.activation(minus_frac[:], turned_rows[:, : 2 * CHUNKS], ACT.Copy, scale=-1.0)
 
         def spread(first, name, spread_rows):
             for c in range(CHUNKS):
@@ -131,8 +131,8 @@ def tile_picked_ynhits_err_p_kernel(
             nc.scalar.activation(rest, spread_rows[:], ACT.Copy, scale=-1.0, bias=1.0)
             return part, rest
 
-        part1, rest1 = spread(0, "frac1", bank("sum0"))
-        part2, rest2 = spread(CHUNKS, "frac2", bank("sum1"))
+        part1, rest1 = spread(0, "frac1", bank("work_a"))
+        part2, rest2 = spread(CHUNKS, "frac2", bank("work_b"))
 
         x_codes = [[None, None] for o in range(PASSES)]
         for o in range(PASSES):
@@ -142,8 +142,8 @@ def tile_picked_ynhits_err_p_kernel(
                 nc.vector.tensor_copy(picked[:], x_table[o][:].indirect(offs_t[:, cols]))
                 x_codes[o][half] = picked
 
-        def interleave(raw, grouped):
-            nc.vector.tensor_copy(
+        def interleave(raw, grouped, engine_copy):
+            engine_copy(
                 grouped.rearrange("p (c i j) -> p c j i", i=PACK, j=PACK),
                 raw[:].rearrange("p j (c i) -> p c j i", i=PACK),
             )
@@ -208,19 +208,16 @@ def tile_picked_ynhits_err_p_kernel(
             nc.scalar.activation(plain, window[:].indirect(lst), ACT.Copy, scale=sign)
             return plain
 
-        def turn_out(total, name):
+        def turn_out(total, func, name):
             turned = row(name)
-            nc.scalar.copy(turned, total[:])
+            nc.scalar.activation(turned, total[:], func)
             return turned
 
-        def interpolate(diff, turned, name):
-            whole = row(name)
-            for c in range(CHUNKS):
-                cols = slice(c * P, (c + 1) * P)
-                nc.vector.scalar_tensor_tensor(
-                    whole[:, cols], diff[:, cols], minus_frac1[:, c : c + 1], turned[:, cols], ALU.mult, ALU.add
-                )
-            return whole
+        def scaled(diff, rate, name):
+            step = held([P, CHUNKS, P], F32, name)
+            weight = minus_frac[:, rate * CHUNKS : (rate + 1) * CHUNKS].unsqueeze(2).to_broadcast([P, CHUNKS, P])
+            nc.vector.tensor_tensor(step[:], diff[:].rearrange("p (c t) -> p c t", c=CHUNKS), weight, ALU.mult)
+            return step[:].rearrange("p c t -> p (c t)")
 
         def turn_in(turned, back):
             for c in range(CHUNKS):
@@ -228,93 +225,101 @@ def tile_picked_ynhits_err_p_kernel(
                 nc.tensor.transpose(back[:, cols], turned[:, cols], identity[:])
             return back
 
-        def store(b, back):
+        def store(b, back, func):
             result = row("result%d" % b)
-            nc.scalar.activation(result, back[:], ACT.Abs)
+            nc.scalar.activation(result, back[:], func)
             nc.sync.dma_start(out[b * P : (b + 1) * P, :], result)
 
         kn1_grouped = held([P, PACK * G], BF16, "kn1_grouped")
-        interleave(kn1_raw, kn1_grouped[:])
-        hidden = {b: hidden_block(b, bank(name)) for b, name in ((1, "diff_b"), (0, "sum2"), (2, "sum3"))}
+        interleave(kn1_raw, kn1_grouped[:], nc.vector.tensor_copy)
+        hidden = [hidden_block(b, bank("sum%d" % b)) for b in range(BLOCKS)]
+        h_q = [quantize(hidden[0], P, "h0")]
         kn1_q = quantize(kn1_grouped, G, "kn1")
-        h_q = {b: quantize(hidden[b], P, "h%d" % b) for b in (1, 0)}
-        kn2_grouped = held([P, PACK * W], BF16, "hidden0")
-        interleave(kn2_raw[0], kn2_grouped[:, : PACK * W // 2])
-        h_q[2] = quantize(hidden[2], P, "h2")
-        interleave(kn2_raw[1], kn2_grouped[:, PACK * W // 2 :])
-        kn2_q = quantize(kn2_grouped, W, "kn2")
-        knots(1, kn1_q, knots1[1], bank("work_a")[:, :G])
-        left1_1 = fetched(knots1[1], left1_t[:], row("left1_1"), 1.0)
-        knots(0, kn1_q, knots1[0], bank("work_b")[:, :G])
-        right1_1 = fetched(knots1[1], right1_t[:], row("right1_1"), -1.0)
-        early2 = bank("diff_b")[:, :G]
-        product(h_q[2], kn1_q, early2)
+        h_q.append(quantize(hidden[1], P, "h1"))
+        first = bank("work_a")[:, :G]
+        product(h_q[0], kn1_q, first)
+        nc.vector.tensor_scalar_mul(knots1[0][:, :G], first, -1.0)
+        knots(1, kn1_q, knots1[1], bank("work_b")[:, :G])
+        h_q.append(quantize(hidden[2], P, "h2"))
+        knots(2, kn1_q, knots1[2], bank("work_c")[:, :G])
+        right1_0 = weighted(knots1[0], right1_t[:], part1, row("right1_0"))
+        h_q.append(quantize(hidden[3], P, "h3"))
+        kn2_grouped = held([P, PACK * W], BF16, "kn2_grouped")
+        interleave(kn2_raw, kn2_grouped[:], lambda dst, src: nc.scalar.activation(dst, src, ACT.Copy))
+        knots(3, kn1_q, knots1[3], bank("diff3")[:, :G])
 
         sums = [bank("sum%d" % b) for b in range(BLOCKS)]
+        add_turned(sums[0], true_t[0], start=True)
         add_turned(sums[1], true_t[1], start=True)
-        add_turned(sums[2], true_t[2], start=True)
-        add_turned(sums[1], left1_1)
-        knots(1, kn2_q, knots2[1], bank("diff_a")[:])
-        knots_out(early2, knots1[2])
-        left1_2 = fetched(knots1[2], left1_t[:], row("h1_codes"), 1.0)
-        knots(2, kn2_q, knots2[2], bank("work_a")[:])
-        right1_2 = fetched(knots1[2], right1_t[:], row("h2_codes"), -1.0)
+        add_turned(sums[0], right1_0)
         add_turned(sums[3], true_t[3], start=True)
-        terms0 = held([P, 2, R], F32, "hidden0")
-        add_turned(sums[0], weighted(knots1[0], right1_t[:], part1, terms0[:, 0, :]), start=True)
-        weighted(knots1[0], left1_t[:], rest1, terms0[:, 1, :])
-        diff1 = bank("diff_a")
-        add_turned(diff1, left1_1, start=True)
-        add_turned(diff1, right1_1, stop=True)
-        add_turned(sums[0], true_t[0])
-        add_turned(sums[1], weighted(knots2[1], left2_t[:], rest2, row("left2_1")))
-        right2_1 = weighted(knots2[1], right2_t[:], part2, row("right2_1"))
-        left2_2 = weighted(knots2[2], left2_t[:], rest2, row("left2_2"))
-        h_q[3] = quantize(hidden_block(3, bank("work_a")), P, "h3")
-        add_turned(sums[1], right2_1, stop=True)
-        turned1 = turn_out(sums[1], "turned1")
-        diff2 = bank("diff_b")
-        add_turned(sums[2], left1_2)
-        add_turned(diff2, left1_2, start=True)
-        knots(3, kn2_q, knots2[3], bank("work_b")[:])
-        shared = bank("work_a")
-        warm_up(shared[:, G:])
-        knots(3, kn1_q, knots1[3], shared[:, :G])
-        left1_3 = fetched(knots1[3], left1_t[:], row("left1_3"), 1.0)
-        right1_3 = fetched(knots1[3], right1_t[:], row("right1_3"), -1.0)
-        add_turned(diff2, right1_2, stop=True)
-        add_turned(sums[2], left2_2)
-        add_turned(sums[2], weighted(knots2[2], right2_t[:], part2, row("hidden3")), stop=True)
-        turned2 = turn_out(sums[2], "turned2")
-        whole1 = interpolate(diff1, turned1, "whole1")
-        shared = bank("diff_a")
-        warm_up(shared[:])
-        knots(0, kn2_q, knots2[0], shared[:])
-        store(1, turn_in(whole1, bank("sum1")))
-        diff3 = bank("work_b")
+        add_turned(sums[0], weighted(knots1[0], left1_t[:], rest1, row("left1_0")))
+        add_turned(sums[2], true_t[2], start=True)
+        add_turned(sums[1], weighted(knots1[1], right1_t[:], part1, row("right1_1")))
+        kn2_q = quantize(kn2_grouped, W, "kn2")
+        plains3 = held([P, 2, R], F32, "kn2_raw")
+        left1_3 = fetched(knots1[3], left1_t[:], plains3[:, 0, :], 1.0)
+        right1_3 = fetched(knots1[3], right1_t[:], plains3[:, 1, :], -1.0)
+        knots(3, kn2_q, knots2[3], bank("work_a")[:])
+        knots(0, kn2_q, knots2[0], bank("work_b")[:])
+        left2_3 = fetched(knots2[3], left2_t[:], row("left2_3"), 1.0)
+        knots(1, kn2_q, knots2[1], bank("work_c")[:])
+        diff3 = bank("diff3")
         add_turned(sums[3], left1_3)
         add_turned(diff3, left1_3, start=True)
-        add_turned(sums[3], weighted(knots2[3], left2_t[:], rest2, row("left2_3")))
-        right2_3 = weighted(knots2[3], right2_t[:], part2, row("right2_3"))
+        late1 = held([P, 3, R], F32, "kn2_grouped")
+        add_turned(sums[1], weighted(knots1[1], left1_t[:], rest1, late1[:, 0, :]))
+        shared = bank("work_b")[:]
+        warm_up(shared)
+        knots(2, kn2_q, knots2[2], shared)
+        left2_1 = fetched(knots2[1], left2_t[:], row("h2_codes"), 1.0)
         add_turned(diff3, right1_3, stop=True)
-        back2 = bank("sum2")
-        warm_up(back2[:])
-        warm_up(back2[:])
-        add_turned(sums[3], right2_3, stop=True)
-        turned3 = turn_out(sums[3], "turned3")
-        store(2, turn_in(interpolate(diff2, turned2, "whole2"), back2))
-        add_turned(sums[0], terms0[:, 1, :])
-        add_turned(sums[0], weighted(knots2[0], left2_t[:], rest2, row("left2_0")), stop=True)
-        turned0 = turn_out(sums[0], "turned0")
-        store(3, turn_in(interpolate(diff3, turned3, "whole3"), bank("sum3")))
-        partial = turn_in(turned0, bank("sum0"))
+        add_turned(sums[2], weighted(knots1[2], right1_t[:], part1, late1[:, 1, :]))
+        add_turned(sums[3], left2_3, stop=True)
+        turned3 = turn_out(sums[3], ACT.Copy, "turned3")
+        add_turned(sums[2], weighted(knots1[2], left1_t[:], rest1, late1[:, 2, :]))
+        right2_1 = fetched(knots2[1], right2_t[:], row("kn2_grouped"), -1.0)
+        add_turned(sums[0], weighted(knots2[0], left2_t[:], rest2, row("left2_0")))
+        right2_0 = weighted(knots2[0], right2_t[:], part2, row("right2_0"))
+        spare = bank("work_b")
+        for width in (W, G,):
+            warm_up(spare[:, :width])
+        add_turned(sums[0], right2_0, stop=True)
+        add_turned(sums[1], left2_1, stop=True)
+        turned1 = turn_out(sums[1], ACT.Copy, "turned1")
+        turned0 = turn_out(sums[0], ACT.Abs, "h2_codes")
+        partial = bank("sum3")
+        for width in (W,):
+            warm_up(partial[:, :width])
+        left2_2 = weighted(knots2[2], left2_t[:], rest2, row("left2_2"))
+        right2_2 = weighted(knots2[2], right2_t[:], part2, row("right2_2"))
+        step3 = scaled(diff3, 0, "step3")
+        diff1 = bank("work_a")
+        add_turned(diff1, left2_1, start=True)
+        add_turned(sums[2], left2_2)
+        add_turned(diff1, right2_1, stop=True)
+        step1 = scaled(diff1, 1, "whole1")
+        add_turned(sums[2], right2_2, stop=True)
+        turned2 = turn_out(sums[2], ACT.Abs, "turned2")
+        back1 = bank("sum1")
+        add_turned(back1, turned1, start=True)
+        store(0, turn_in(turned0, bank("sum0")), ACT.Copy)
+        add_turned(back1, step1, stop=True)
+        store(1, back1, ACT.Abs)
+        add_turned(partial, turned3, start=True)
+        store(2, turn_in(turned2, bank("sum2")), ACT.Copy)
+        add_turned(partial, step3, stop=True)
 
-        last_term = row("turned3")
+        gaps = row("right2_2")
+        steps = row("steps")
         for cols in HALVES:
-            weighted(knots2[0], part_of(right2_t, cols), part2[:, cols], last_term[:, cols])
+            window = knots2[3][:].indirect(part_of(right2_t, cols))
+            nc.vector.tensor_tensor(gaps[:, cols], window, left2_3[:, cols], ALU.subtract)
+        for cols in HALVES:
+            nc.vector.tensor_tensor(steps[:, cols], gaps[:, cols], part2[:, cols], ALU.mult)
+        result = row("turned2")
         for i, cols in enumerate(HALVES):
             total = held([P, R // 2], F32, "total%d" % i)
-            nc.vector.tensor_tensor(total[:], partial[:, cols], last_term[:, cols], ALU.add)
-            result = held([P, R // 2], F32, "result0_%d" % i)
-            nc.scalar.activation(result[:], total[:], ACT.Abs)
-            nc.sync.dma_start(out[:P, cols], result[:])
+            nc.vector.tensor_tensor(total[:], partial[:, cols], steps[:, cols], ALU.add)
+            nc.scalar.activation(result[:, cols], total[:], ACT.Abs)
+            nc.sync.dma_start(out[3 * P :, cols], result[:, cols])

@@ -127,8 +127,8 @@ def tile_picked_ynhits_err_p_kernel(
                 nc.tensor.transpose(spread_rows[:, c * P : (c + 1) * P], column.to_broadcast([P, P]), identity[:])
             part = row(name + "_part")
             rest = row(name + "_rest")
-            nc.scalar.copy(part, spread_rows[:])
-            nc.scalar.activation(rest, spread_rows[:], ACT.Copy, scale=-1.0, bias=1.0)
+            nc.scalar.activation(part, spread_rows[:], ACT.Copy, scale=-1.0)
+            nc.scalar.activation(rest, spread_rows[:], ACT.Copy, bias=-1.0)
             return part, rest
 
         part1, rest1 = spread(0, "frac1", bank("work_a"))
@@ -183,7 +183,7 @@ def tile_picked_ynhits_err_p_kernel(
             product(h_q[0], w1_q[0], acc)
 
         def knots_out(acc, window):
-            nc.scalar.activation(window[:, : acc.shape[1]], acc, ACT.Copy, scale=-1.0)
+            nc.scalar.copy(window[:, : acc.shape[1]], acc)
 
         def knots(b, kn_q, window, acc):
             product(h_q[b], kn_q, acc)
@@ -208,9 +208,15 @@ def tile_picked_ynhits_err_p_kernel(
             nc.scalar.activation(plain, window[:].indirect(lst), ACT.Copy, scale=sign)
             return plain
 
+        def leave(dst, src, func):
+            if func == ACT.Copy:
+                nc.scalar.copy(dst, src)
+            else:
+                nc.scalar.activation(dst, src, func)
+
         def turn_out(total, func, name):
             turned = row(name)
-            nc.scalar.activation(turned, total[:], func)
+            leave(turned, total[:], func)
             return turned
 
         def scaled(diff, rate, name):
@@ -227,7 +233,7 @@ def tile_picked_ynhits_err_p_kernel(
 
         def store(b, back, func):
             result = row("result%d" % b)
-            nc.scalar.activation(result, back[:], func)
+            leave(result, back[:], func)
             nc.sync.dma_start(out[b * P : (b + 1) * P, :], result)
 
         kn1_grouped = held([P, PACK * G], BF16, "kn1_grouped")
@@ -238,7 +244,7 @@ def tile_picked_ynhits_err_p_kernel(
         h_q.append(quantize(hidden[1], P, "h1"))
         first = bank("work_a")[:, :G]
         product(h_q[0], kn1_q, first)
-        nc.vector.tensor_scalar_mul(knots1[0][:, :G], first, -1.0)
+        nc.vector.tensor_copy(knots1[0][:, :G], first)
         knots(1, kn1_q, knots1[1], bank("work_b")[:, :G])
         h_q.append(quantize(hidden[2], P, "h2"))
         knots(2, kn1_q, knots1[2], bank("work_c")[:, :G])
@@ -258,11 +264,11 @@ def tile_picked_ynhits_err_p_kernel(
         add_turned(sums[1], weighted(knots1[1], right1_t[:], part1, row("right1_1")))
         kn2_q = quantize(kn2_grouped, W, "kn2")
         plains3 = held([P, 2, R], F32, "kn2_raw")
-        left1_3 = fetched(knots1[3], left1_t[:], plains3[:, 0, :], 1.0)
-        right1_3 = fetched(knots1[3], right1_t[:], plains3[:, 1, :], -1.0)
+        left1_3 = fetched(knots1[3], left1_t[:], plains3[:, 0, :], -1.0)
+        right1_3 = fetched(knots1[3], right1_t[:], plains3[:, 1, :], 1.0)
         knots(3, kn2_q, knots2[3], bank("work_a")[:])
         knots(0, kn2_q, knots2[0], bank("work_b")[:])
-        left2_3 = fetched(knots2[3], left2_t[:], row("left2_3"), 1.0)
+        left2_3 = fetched(knots2[3], left2_t[:], row("left2_3"), -1.0)
         knots(1, kn2_q, knots2[1], bank("work_c")[:])
         diff3 = bank("diff3")
         add_turned(sums[3], left1_3)
@@ -272,13 +278,12 @@ def tile_picked_ynhits_err_p_kernel(
         shared = bank("work_b")[:]
         warm_up(shared)
         knots(2, kn2_q, knots2[2], shared)
-        left2_1 = fetched(knots2[1], left2_t[:], row("h2_codes"), 1.0)
+        left2_1 = fetched(knots2[1], left2_t[:], row("h2_codes"), -1.0)
         add_turned(diff3, right1_3, stop=True)
         add_turned(sums[2], weighted(knots1[2], right1_t[:], part1, late1[:, 1, :]))
         add_turned(sums[3], left2_3, stop=True)
-        turned3 = turn_out(sums[3], ACT.Copy, "turned3")
         add_turned(sums[2], weighted(knots1[2], left1_t[:], rest1, late1[:, 2, :]))
-        right2_1 = fetched(knots2[1], right2_t[:], row("kn2_grouped"), -1.0)
+        right2_1 = fetched(knots2[1], right2_t[:], row("kn2_grouped"), 1.0)
         add_turned(sums[0], weighted(knots2[0], left2_t[:], rest2, row("left2_0")))
         right2_0 = weighted(knots2[0], right2_t[:], part2, row("right2_0"))
         spare = bank("work_b")
@@ -288,9 +293,6 @@ def tile_picked_ynhits_err_p_kernel(
         add_turned(sums[1], left2_1, stop=True)
         turned1 = turn_out(sums[1], ACT.Copy, "turned1")
         turned0 = turn_out(sums[0], ACT.Abs, "h2_codes")
-        partial = bank("sum3")
-        for width in (W,):
-            warm_up(partial[:, :width])
         left2_2 = weighted(knots2[2], left2_t[:], rest2, row("left2_2"))
         right2_2 = weighted(knots2[2], right2_t[:], part2, row("right2_2"))
         step3 = scaled(diff3, 0, "step3")
@@ -298,23 +300,25 @@ def tile_picked_ynhits_err_p_kernel(
         add_turned(diff1, left2_1, start=True)
         add_turned(sums[2], left2_2)
         add_turned(diff1, right2_1, stop=True)
-        step1 = scaled(diff1, 1, "whole1")
+        step1 = scaled(diff1, 1, "step1")
+        whole3 = row("kn2_grouped")
+        nc.vector.tensor_tensor(whole3, sums[3][:], step3, ALU.add)
+        back1 = bank("sum1")
+        warm_up(back1[:])
+        store(0, turn_in(turned0, bank("sum0")), ACT.Copy)
         add_turned(sums[2], right2_2, stop=True)
         turned2 = turn_out(sums[2], ACT.Abs, "turned2")
-        back1 = bank("sum1")
         add_turned(back1, turned1, start=True)
-        store(0, turn_in(turned0, bank("sum0")), ACT.Copy)
         add_turned(back1, step1, stop=True)
         store(1, back1, ACT.Abs)
-        add_turned(partial, turned3, start=True)
         store(2, turn_in(turned2, bank("sum2")), ACT.Copy)
-        add_turned(partial, step3, stop=True)
+        partial = turn_in(whole3, bank("sum3"))
 
-        gaps = row("right2_2")
+        gaps = row("w1_0_codes")
         steps = row("steps")
         for cols in HALVES:
             window = knots2[3][:].indirect(part_of(right2_t, cols))
-            nc.vector.tensor_tensor(gaps[:, cols], window, left2_3[:, cols], ALU.subtract)
+            nc.vector.tensor_tensor(gaps[:, cols], window, left2_3[:, cols], ALU.add)
         for cols in HALVES:
             nc.vector.tensor_tensor(steps[:, cols], gaps[:, cols], part2[:, cols], ALU.mult)
         result = row("turned2")

@@ -87,12 +87,13 @@ def tile_picked_ynhits_err_p_kernel(
         right1_t = load_list(right1, "right1_t")
         left1_t = load_list(left1, "left1_t")
         kn2_raw = load_rows(kn2, W, "kn2_raw")
-        right2_t = load_list(right2, "right2_t")
-        left2_t = load_list(left2, "left2_t")
         true_t = {}
         for b in (0, 1, 3, 2):
             true_t[b] = row("true%d" % b)
             nc.sync.dma_start(true_t[b], true[b * P : (b + 1) * P, :])
+
+        left2_t = load_list(left2, "left2_t")
+        right2_t = load_list(right2, "right2_t")
 
         knots1 = [held([P, WINDOW], F32, "knots1_%d" % b) for b in range(BLOCKS)]
         knots2 = [held([P, WINDOW], F32, "knots2_%d" % b) for b in range(BLOCKS)]
@@ -118,8 +119,6 @@ def tile_picked_ynhits_err_p_kernel(
         nc.tensor.transpose(turned_rows[:, :P], frac_rows[:], identity[:])
         frac_cols = held([P, 2 * CHUNKS], F32, "frac_cols")
         nc.scalar.copy(frac_cols[:], turned_rows[:, : 2 * CHUNKS])
-        minus_frac = held([P, 2 * CHUNKS], F32, "minus_frac")
-        nc.scalar.activation(minus_frac[:], turned_rows[:, : 2 * CHUNKS], ACT.Copy, scale=-1.0)
 
         def spread(first, name, spread_rows):
             for c in range(CHUNKS):
@@ -133,6 +132,13 @@ def tile_picked_ynhits_err_p_kernel(
 
         part1, rest1 = spread(0, "frac1", bank("work_a"))
         part2, rest2 = spread(CHUNKS, "frac2", bank("work_b"))
+
+        turned_part = []
+        for rate in range(2):
+            wide = held([P, CHUNKS, P], F32, "turned_part%d" % rate)
+            columns = frac_cols[:, rate * CHUNKS : (rate + 1) * CHUNKS]
+            nc.scalar.activation(wide[:], columns.unsqueeze(2).to_broadcast([P, CHUNKS, P]), ACT.Copy, scale=-1.0)
+            turned_part.append(wide[:].rearrange("p c t -> p (c t)"))
 
         x_codes = [[None, None] for o in range(PASSES)]
         for o in range(PASSES):
@@ -220,10 +226,9 @@ def tile_picked_ynhits_err_p_kernel(
             return turned
 
         def scaled(diff, rate, name):
-            step = held([P, CHUNKS, P], F32, name)
-            weight = minus_frac[:, rate * CHUNKS : (rate + 1) * CHUNKS].unsqueeze(2).to_broadcast([P, CHUNKS, P])
-            nc.vector.tensor_tensor(step[:], diff[:].rearrange("p (c t) -> p c t", c=CHUNKS), weight, ALU.mult)
-            return step[:].rearrange("p c t -> p (c t)")
+            step = row(name)
+            nc.vector.tensor_tensor(step, diff[:], turned_part[rate], ALU.mult)
+            return step
 
         def turn_in(turned, back):
             for c in range(CHUNKS):
@@ -263,9 +268,9 @@ def tile_picked_ynhits_err_p_kernel(
         add_turned(sums[2], true_t[2], start=True)
         add_turned(sums[1], weighted(knots1[1], right1_t[:], part1, row("right1_1")))
         kn2_q = quantize(kn2_grouped, W, "kn2")
-        plains3 = held([P, 2, R], F32, "kn2_raw")
-        left1_3 = fetched(knots1[3], left1_t[:], plains3[:, 0, :], -1.0)
-        right1_3 = fetched(knots1[3], right1_t[:], plains3[:, 1, :], 1.0)
+        after_kn2 = held([P, 5, R], F32, "kn2_raw")
+        left1_3 = fetched(knots1[3], left1_t[:], after_kn2[:, 3, :], -1.0)
+        right1_3 = fetched(knots1[3], right1_t[:], after_kn2[:, 4, :], 1.0)
         knots(3, kn2_q, knots2[3], bank("work_a")[:])
         knots(0, kn2_q, knots2[0], bank("work_b")[:])
         left2_3 = fetched(knots2[3], left2_t[:], row("left2_3"), -1.0)
@@ -273,17 +278,16 @@ def tile_picked_ynhits_err_p_kernel(
         diff3 = bank("diff3")
         add_turned(sums[3], left1_3)
         add_turned(diff3, left1_3, start=True)
-        late1 = held([P, 3, R], F32, "kn2_grouped")
-        add_turned(sums[1], weighted(knots1[1], left1_t[:], rest1, late1[:, 0, :]))
+        add_turned(sums[1], weighted(knots1[1], left1_t[:], rest1, after_kn2[:, 0, :]))
         shared = bank("work_b")[:]
         warm_up(shared)
         knots(2, kn2_q, knots2[2], shared)
         left2_1 = fetched(knots2[1], left2_t[:], row("h2_codes"), -1.0)
         add_turned(diff3, right1_3, stop=True)
-        add_turned(sums[2], weighted(knots1[2], right1_t[:], part1, late1[:, 1, :]))
+        add_turned(sums[2], weighted(knots1[2], right1_t[:], part1, after_kn2[:, 1, :]))
         add_turned(sums[3], left2_3, stop=True)
-        add_turned(sums[2], weighted(knots1[2], left1_t[:], rest1, late1[:, 2, :]))
-        right2_1 = fetched(knots2[1], right2_t[:], row("kn2_grouped"), 1.0)
+        add_turned(sums[2], weighted(knots1[2], left1_t[:], rest1, after_kn2[:, 2, :]))
+        right2_1 = fetched(knots2[1], right2_t[:], row("kn2_raw"), 1.0)
         add_turned(sums[0], weighted(knots2[0], left2_t[:], rest2, row("left2_0")))
         right2_0 = weighted(knots2[0], right2_t[:], part2, row("right2_0"))
         spare = bank("work_b")
@@ -301,7 +305,7 @@ def tile_picked_ynhits_err_p_kernel(
         add_turned(sums[2], left2_2)
         add_turned(diff1, right2_1, stop=True)
         step1 = scaled(diff1, 1, "step1")
-        whole3 = row("kn2_grouped")
+        whole3 = row("kn2_raw")
         nc.vector.tensor_tensor(whole3, sums[3][:], step3, ALU.add)
         back1 = bank("sum1")
         warm_up(back1[:])

@@ -291,34 +291,37 @@ def tile_picked_ynhits_err_p_kernel(
         add_turned(sums[0], weighted(knots2[0], left2_t[:], rest2, row("left2_0")))
         right2_0 = weighted(knots2[0], right2_t[:], part2, row("right2_0"))
         spare = bank("work_b")
-        for width in (W, G,):
+        for width in (W, G):
             warm_up(spare[:, :width])
         add_turned(sums[0], right2_0, stop=True)
-        add_turned(sums[1], left2_1, stop=True)
-        turned1 = turn_out(sums[1], ACT.Copy, "turned1")
-        turned0 = turn_out(sums[0], ACT.Abs, "h2_codes")
         left2_2 = weighted(knots2[2], left2_t[:], rest2, row("left2_2"))
         right2_2 = weighted(knots2[2], right2_t[:], part2, row("right2_2"))
-        step3 = scaled(diff3, 0, "step3")
+        add_turned(sums[1], left2_1, stop=True)
+        turned0 = turn_out(sums[0], ACT.Abs, "turned0")
+        turned1 = turn_out(sums[1], ACT.Copy, "turned1")
         diff1 = bank("work_a")
         add_turned(diff1, left2_1, start=True)
-        add_turned(sums[2], left2_2)
+        turned3 = turn_out(sums[3], ACT.Copy, "h2_codes")
         add_turned(diff1, right2_1, stop=True)
         step1 = scaled(diff1, 1, "step1")
-        whole3 = row("kn2_raw")
-        nc.vector.tensor_tensor(whole3, sums[3][:], step3, ALU.add)
+        step3 = scaled(diff3, 0, "kn2_raw")
+        add_turned(sums[2], left2_2)
+        spare = bank("sum0")
+        for width in (W,):
+            warm_up(spare[:, :width])
+        store(0, turn_in(turned0, bank("work_b")), ACT.Copy)
         back1 = bank("sum1")
-        warm_up(back1[:])
-        store(0, turn_in(turned0, bank("sum0")), ACT.Copy)
+        add_turned(back1, turned1, start=True)
         add_turned(sums[2], right2_2, stop=True)
         turned2 = turn_out(sums[2], ACT.Abs, "turned2")
-        add_turned(back1, turned1, start=True)
         add_turned(back1, step1, stop=True)
         store(1, back1, ACT.Abs)
+        partial = bank("work_c")
+        add_turned(partial, turned3, start=True)
+        add_turned(partial, step3, stop=True)
         store(2, turn_in(turned2, bank("sum2")), ACT.Copy)
-        partial = turn_in(whole3, bank("sum3"))
 
-        gaps = row("w1_0_codes")
+        gaps = row("left2_2")
         steps = row("steps")
         for cols in HALVES:
             window = knots2[3][:].indirect(part_of(right2_t, cols))

@@ -65,44 +65,42 @@ def tile_picked_ynhits_err_p_kernel(
             nc.vector.quantize_mx(out=codes[:].bitcast(FP8X4), scales=scales[:], in_=grouped[:])
             return codes, scales
 
-        x_scale_rows = held([P, T], U8, "x_scale_rows")
-        nc.gpsimd.memset(x_scale_rows[:].bitcast(I32), 0)
-        frac_rows = held([P, P], F32, "frac_rows")
-        nc.gpsimd.memset(frac_rows[:], 0.0)
         identity = held([P, P], F32, "identity")
         make_identity(nc, identity[:])
+        x_scale_rows = held([P, PASSES, T], U8, "x_table1")
+        nc.vector.memset(x_scale_rows[:].rearrange("p o n -> p (o n)").bitcast(I32), 0)
+        x_scale = held([P, PASSES, S], U8, "x_scale")
+        nc.vector.memset(x_scale[:].rearrange("p o n -> p (o n)").bitcast(I32), 0)
 
-        offs_t = load_list(offs, "offs_t")
         w1_raw = [load_rows(w1[:K_PASS, :], H, "w1_raw0")]
-        for q in range(4):
-            nc.sync.dma_start(
-                x_scale_rows[32 * q : 32 * q + 4 * PASSES, :].bitcast(I32),
-                x_scales[:, 4 * q : 4 * q + 4, :].bitcast(I32),
-            )
+        offs_t = load_list(offs, "offs_t")
+        nc.sync.dma_start(x_scale_rows[::8].bitcast(I32), x_scales.rearrange("o q n -> q o n").bitcast(I32))
+        frac_cols = []
         for i, frac in enumerate((frac1, frac2)):
-            nc.sync.dma_start(frac_rows[i * CHUNKS : (i + 1) * CHUNKS, :], frac[0].rearrange("(c n) -> c n", n=P))
-        w1_raw.append(load_rows(w1[K_PASS:, :], H, "w1_raw1"))
-        x_table = [load_words(o) for o in range(PASSES)]
-        kn1_raw = load_rows(kn1, G, "kn1_raw")
+            frac_cols.append(held([P, PACK], F32, "frac_cols%d" % i))
+            nc.sync.dma_start(frac_cols[i][:], frac[0].rearrange("(p j) -> p j", j=PACK))
         right1_t = load_list(right1, "right1_t")
         left1_t = load_list(left1, "left1_t")
-        kn2_raw = load_rows(kn2, W, "kn2_raw")
-        true_t = {}
-        for b in (0, 1, 3, 2):
-            true_t[b] = row("true%d" % b)
-            nc.sync.dma_start(true_t[b], true[b * P : (b + 1) * P, :])
-
+        w1_raw.append(load_rows(w1[K_PASS:, :], H, "kn2_raw"))
+        x_table = [load_words(0)]
         left2_t = load_list(left2, "left2_t")
         right2_t = load_list(right2, "right2_t")
+
+        picked_scales = held([P, PASSES, S], U8, "picked_scales")
+        for o in range(PASSES):
+            nc.vector.tensor_copy(picked_scales[:, o, :], x_scale_rows[:, o, :].indirect(offs_t[:]))
+        for q in range(4):
+            nc.sync.dma_start(
+                x_scale[32 * q : 32 * q + 4].rearrange("p o n -> p (o n)").bitcast(I32),
+                picked_scales[32 * q : 32 * q + 32 : 8].rearrange("p o n -> p (o n)").bitcast(I32),
+            )
+        x_table.append(load_words(1))
 
         knots1 = [held([P, WINDOW], F32, "knots1_%d" % b) for b in range(BLOCKS)]
         knots2 = [held([P, WINDOW], F32, "knots2_%d" % b) for b in range(BLOCKS)]
         for b in range(BLOCKS):
             nc.vector.memset(knots1[b][:, G:], 0.0)
             nc.vector.memset(knots2[b][:, W:], 0.0)
-
-        x_scale = held([P, S], U8, "x_scale")
-        nc.vector.tensor_copy(x_scale[:], x_scale_rows[:].indirect(offs_t[:]))
 
         w1_q = []
         for o in range(PASSES):
@@ -115,30 +113,33 @@ def tile_picked_ynhits_err_p_kernel(
                 nc.vector.tensor_copy(dst, src)
             w1_q.append(quantize(grouped, H, "w1_%d" % o))
 
-        turned_rows = bank("work_c")
-        nc.tensor.transpose(turned_rows[:, :P], frac_rows[:], identity[:])
-        frac_cols = held([P, 2 * CHUNKS], F32, "frac_cols")
-        nc.scalar.copy(frac_cols[:], turned_rows[:, : 2 * CHUNKS])
+        kn1_raw = load_rows(kn1, G, "w1_raw0")
+        kn2_raw = load_rows(kn2, W, "kn2_raw")
+        true_rows = held([P, BLOCKS, R], F32, "w1_grouped1")
+        true_t = {}
+        for b in (0, 1, 3, 2):
+            true_t[b] = true_rows[:, b, :]
+            nc.sync.dma_start(true_t[b], true[b * P : (b + 1) * P, :])
 
-        def spread(first, name, spread_rows):
-            for c in range(CHUNKS):
-                column = frac_cols[:, first + c : first + c + 1]
-                nc.tensor.transpose(spread_rows[:, c * P : (c + 1) * P], column.to_broadcast([P, P]), identity[:])
+        def spread(rate, name, spread_rows, turned_rows):
+            for j in range(PACK):
+                column = frac_cols[rate][:, j : j + 1]
+                nc.tensor.transpose(spread_rows[:, j * P : (j + 1) * P], column.to_broadcast([P, P]), identity[:])
             part = row(name + "_part")
             rest = row(name + "_rest")
-            nc.scalar.activation(part, spread_rows[:], ACT.Copy, scale=-1.0)
-            nc.scalar.activation(rest, spread_rows[:], ACT.Copy, bias=-1.0)
-            return part, rest
+            in_order = spread_rows[:].rearrange("p (j n) -> p n j", j=PACK)
+            nc.scalar.activation(part.rearrange("p (n j) -> p n j", j=PACK), in_order, ACT.Copy, scale=-1.0)
+            nc.scalar.activation(rest.rearrange("p (n j) -> p n j", j=PACK), in_order, ACT.Copy, bias=-1.0)
+            for c in range(CHUNKS):
+                cols = slice(c * P, (c + 1) * P)
+                nc.tensor.transpose(turned_rows[:, cols], part[:, cols], identity[:])
+            turned = row(name + "_turned")
+            nc.scalar.copy(turned, turned_rows[:])
+            return part, rest, turned
 
-        part1, rest1 = spread(0, "frac1", bank("work_a"))
-        part2, rest2 = spread(CHUNKS, "frac2", bank("work_b"))
-
-        turned_part = []
-        for rate in range(2):
-            wide = held([P, CHUNKS, P], F32, "turned_part%d" % rate)
-            columns = frac_cols[:, rate * CHUNKS : (rate + 1) * CHUNKS]
-            nc.scalar.activation(wide[:], columns.unsqueeze(2).to_broadcast([P, CHUNKS, P]), ACT.Copy, scale=-1.0)
-            turned_part.append(wide[:].rearrange("p c t -> p (c t)"))
+        part1, rest1, turned_part1 = spread(0, "frac1", bank("work_a"), bank("work_c"))
+        part2, rest2, turned_part2 = spread(1, "frac2", bank("work_b"), bank("diff3"))
+        turned_part = [turned_part1, turned_part2]
 
         x_codes = [[None, None] for o in range(PASSES)]
         for o in range(PASSES):
@@ -163,7 +164,7 @@ def tile_picked_ynhits_err_p_kernel(
                         lhsT=w1_q[o][0][:, t * P : (t + 1) * P].bitcast(FP8X4),
                         lhsT_scale=w1_q[o][1][:, t * P : (t + 1) * P],
                         rhs=x_codes[o][half][:, first : first + P].bitcast(FP8X4),
-                        rhs_scale=x_scale[4 * o :, b * P : (b + 1) * P],
+                        rhs_scale=x_scale[:, o, b * P : (b + 1) * P],
                         start=(o == 0 and t == 0),
                         stop=(o == PASSES - 1 and t == PACK - 1),
                     )

@@ -22,7 +22,7 @@ K_PASS = P * PACK
 PASSES = K // K_PASS
 BLOCKS = S // P
 CHUNKS = R // P
-HALF = S // 2
+SHARE = 88
 WINDOW = R + 16
 HALVES = (slice(0, R // 2), slice(R // 2, R))
 
@@ -67,32 +67,32 @@ def tile_picked_ynhits_err_p_kernel(
 
         identity = held([P, P], F32, "identity")
         make_identity(nc, identity[:])
-        x_scale_rows = held([P, PASSES, T], U8, "x_table1")
-        nc.vector.memset(x_scale_rows[:].rearrange("p o n -> p (o n)").bitcast(I32), 0)
+        x_scale_rows = held([P, T], U8, "x_table1")
+        for first, last in ((32, 64), (64, P)):
+            nc.vector.memset(x_scale_rows[first:last, :].bitcast(I32), 0)
         x_scale = held([P, PASSES, S], U8, "x_scale")
         nc.vector.memset(x_scale[:].rearrange("p o n -> p (o n)").bitcast(I32), 0)
 
-        w1_raw = [load_rows(w1[:K_PASS, :], H, "w1_raw0")]
         offs_t = load_list(offs, "offs_t")
-        nc.sync.dma_start(x_scale_rows[::8].bitcast(I32), x_scales.rearrange("o q n -> q o n").bitcast(I32))
+        nc.sync.dma_start(x_scale_rows[:32, :].bitcast(I32), x_scales.rearrange("o q n -> q o n").bitcast(I32))
+        w1_raw = [load_rows(w1[:K_PASS, :], H, "w1_raw0")]
         frac_cols = []
         for i, frac in enumerate((frac1, frac2)):
             frac_cols.append(held([P, PACK], F32, "frac_cols%d" % i))
             nc.sync.dma_start(frac_cols[i][:], frac[0].rearrange("(p j) -> p j", j=PACK))
         right1_t = load_list(right1, "right1_t")
         left1_t = load_list(left1, "left1_t")
-        w1_raw.append(load_rows(w1[K_PASS:, :], H, "kn2_raw"))
         x_table = [load_words(0)]
+        w1_raw.append(load_rows(w1[K_PASS:, :], H, "kn2_raw"))
         left2_t = load_list(left2, "left2_t")
         right2_t = load_list(right2, "right2_t")
 
-        picked_scales = held([P, PASSES, S], U8, "picked_scales")
-        for o in range(PASSES):
-            nc.vector.tensor_copy(picked_scales[:, o, :], x_scale_rows[:, o, :].indirect(offs_t[:]))
+        picked_scales = held([P, S], U8, "picked_scales")
+        nc.vector.tensor_copy(picked_scales[:], x_scale_rows[:].indirect(offs_t[:]))
         for q in range(4):
             nc.sync.dma_start(
-                x_scale[32 * q : 32 * q + 4].rearrange("p o n -> p (o n)").bitcast(I32),
-                picked_scales[32 * q : 32 * q + 32 : 8].rearrange("p o n -> p (o n)").bitcast(I32),
+                x_scale[32 * q : 32 * q + 4].bitcast(I32),
+                picked_scales[8 * q : 8 * q + 8, :].bitcast(I32),
             )
         x_table.append(load_words(1))
 
@@ -108,9 +108,10 @@ def tile_picked_ynhits_err_p_kernel(
             dst = grouped[:].rearrange("p (t m j) -> p m t j", t=PACK, j=PACK)
             src = w1_raw[o][:].rearrange("p j (m t) -> p m t j", t=PACK)
             if o == 0:
-                nc.scalar.activation(dst, src, ACT.Copy)
-            else:
                 nc.vector.tensor_copy(dst, src)
+            else:
+                nc.vector.tensor_copy(dst[:, :SHARE], src[:, :SHARE])
+                nc.scalar.activation(dst[:, SHARE:], src[:, SHARE:], ACT.Copy)
             w1_q.append(quantize(grouped, H, "w1_%d" % o))
 
         kn1_raw = load_rows(kn1, G, "w1_raw0")
@@ -141,13 +142,14 @@ def tile_picked_ynhits_err_p_kernel(
         part2, rest2, turned_part2 = spread(1, "frac2", bank("work_b"), bank("diff3"))
         turned_part = [turned_part1, turned_part2]
 
-        x_codes = [[None, None] for o in range(PASSES)]
-        for o in range(PASSES):
-            for half in range(2):
-                picked = held([P, HALF], U32, "x_codes%d_%d" % (o, half))
-                cols = slice(half * HALF // 16, (half + 1) * HALF // 16)
+        x_codes = [[] for o in range(PASSES)]
+        for o, pieces in enumerate(((2, 2), (1, 1, 2))):
+            for blocks in pieces:
+                first = len(x_codes[o])
+                picked = held([P, blocks * P], U32, "x_codes%d_%d" % (o, first))
+                cols = slice(first * P // 16, (first + blocks) * P // 16)
                 nc.vector.tensor_copy(picked[:], x_table[o][:].indirect(offs_t[:, cols]))
-                x_codes[o][half] = picked
+                x_codes[o].extend(picked[:, i * P : (i + 1) * P] for i in range(blocks))
 
         def interleave(raw, grouped, engine_copy):
             engine_copy(
@@ -155,19 +157,20 @@ def tile_picked_ynhits_err_p_kernel(
                 raw[:].rearrange("p j (c i) -> p c j i", i=PACK),
             )
 
+        def hidden_pass(b, o, acc):
+            for t in range(PACK):
+                nc.tensor.matmul_mx(
+                    out=acc[:, t * P : (t + 1) * P],
+                    lhsT=w1_q[o][0][:, t * P : (t + 1) * P].bitcast(FP8X4),
+                    lhsT_scale=w1_q[o][1][:, t * P : (t + 1) * P],
+                    rhs=x_codes[o][b].bitcast(FP8X4),
+                    rhs_scale=x_scale[:, o, b * P : (b + 1) * P],
+                    start=(o == 0 and t == 0),
+                    stop=(o == PASSES - 1 and t == PACK - 1),
+                )
+
         def hidden_block(b, acc):
-            half, first = divmod(b * P, HALF)
-            for o in range(PASSES):
-                for t in range(PACK):
-                    nc.tensor.matmul_mx(
-                        out=acc[:, t * P : (t + 1) * P],
-                        lhsT=w1_q[o][0][:, t * P : (t + 1) * P].bitcast(FP8X4),
-                        lhsT_scale=w1_q[o][1][:, t * P : (t + 1) * P],
-                        rhs=x_codes[o][half][:, first : first + P].bitcast(FP8X4),
-                        rhs_scale=x_scale[:, o, b * P : (b + 1) * P],
-                        start=(o == 0 and t == 0),
-                        stop=(o == PASSES - 1 and t == PACK - 1),
-                    )
+            hidden_pass(b, PASSES - 1, acc)
             hidden = held([P, PACK * P], BF16, "hidden%d" % b)
             nc.scalar.activation(
                 hidden[:].rearrange("p (n t) -> p n t", t=PACK), acc[:].rearrange("p (t n) -> p n t", t=PACK), ACT.Relu
@@ -244,7 +247,10 @@ def tile_picked_ynhits_err_p_kernel(
 
         kn1_grouped = held([P, PACK * G], BF16, "kn1_grouped")
         interleave(kn1_raw, kn1_grouped[:], nc.vector.tensor_copy)
-        hidden = [hidden_block(b, bank("sum%d" % b)) for b in range(BLOCKS)]
+        before_relu = [bank("sum%d" % b) for b in range(BLOCKS)]
+        for b in range(BLOCKS):
+            hidden_pass(b, 0, before_relu[b])
+        hidden = [hidden_block(b, before_relu[b]) for b in range(BLOCKS)]
         h_q = [quantize(hidden[0], P, "h0")]
         kn1_q = quantize(kn1_grouped, G, "kn1")
         h_q.append(quantize(hidden[1], P, "h1"))

@@ -23,6 +23,7 @@ PASSES = K // K_PASS
 BLOCKS = S // P
 CHUNKS = R // P
 SHARE = 88
+KN2_SHARE = 256
 WINDOW = R + 16
 HALVES = (slice(0, R // 2), slice(R // 2, R))
 
@@ -73,9 +74,9 @@ def tile_picked_ynhits_err_p_kernel(
         x_scale = held([P, PASSES, S], U8, "x_scale")
         nc.vector.memset(x_scale[:].rearrange("p o n -> p (o n)").bitcast(I32), 0)
 
+        w1_raw = [load_rows(w1[:K_PASS, :], H, "w1_raw0")]
         offs_t = load_list(offs, "offs_t")
         nc.sync.dma_start(x_scale_rows[:32, :].bitcast(I32), x_scales.rearrange("o q n -> q o n").bitcast(I32))
-        w1_raw = [load_rows(w1[:K_PASS, :], H, "w1_raw0")]
         frac_cols = []
         for i, frac in enumerate((frac1, frac2)):
             frac_cols.append(held([P, PACK], F32, "frac_cols%d" % i))
@@ -115,7 +116,8 @@ def tile_picked_ynhits_err_p_kernel(
             w1_q.append(quantize(grouped, H, "w1_%d" % o))
 
         kn1_raw = load_rows(kn1, G, "w1_raw0")
-        kn2_raw = load_rows(kn2, W, "kn2_raw")
+        kn2_first = load_rows(kn2[:, :KN2_SHARE], KN2_SHARE, "x_table0")
+        kn2_raw = load_rows(kn2[:, KN2_SHARE:], W - KN2_SHARE, "kn2_raw")
         true_rows = held([P, BLOCKS, R], F32, "w1_grouped1")
         true_t = {}
         for b in (0, 1, 3, 2):
@@ -154,7 +156,7 @@ def tile_picked_ynhits_err_p_kernel(
         def interleave(raw, grouped, engine_copy):
             engine_copy(
                 grouped.rearrange("p (c i j) -> p c j i", i=PACK, j=PACK),
-                raw[:].rearrange("p j (c i) -> p c j i", i=PACK),
+                raw.rearrange("p j (c i) -> p c j i", i=PACK),
             )
 
         def hidden_pass(b, o, acc):
@@ -234,6 +236,14 @@ def tile_picked_ynhits_err_p_kernel(
             nc.vector.tensor_tensor(step, diff[:], turned_part[rate], ALU.mult)
             return step
 
+        def scaled_out(diff, rate, name):
+            step = row(name)
+            for c in range(CHUNKS):
+                cols = slice(c * P, (c + 1) * P)
+                weight = turned_part[rate][:, c * P : c * P + 1]
+                nc.scalar.activation(step[:, cols], diff[:, cols], ACT.Copy, scale=weight)
+            return step
+
         def turn_in(turned, back):
             for c in range(CHUNKS):
                 cols = slice(c * P, (c + 1) * P)
@@ -246,7 +256,7 @@ def tile_picked_ynhits_err_p_kernel(
             nc.sync.dma_start(out[b * P : (b + 1) * P, :], result)
 
         kn1_grouped = held([P, PACK * G], BF16, "kn1_grouped")
-        interleave(kn1_raw, kn1_grouped[:], nc.vector.tensor_copy)
+        interleave(kn1_raw[:], kn1_grouped[:], nc.vector.tensor_copy)
         before_relu = [bank("sum%d" % b) for b in range(BLOCKS)]
         for b in range(BLOCKS):
             hidden_pass(b, 0, before_relu[b])
@@ -260,72 +270,76 @@ def tile_picked_ynhits_err_p_kernel(
         knots(1, kn1_q, knots1[1], bank("work_b")[:, :G])
         h_q.append(quantize(hidden[2], P, "h2"))
         knots(2, kn1_q, knots1[2], bank("work_c")[:, :G])
-        right1_0 = weighted(knots1[0], right1_t[:], part1, row("right1_0"))
-        h_q.append(quantize(hidden[3], P, "h3"))
         kn2_grouped = held([P, PACK * W], BF16, "kn2_grouped")
-        interleave(kn2_raw, kn2_grouped[:], lambda dst, src: nc.scalar.activation(dst, src, ACT.Copy))
+        interleave(kn2_first[:], kn2_grouped[:, : PACK * KN2_SHARE], nc.vector.tensor_copy)
+        h_q.append(quantize(hidden[3], P, "h3"))
+        right1_0 = weighted(knots1[0], right1_t[:], part1, row("x_table0"))
         knots(3, kn1_q, knots1[3], bank("diff3")[:, :G])
+        interleave(
+            kn2_raw[:],
+            kn2_grouped[:, PACK * KN2_SHARE :],
+            lambda dst, src: nc.scalar.activation(dst, src, ACT.Copy),
+        )
 
         sums = [bank("sum%d" % b) for b in range(BLOCKS)]
         add_turned(sums[0], true_t[0], start=True)
         add_turned(sums[1], true_t[1], start=True)
         add_turned(sums[0], right1_0)
-        add_turned(sums[3], true_t[3], start=True)
         add_turned(sums[0], weighted(knots1[0], left1_t[:], rest1, row("left1_0")))
-        add_turned(sums[2], true_t[2], start=True)
-        add_turned(sums[1], weighted(knots1[1], right1_t[:], part1, row("right1_1")))
         kn2_q = quantize(kn2_grouped, W, "kn2")
-        after_kn2 = held([P, 5, R], F32, "kn2_raw")
+        after_kn2 = held([P, 6, R], F32, "kn2_raw")
+        right1_1 = weighted(knots1[1], right1_t[:], part1, after_kn2[:, 5, :])
         left1_3 = fetched(knots1[3], left1_t[:], after_kn2[:, 3, :], -1.0)
         right1_3 = fetched(knots1[3], right1_t[:], after_kn2[:, 4, :], 1.0)
         knots(3, kn2_q, knots2[3], bank("work_a")[:])
         knots(0, kn2_q, knots2[0], bank("work_b")[:])
         left2_3 = fetched(knots2[3], left2_t[:], row("left2_3"), -1.0)
         knots(1, kn2_q, knots2[1], bank("work_c")[:])
+        add_turned(sums[3], true_t[3], start=True)
+        add_turned(sums[1], right1_1)
         diff3 = bank("diff3")
         add_turned(sums[3], left1_3)
         add_turned(diff3, left1_3, start=True)
         add_turned(sums[1], weighted(knots1[1], left1_t[:], rest1, after_kn2[:, 0, :]))
+        add_turned(diff3, right1_3, stop=True)
+        step3 = scaled_out(diff3, 0, "step3")
         shared = bank("work_b")[:]
         warm_up(shared)
         knots(2, kn2_q, knots2[2], shared)
         left2_1 = fetched(knots2[1], left2_t[:], row("h2_codes"), -1.0)
-        add_turned(diff3, right1_3, stop=True)
+        add_turned(sums[2], true_t[2], start=True)
         add_turned(sums[2], weighted(knots1[2], right1_t[:], part1, after_kn2[:, 1, :]))
         add_turned(sums[3], left2_3, stop=True)
         add_turned(sums[2], weighted(knots1[2], left1_t[:], rest1, after_kn2[:, 2, :]))
         right2_1 = fetched(knots2[1], right2_t[:], row("kn2_raw"), 1.0)
+        turned3 = turn_out(sums[3], ACT.Copy, "turned3")
         add_turned(sums[0], weighted(knots2[0], left2_t[:], rest2, row("left2_0")))
+        partial = bank("diff3")
+        add_turned(partial, step3, start=True)
         right2_0 = weighted(knots2[0], right2_t[:], part2, row("right2_0"))
         spare = bank("work_b")
         for width in (W, G):
             warm_up(spare[:, :width])
-        add_turned(sums[0], right2_0, stop=True)
-        left2_2 = weighted(knots2[2], left2_t[:], rest2, row("left2_2"))
-        right2_2 = weighted(knots2[2], right2_t[:], part2, row("right2_2"))
         add_turned(sums[1], left2_1, stop=True)
-        turned0 = turn_out(sums[0], ACT.Abs, "turned0")
         turned1 = turn_out(sums[1], ACT.Copy, "turned1")
         diff1 = bank("work_a")
         add_turned(diff1, left2_1, start=True)
-        turned3 = turn_out(sums[3], ACT.Copy, "h2_codes")
+        add_turned(sums[0], right2_0, stop=True)
+        turned0 = turn_out(sums[0], ACT.Abs, "turned0")
+        left2_2 = weighted(knots2[2], left2_t[:], rest2, row("left2_2"))
+        right2_2 = weighted(knots2[2], right2_t[:], part2, row("right2_2"))
+        add_turned(partial, turned3, stop=True)
         add_turned(diff1, right2_1, stop=True)
         step1 = scaled(diff1, 1, "step1")
-        step3 = scaled(diff3, 0, "kn2_raw")
         add_turned(sums[2], left2_2)
-        spare = bank("sum0")
-        for width in (W,):
-            warm_up(spare[:, :width])
+        warm_up(bank("work_c")[:])
         store(0, turn_in(turned0, bank("work_b")), ACT.Copy)
-        back1 = bank("sum1")
-        add_turned(back1, turned1, start=True)
         add_turned(sums[2], right2_2, stop=True)
         turned2 = turn_out(sums[2], ACT.Abs, "turned2")
+        back1 = bank("sum1")
+        add_turned(back1, turned1, start=True)
         add_turned(back1, step1, stop=True)
         store(1, back1, ACT.Abs)
-        partial = bank("work_c")
-        add_turned(partial, turned3, start=True)
-        add_turned(partial, step3, stop=True)
         store(2, turn_in(turned2, bank("sum2")), ACT.Copy)
 
         gaps = row("left2_2")

@@ -74,19 +74,19 @@ def tile_picked_ynhits_err_p_kernel(
         x_scale = held([P, PASSES, S], U8, "x_scale")
         nc.vector.memset(x_scale[:].rearrange("p o n -> p (o n)").bitcast(I32), 0)
 
-        w1_raw = [load_rows(w1[:K_PASS, :], H, "w1_raw0")]
         offs_t = load_list(offs, "offs_t")
         nc.sync.dma_start(x_scale_rows[:32, :].bitcast(I32), x_scales.rearrange("o q n -> q o n").bitcast(I32))
+        w1_raw = [load_rows(w1[:K_PASS, :], H, "w1_raw0")]
         frac_cols = []
         for i, frac in enumerate((frac1, frac2)):
             frac_cols.append(held([P, PACK], F32, "frac_cols%d" % i))
             nc.sync.dma_start(frac_cols[i][:], frac[0].rearrange("(p j) -> p j", j=PACK))
         right1_t = load_list(right1, "right1_t")
         left1_t = load_list(left1, "left1_t")
-        x_table = [load_words(0)]
-        w1_raw.append(load_rows(w1[K_PASS:, :], H, "kn2_raw"))
         left2_t = load_list(left2, "left2_t")
         right2_t = load_list(right2, "right2_t")
+        x_table = [load_words(0)]
+        w1_raw.append(load_rows(w1[K_PASS:, :], H, "kn2_raw"))
 
         picked_scales = held([P, S], U8, "picked_scales")
         nc.vector.tensor_copy(picked_scales[:], x_scale_rows[:].indirect(offs_t[:]))
@@ -264,91 +264,86 @@ def tile_picked_ynhits_err_p_kernel(
         h_q = [quantize(hidden[0], P, "h0")]
         kn1_q = quantize(kn1_grouped, G, "kn1")
         h_q.append(quantize(hidden[1], P, "h1"))
-        first = bank("work_a")[:, :G]
-        product(h_q[0], kn1_q, first)
-        nc.vector.tensor_copy(knots1[0][:, :G], first)
+        knots(0, kn1_q, knots1[0], bank("work_a")[:, :G])
         knots(1, kn1_q, knots1[1], bank("work_b")[:, :G])
+        kn2_grouped = [held([P, PACK * KN2_SHARE], BF16, "kn2_grouped")]
+        interleave(kn2_first[:], kn2_grouped[0][:], nc.vector.tensor_copy)
         h_q.append(quantize(hidden[2], P, "h2"))
-        knots(2, kn1_q, knots1[2], bank("work_c")[:, :G])
-        kn2_grouped = held([P, PACK * W], BF16, "kn2_grouped")
-        interleave(kn2_first[:], kn2_grouped[:, : PACK * KN2_SHARE], nc.vector.tensor_copy)
         h_q.append(quantize(hidden[3], P, "h3"))
         right1_0 = weighted(knots1[0], right1_t[:], part1, row("x_table0"))
+        kn2_grouped.append(held([P, PACK * KN2_SHARE], BF16, "kn2_grouped1"))
+        interleave(kn2_raw[:], kn2_grouped[1][:], lambda dst, src: nc.scalar.activation(dst, src, ACT.Copy))
         knots(3, kn1_q, knots1[3], bank("diff3")[:, :G])
-        interleave(
-            kn2_raw[:],
-            kn2_grouped[:, PACK * KN2_SHARE :],
-            lambda dst, src: nc.scalar.activation(dst, src, ACT.Copy),
-        )
-
+        knots(2, kn1_q, knots1[2], bank("work_c")[:, :G])
         sums = [bank("sum%d" % b) for b in range(BLOCKS)]
         add_turned(sums[0], true_t[0], start=True)
-        add_turned(sums[1], true_t[1], start=True)
+
         add_turned(sums[0], right1_0)
-        add_turned(sums[0], weighted(knots1[0], left1_t[:], rest1, row("left1_0")))
-        kn2_q = quantize(kn2_grouped, W, "kn2")
+        add_turned(sums[1], true_t[1], start=True)
+        left1_0 = weighted(knots1[0], left1_t[:], rest1, row("left1_0"))
+        kn2_q = held([P, W], U32, "kn2_codes"), held([P, W], U8, "kn2_scales")
+        for grouped, cols in zip(kn2_grouped, HALVES):
+            nc.vector.quantize_mx(out=kn2_q[0][:, cols].bitcast(FP8X4), scales=kn2_q[1][:, cols], in_=grouped[:])
         after_kn2 = held([P, 6, R], F32, "kn2_raw")
         right1_1 = weighted(knots1[1], right1_t[:], part1, after_kn2[:, 5, :])
         left1_3 = fetched(knots1[3], left1_t[:], after_kn2[:, 3, :], -1.0)
         right1_3 = fetched(knots1[3], right1_t[:], after_kn2[:, 4, :], 1.0)
-        knots(3, kn2_q, knots2[3], bank("work_a")[:])
+        knots(1, kn2_q, knots2[1], bank("work_a")[:])
         knots(0, kn2_q, knots2[0], bank("work_b")[:])
-        left2_3 = fetched(knots2[3], left2_t[:], row("left2_3"), -1.0)
-        knots(1, kn2_q, knots2[1], bank("work_c")[:])
-        add_turned(sums[3], true_t[3], start=True)
-        add_turned(sums[1], right1_1)
+        left2_1 = fetched(knots2[1], left2_t[:], row("left2_1"), -1.0)
         diff3 = bank("diff3")
-        add_turned(sums[3], left1_3)
         add_turned(diff3, left1_3, start=True)
-        add_turned(sums[1], weighted(knots1[1], left1_t[:], rest1, after_kn2[:, 0, :]))
         add_turned(diff3, right1_3, stop=True)
         step3 = scaled_out(diff3, 0, "step3")
-        shared = bank("work_b")[:]
-        warm_up(shared)
-        knots(2, kn2_q, knots2[2], shared)
-        left2_1 = fetched(knots2[1], left2_t[:], row("h2_codes"), -1.0)
+        add_turned(sums[0], left1_0)
+        right2_1 = fetched(knots2[1], right2_t[:], row("left1_0"), 1.0)
+        add_turned(sums[3], true_t[3], start=True)
+        add_turned(sums[3], left1_3)
+        add_turned(sums[1], right1_1)
+        add_turned(sums[1], weighted(knots1[1], left1_t[:], rest1, after_kn2[:, 0, :]))
         add_turned(sums[2], true_t[2], start=True)
         add_turned(sums[2], weighted(knots1[2], right1_t[:], part1, after_kn2[:, 1, :]))
-        add_turned(sums[3], left2_3, stop=True)
-        add_turned(sums[2], weighted(knots1[2], left1_t[:], rest1, after_kn2[:, 2, :]))
-        right2_1 = fetched(knots2[1], right2_t[:], row("kn2_raw"), 1.0)
-        turned3 = turn_out(sums[3], ACT.Copy, "turned3")
-        add_turned(sums[0], weighted(knots2[0], left2_t[:], rest2, row("left2_0")))
-        partial = bank("diff3")
-        add_turned(partial, step3, start=True)
-        right2_0 = weighted(knots2[0], right2_t[:], part2, row("right2_0"))
-        spare = bank("work_b")
-        for width in (W, G):
-            warm_up(spare[:, :width])
-        add_turned(sums[1], left2_1, stop=True)
-        turned1 = turn_out(sums[1], ACT.Copy, "turned1")
         diff1 = bank("work_a")
         add_turned(diff1, left2_1, start=True)
+        left1_2 = weighted(knots1[2], left1_t[:], rest1, after_kn2[:, 2, :])
+        knots(3, kn2_q, knots2[3], bank("work_c")[:])
+        knots(2, kn2_q, knots2[2], bank("work_b")[:])
+        add_turned(sums[2], left1_2)
+        add_turned(diff1, right2_1, stop=True)
+        left2_3 = fetched(knots2[3], left2_t[:], row("left2_3"), -1.0)
+        add_turned(sums[0], weighted(knots2[0], left2_t[:], rest2, row("left2_0")))
+        right2_0 = weighted(knots2[0], right2_t[:], part2, row("right2_0"))
+        spare = bank("work_b")
+        warm_up(spare[:, :512])
         add_turned(sums[0], right2_0, stop=True)
         turned0 = turn_out(sums[0], ACT.Abs, "turned0")
+        add_turned(sums[1], left2_1, stop=True)
+        turned1 = turn_out(sums[1], ACT.Copy, "turned1")
+        step1 = scaled_out(diff1, 1, "left2_1")
         left2_2 = weighted(knots2[2], left2_t[:], rest2, row("left2_2"))
         right2_2 = weighted(knots2[2], right2_t[:], part2, row("right2_2"))
-        add_turned(partial, turned3, stop=True)
-        add_turned(diff1, right2_1, stop=True)
-        step1 = scaled(diff1, 1, "step1")
+        add_turned(sums[3], left2_3, stop=True)
         add_turned(sums[2], left2_2)
-        warm_up(bank("work_c")[:])
-        store(0, turn_in(turned0, bank("work_b")), ACT.Copy)
+        back0 = turn_in(turned0, bank("work_b"))
+        turned3 = row("turned3")
+        nc.vector.tensor_tensor(turned3, sums[3][:], step3, ALU.add)
+        store(0, back0, ACT.Copy)
         add_turned(sums[2], right2_2, stop=True)
         turned2 = turn_out(sums[2], ACT.Abs, "turned2")
-        back1 = bank("sum1")
+        back1 = bank("diff3")
         add_turned(back1, turned1, start=True)
         add_turned(back1, step1, stop=True)
         store(1, back1, ACT.Abs)
+        partial = turn_in(turned3, bank("work_c"))
         store(2, turn_in(turned2, bank("sum2")), ACT.Copy)
 
-        gaps = row("left2_2")
-        steps = row("steps")
-        for cols in HALVES:
+        gaps = [held([P, R // 2], F32, name) for name in ("gaps", "left2_2")]
+        steps = row("right2_2")
+        for gap, cols in zip(gaps, HALVES):
             window = knots2[3][:].indirect(part_of(right2_t, cols))
-            nc.vector.tensor_tensor(gaps[:, cols], window, left2_3[:, cols], ALU.add)
-        for cols in HALVES:
-            nc.vector.tensor_tensor(steps[:, cols], gaps[:, cols], part2[:, cols], ALU.mult)
+            nc.vector.tensor_tensor(gap[:], window, left2_3[:, cols], ALU.add)
+        for gap, cols in zip(gaps, HALVES):
+            nc.vector.tensor_tensor(steps[:, cols], gap[:], part2[:, cols], ALU.mult)
         result = row("turned2")
         for i, cols in enumerate(HALVES):
             total = held([P, R // 2], F32, "total%d" % i)

@@ -120,7 +120,7 @@ def tile_picked_ynhits_err_p_kernel(
         kn2_raw = load_rows(kn2[:, KN2_SHARE:], W - KN2_SHARE, "kn2_raw")
         true_rows = held([P, BLOCKS, R], F32, "w1_grouped1")
         true_t = {}
-        for b in (0, 1, 3, 2):
+        for b in range(BLOCKS):
             true_t[b] = true_rows[:, b, :]
             nc.sync.dma_start(true_t[b], true[b * P : (b + 1) * P, :])
 
@@ -267,14 +267,14 @@ def tile_picked_ynhits_err_p_kernel(
         knots(0, kn1_q, knots1[0], bank("work_a")[:, :G])
         knots(1, kn1_q, knots1[1], bank("work_b")[:, :G])
         kn2_grouped = [held([P, PACK * KN2_SHARE], BF16, "kn2_grouped")]
-        interleave(kn2_first[:], kn2_grouped[0][:], nc.vector.tensor_copy)
         h_q.append(quantize(hidden[2], P, "h2"))
+        knots(2, kn1_q, knots1[2], bank("work_c")[:, :G])
+        interleave(kn2_first[:], kn2_grouped[0][:], nc.vector.tensor_copy)
         h_q.append(quantize(hidden[3], P, "h3"))
         right1_0 = weighted(knots1[0], right1_t[:], part1, row("x_table0"))
         kn2_grouped.append(held([P, PACK * KN2_SHARE], BF16, "kn2_grouped1"))
         interleave(kn2_raw[:], kn2_grouped[1][:], lambda dst, src: nc.scalar.activation(dst, src, ACT.Copy))
         knots(3, kn1_q, knots1[3], bank("diff3")[:, :G])
-        knots(2, kn1_q, knots1[2], bank("work_c")[:, :G])
         sums = [bank("sum%d" % b) for b in range(BLOCKS)]
         add_turned(sums[0], true_t[0], start=True)
 
@@ -286,67 +286,69 @@ def tile_picked_ynhits_err_p_kernel(
             nc.vector.quantize_mx(out=kn2_q[0][:, cols].bitcast(FP8X4), scales=kn2_q[1][:, cols], in_=grouped[:])
         after_kn2 = held([P, 6, R], F32, "kn2_raw")
         right1_1 = weighted(knots1[1], right1_t[:], part1, after_kn2[:, 5, :])
-        left1_3 = fetched(knots1[3], left1_t[:], after_kn2[:, 3, :], -1.0)
-        right1_3 = fetched(knots1[3], right1_t[:], after_kn2[:, 4, :], 1.0)
+        left1_2 = fetched(knots1[2], left1_t[:], after_kn2[:, 3, :], -1.0)
+        right1_2 = fetched(knots1[2], right1_t[:], after_kn2[:, 4, :], 1.0)
         knots(1, kn2_q, knots2[1], bank("work_a")[:])
         knots(0, kn2_q, knots2[0], bank("work_b")[:])
+        product(h_q[0], kn2_q, bank("diff3")[:])
         left2_1 = fetched(knots2[1], left2_t[:], row("left2_1"), -1.0)
-        diff3 = bank("diff3")
-        add_turned(diff3, left1_3, start=True)
-        add_turned(diff3, right1_3, stop=True)
-        step3 = scaled_out(diff3, 0, "step3")
+        diff2 = bank("work_c")
+        add_turned(diff2, left1_2, start=True)
+        add_turned(diff2, right1_2, stop=True)
+        step2 = scaled_out(diff2, 0, "step2")
         add_turned(sums[0], left1_0)
         right2_1 = fetched(knots2[1], right2_t[:], row("left1_0"), 1.0)
-        add_turned(sums[3], true_t[3], start=True)
-        add_turned(sums[3], left1_3)
+        add_turned(sums[2], true_t[2], start=True)
+        add_turned(sums[2], left1_2)
         add_turned(sums[1], right1_1)
         add_turned(sums[1], weighted(knots1[1], left1_t[:], rest1, after_kn2[:, 0, :]))
-        add_turned(sums[2], true_t[2], start=True)
-        add_turned(sums[2], weighted(knots1[2], right1_t[:], part1, after_kn2[:, 1, :]))
+        right1_3 = weighted(knots1[3], right1_t[:], part1, after_kn2[:, 1, :])
+        left1_3 = weighted(knots1[3], left1_t[:], rest1, after_kn2[:, 2, :])
+        knots(2, kn2_q, knots2[2], bank("diff3")[:])
+        knots(3, kn2_q, knots2[3], bank("work_b")[:])
+        left2_2 = fetched(knots2[2], left2_t[:], row("left2_2"), -1.0)
+        add_turned(sums[3], true_t[3], start=True)
+        add_turned(sums[3], right1_3)
         diff1 = bank("work_a")
         add_turned(diff1, left2_1, start=True)
-        left1_2 = weighted(knots1[2], left1_t[:], rest1, after_kn2[:, 2, :])
-        knots(3, kn2_q, knots2[3], bank("work_c")[:])
-        knots(2, kn2_q, knots2[2], bank("work_b")[:])
-        add_turned(sums[2], left1_2)
+        add_turned(sums[1], left2_1, stop=True)
         add_turned(diff1, right2_1, stop=True)
-        left2_3 = fetched(knots2[3], left2_t[:], row("left2_3"), -1.0)
+        turned1 = turn_out(sums[1], ACT.Copy, "turned1")
+        spare = bank("diff3")
+        warm_up(spare[:, :512])
+        add_turned(sums[3], left1_3)
         add_turned(sums[0], weighted(knots2[0], left2_t[:], rest2, row("left2_0")))
         right2_0 = weighted(knots2[0], right2_t[:], part2, row("right2_0"))
-        spare = bank("work_b")
-        warm_up(spare[:, :512])
+        partial = bank("work_c")
+        add_turned(partial, step2, start=True)
         add_turned(sums[0], right2_0, stop=True)
         turned0 = turn_out(sums[0], ACT.Abs, "turned0")
-        add_turned(sums[1], left2_1, stop=True)
-        turned1 = turn_out(sums[1], ACT.Copy, "turned1")
-        step1 = scaled_out(diff1, 1, "left2_1")
-        left2_2 = weighted(knots2[2], left2_t[:], rest2, row("left2_2"))
-        right2_2 = weighted(knots2[2], right2_t[:], part2, row("right2_2"))
-        add_turned(sums[3], left2_3, stop=True)
-        add_turned(sums[2], left2_2)
-        back0 = turn_in(turned0, bank("work_b"))
-        turned3 = row("turned3")
-        nc.vector.tensor_tensor(turned3, sums[3][:], step3, ALU.add)
-        store(0, back0, ACT.Copy)
-        add_turned(sums[2], right2_2, stop=True)
-        turned2 = turn_out(sums[2], ACT.Abs, "turned2")
-        back1 = bank("diff3")
+        left2_3 = weighted(knots2[3], left2_t[:], rest2, row("left2_3"))
+        right2_3 = weighted(knots2[3], right2_t[:], part2, row("right2_3"))
+        add_turned(sums[2], left2_2, stop=True)
+        turned2 = turn_out(sums[2], ACT.Copy, "turned2")
+        add_turned(sums[3], left2_3)
+        step1 = scaled(diff1, 1, "left2_3")
+        back1 = bank("work_b")
         add_turned(back1, turned1, start=True)
+        store(0, turn_in(turned0, bank("sum0")), ACT.Copy)
+        add_turned(sums[3], right2_3, stop=True)
+        turned3 = turn_out(sums[3], ACT.Abs, "turned3")
+        add_turned(partial, turned2, stop=True)
         add_turned(back1, step1, stop=True)
         store(1, back1, ACT.Abs)
-        partial = turn_in(turned3, bank("work_c"))
-        store(2, turn_in(turned2, bank("sum2")), ACT.Copy)
+        store(3, turn_in(turned3, bank("sum3")), ACT.Copy)
 
-        gaps = [held([P, R // 2], F32, name) for name in ("gaps", "left2_2")]
-        steps = row("right2_2")
-        for gap, cols in zip(gaps, HALVES):
-            window = knots2[3][:].indirect(part_of(right2_t, cols))
-            nc.vector.tensor_tensor(gap[:], window, left2_3[:, cols], ALU.add)
-        for gap, cols in zip(gaps, HALVES):
-            nc.vector.tensor_tensor(steps[:, cols], gap[:], part2[:, cols], ALU.mult)
-        result = row("turned2")
+        gaps = row("turned1")
+        steps = row("steps")
+        for cols in HALVES:
+            window = knots2[2][:].indirect(part_of(right2_t, cols))
+            nc.vector.tensor_tensor(gaps[:, cols], window, left2_2[:, cols], ALU.add)
+        for cols in HALVES:
+            nc.vector.tensor_tensor(steps[:, cols], gaps[:, cols], part2[:, cols], ALU.mult)
+        result = row("turned3")
         for i, cols in enumerate(HALVES):
             total = held([P, R // 2], F32, "total%d" % i)
             nc.vector.tensor_tensor(total[:], partial[:, cols], steps[:, cols], ALU.add)
             nc.scalar.activation(result[:, cols], total[:], ACT.Abs)
-            nc.sync.dma_start(out[3 * P :, cols], result[:, cols])
+            nc.sync.dma_start(out[2 * P : 3 * P, cols], result[:, cols])

@@ -191,6 +191,24 @@ def tile_picked_ynhits_err_p_kernel(
                 stop=True,
             )
 
+        def half_product(b, acc, half):
+            cols = HALVES[half]
+            nc.tensor.matmul_mx(
+                out=acc[:, cols],
+                lhsT=h_q[b][0][:].bitcast(FP8X4),
+                lhsT_scale=h_q[b][1][:],
+                rhs=kn2_q[0][:, cols].bitcast(FP8X4),
+                rhs_scale=kn2_q[1][:, cols],
+                start=(half == 0),
+                stop=(half == 1),
+            )
+
+        def quantize_half(half):
+            cols = HALVES[half]
+            nc.vector.quantize_mx(
+                out=kn2_q[0][:, cols].bitcast(FP8X4), scales=kn2_q[1][:, cols], in_=kn2_grouped[half][:]
+            )
+
         def warm_up(acc):
             product(h_q[0], w1_q[0], acc)
 
@@ -271,67 +289,77 @@ def tile_picked_ynhits_err_p_kernel(
         knots(2, kn1_q, knots1[2], bank("work_c")[:, :G])
         interleave(kn2_first[:], kn2_grouped[0][:], nc.vector.tensor_copy)
         h_q.append(quantize(hidden[3], P, "h3"))
+        kn2_q = held([P, W], U32, "kn2_codes"), held([P, W], U8, "kn2_scales")
+        quantize_half(0)
         right1_0 = weighted(knots1[0], right1_t[:], part1, row("x_table0"))
         kn2_grouped.append(held([P, PACK * KN2_SHARE], BF16, "kn2_grouped1"))
         interleave(kn2_raw[:], kn2_grouped[1][:], lambda dst, src: nc.scalar.activation(dst, src, ACT.Copy))
         knots(3, kn1_q, knots1[3], bank("diff3")[:, :G])
+        out2_1 = bank("work_a")
+        half_product(1, out2_1, 0)
+        product(h_q[3], kn2_q, bank("sum0")[:, :G])
         sums = [bank("sum%d" % b) for b in range(BLOCKS)]
         add_turned(sums[0], true_t[0], start=True)
-
         add_turned(sums[0], right1_0)
         add_turned(sums[1], true_t[1], start=True)
+        warm_up(bank("diff3")[:, :256])
+        out2_0 = bank("diff3")
+        half_product(0, out2_0, 0)
+        add_turned(sums[2], true_t[2], start=True)
         left1_0 = weighted(knots1[0], left1_t[:], rest1, row("left1_0"))
-        kn2_q = held([P, W], U32, "kn2_codes"), held([P, W], U8, "kn2_scales")
-        for grouped, cols in zip(kn2_grouped, HALVES):
-            nc.vector.quantize_mx(out=kn2_q[0][:, cols].bitcast(FP8X4), scales=kn2_q[1][:, cols], in_=grouped[:])
+        add_turned(sums[0], left1_0)
+        quantize_half(1)
         after_kn2 = held([P, 6, R], F32, "kn2_raw")
         right1_1 = weighted(knots1[1], right1_t[:], part1, after_kn2[:, 5, :])
         left1_2 = fetched(knots1[2], left1_t[:], after_kn2[:, 3, :], -1.0)
         right1_2 = fetched(knots1[2], right1_t[:], after_kn2[:, 4, :], 1.0)
-        knots(1, kn2_q, knots2[1], bank("work_a")[:])
-        knots(0, kn2_q, knots2[0], bank("work_b")[:])
-        product(h_q[0], kn2_q, bank("diff3")[:])
-        left2_1 = fetched(knots2[1], left2_t[:], row("left2_1"), -1.0)
+        half_product(1, out2_1, 1)
+        knots_out(out2_1[:], knots2[1])
+        half_product(0, out2_0, 1)
+        knots_out(out2_0[:], knots2[0])
+        add_turned(sums[3], true_t[3], start=True)
         diff2 = bank("work_c")
         add_turned(diff2, left1_2, start=True)
+        left2_1 = fetched(knots2[1], left2_t[:], row("left2_1"), -1.0)
         add_turned(diff2, right1_2, stop=True)
-        step2 = scaled_out(diff2, 0, "step2")
-        add_turned(sums[0], left1_0)
-        right2_1 = fetched(knots2[1], right2_t[:], row("left1_0"), 1.0)
-        add_turned(sums[2], true_t[2], start=True)
         add_turned(sums[2], left1_2)
         add_turned(sums[1], right1_1)
+        step2 = scaled_out(diff2, 0, "step2")
         add_turned(sums[1], weighted(knots1[1], left1_t[:], rest1, after_kn2[:, 0, :]))
         right1_3 = weighted(knots1[3], right1_t[:], part1, after_kn2[:, 1, :])
         left1_3 = weighted(knots1[3], left1_t[:], rest1, after_kn2[:, 2, :])
-        knots(2, kn2_q, knots2[2], bank("diff3")[:])
-        knots(3, kn2_q, knots2[3], bank("work_b")[:])
-        left2_2 = fetched(knots2[2], left2_t[:], row("left2_2"), -1.0)
-        add_turned(sums[3], true_t[3], start=True)
+        knots(2, kn2_q, knots2[2], bank("work_b")[:])
+        right2_1 = fetched(knots2[1], right2_t[:], row("h2_codes"), 1.0)
         add_turned(sums[3], right1_3)
         diff1 = bank("work_a")
         add_turned(diff1, left2_1, start=True)
         add_turned(sums[1], left2_1, stop=True)
-        add_turned(diff1, right2_1, stop=True)
-        turned1 = turn_out(sums[1], ACT.Copy, "turned1")
-        spare = bank("diff3")
-        warm_up(spare[:, :512])
+        knots(3, kn2_q, knots2[3], bank("diff3")[:])
+        left2_2 = fetched(knots2[2], left2_t[:], row("h3_codes"), -1.0)
         add_turned(sums[3], left1_3)
-        add_turned(sums[0], weighted(knots2[0], left2_t[:], rest2, row("left2_0")))
-        right2_0 = weighted(knots2[0], right2_t[:], part2, row("right2_0"))
+        turned1 = turn_out(sums[1], ACT.Copy, "kn2_raw")
         partial = bank("work_c")
         add_turned(partial, step2, start=True)
+        add_turned(sums[0], weighted(knots2[0], left2_t[:], rest2, row("left2_0")))
+        right2_0 = weighted(knots2[0], right2_t[:], part2, row("right2_0"))
+        spare = bank("work_b")
+        warm_up(spare[:, :512])
+        add_turned(diff1, right2_1, stop=True)
         add_turned(sums[0], right2_0, stop=True)
         turned0 = turn_out(sums[0], ACT.Abs, "turned0")
         left2_3 = weighted(knots2[3], left2_t[:], rest2, row("left2_3"))
         right2_3 = weighted(knots2[3], right2_t[:], part2, row("right2_3"))
+        spare = bank("work_b")
+        warm_up(spare[:, :256])
         add_turned(sums[2], left2_2, stop=True)
         turned2 = turn_out(sums[2], ACT.Copy, "turned2")
+        spare = bank("diff3")
+        warm_up(spare[:, :512])
         add_turned(sums[3], left2_3)
         step1 = scaled(diff1, 1, "left2_3")
+        store(0, turn_in(turned0, bank("sum0")), ACT.Copy)
         back1 = bank("work_b")
         add_turned(back1, turned1, start=True)
-        store(0, turn_in(turned0, bank("sum0")), ACT.Copy)
         add_turned(sums[3], right2_3, stop=True)
         turned3 = turn_out(sums[3], ACT.Abs, "turned3")
         add_turned(partial, turned2, stop=True)
@@ -339,7 +367,7 @@ def tile_picked_ynhits_err_p_kernel(
         store(1, back1, ACT.Abs)
         store(3, turn_in(turned3, bank("sum3")), ACT.Copy)
 
-        gaps = row("turned1")
+        gaps = row("kn2_raw")
         steps = row("steps")
         for cols in HALVES:
             window = knots2[2][:].indirect(part_of(right2_t, cols))

from contextlib import ExitStack

import concourse.mybir as mybir
from concourse.masks import make_identity

K, T, S, H, R, G, W = 1024, 2048, 512, 512, 512, 256, 512
FLOPS = 2 * K * H * S + 2 * H * S * (G + W)

F32 = mybir.dt.float32
BF16 = mybir.dt.bfloat16
U32 = mybir.dt.uint32
I32 = mybir.dt.int32
U16 = mybir.dt.uint16
U8 = mybir.dt.uint8
FP8X4 = mybir.dt.float8_e4m3fn_x4
ACT = mybir.ActivationFunctionType
ALU = mybir.AluOpType

P = 128
PACK = 4
K_PASS = P * PACK
PASSES = K // K_PASS
BLOCKS = S // P
CHUNKS = R // P
SHARE = 88
KN2_SHARE = 256
WINDOW = R + 16
HALVES = (slice(0, R // 2), slice(R // 2, R))


def tile_picked_ynhits_err_p_kernel(
    tc, x_words, x_scales, w1, kn1, frac1, kn2, frac2, true, offs, left1, right1, left2, right2, out
):
    nc = tc.nc
    with ExitStack() as ctx:
        keep = ctx.enter_context(tc.tile_pool(name="keep", bufs=1))
        psum = ctx.enter_context(tc.psum_pool(name="psum", bufs=1))

        def held(shape, dtype, name):
            return keep.tile(shape, dtype, name=name, tag=name, align_bytes=64)

        def row(name):
            return held([P, R], F32, name)[:]

        def bank(name):
            return psum.tile([P, R], F32, name=name, tag=name, bufs=1)

        def load_list(src, name):
            lst = held([P, R // 16], U16, name)
            nc.sync.dma_start(lst[:], src)
            return lst

        def load_rows(src, width, name):
            raw = held([P, PACK, width], F32, name)
            nc.sync.dma_start(raw[:], src.rearrange("(p j) n -> p j n", j=PACK))
            return raw

        def load_words(o):
            words = held([P, T], U32, "x_table%d" % o)
            nc.sync.dma_start(words[:].bitcast(I32), x_words[o].rearrange("p n t -> p (n t)").bitcast(I32))
            return words

        def quantize(grouped, width, name):
            codes = held([P, width], U32, name + "_codes")
            scales = held([P, width], U8, name + "_scales")
            nc.vector.quantize_mx(out=codes[:].bitcast(FP8X4), scales=scales[:], in_=grouped[:])
            return codes, scales

        identity = held([P, P], F32, "identity")
        make_identity(nc, identity[:])
        x_scale_rows = held([P, T], U8, "x_table1")
        for first, last in ((32, 64), (64, P)):
            nc.vector.memset(x_scale_rows[first:last, :].bitcast(I32), 0)
        x_scale = held([P, PASSES, S], U8, "x_scale")
        nc.vector.memset(x_scale[:].rearrange("p o n -> p (o n)").bitcast(I32), 0)

        offs_t = load_list(offs, "offs_t")
        nc.sync.dma_start(x_scale_rows[:32, :].bitcast(I32), x_scales.rearrange("o q n -> q o n").bitcast(I32))
        w1_raw = [load_rows(w1[:K_PASS, :], H, "w1_raw0")]
        frac_cols = []
        for i, frac in enumerate((frac1, frac2)):
            frac_cols.append(held([P, PACK], F32, "frac_cols%d" % i))
            nc.sync.dma_start(frac_cols[i][:], frac[0].rearrange("(p j) -> p j", j=PACK))
        right1_t = load_list(right1, "right1_t")
        left1_t = load_list(left1, "left1_t")
        left2_t = load_list(left2, "left2_t")
        right2_t = load_list(right2, "right2_t")
        x_table = [load_words(0)]
        w1_raw.append(load_rows(w1[K_PASS:, :], H, "kn2_raw"))

        picked_scales = held([P, S], U8, "picked_scales")
        nc.vector.tensor_copy(picked_scales[:], x_scale_rows[:].indirect(offs_t[:]))
        for q in range(4):
            nc.sync.dma_start(
                x_scale[32 * q : 32 * q + 4].bitcast(I32),
                picked_scales[8 * q : 8 * q + 8, :].bitcast(I32),
            )
        x_table.append(load_words(1))

        knots1 = [held([P, WINDOW], F32, "knots1_%d" % b) for b in range(BLOCKS)]
        knots2 = [held([P, WINDOW], F32, "knots2_%d" % b) for b in range(BLOCKS)]
        for b in range(BLOCKS):
            nc.vector.memset(knots1[b][:, G:], 0.0)
            nc.vector.memset(knots2[b][:, W:], 0.0)

        w1_q = []
        for o in range(PASSES):
            grouped = held([P, PACK * H], BF16, "w1_grouped%d" % o)
            dst = grouped[:].rearrange("p (t m j) -> p m t j", t=PACK, j=PACK)
            src = w1_raw[o][:].rearrange("p j (m t) -> p m t j", t=PACK)
            if o == 0:
                nc.vector.tensor_copy(dst, src)
            else:
                nc.vector.tensor_copy(dst[:, :SHARE], src[:, :SHARE])
                nc.scalar.activation(dst[:, SHARE:], src[:, SHARE:], ACT.Copy)
            w1_q.append(quantize(grouped, H, "w1_%d" % o))

        kn1_raw = load_rows(kn1, G, "w1_raw0")
        kn2_first = load_rows(kn2[:, :KN2_SHARE], KN2_SHARE, "x_table0")
        kn2_raw = load_rows(kn2[:, KN2_SHARE:], W - KN2_SHARE, "kn2_raw")
        true_rows = held([P, BLOCKS, R], F32, "w1_grouped1")
        true_t = {}
        for b in range(BLOCKS):
            true_t[b] = true_rows[:, b, :]
            nc.sync.dma_start(true_t[b], true[b * P : (b + 1) * P, :])

        def spread(rate, name, spread_rows, turned_rows):
            for j in range(PACK):
                column = frac_cols[rate][:, j : j + 1]
                nc.tensor.transpose(spread_rows[:, j * P : (j + 1) * P], column.to_broadcast([P, P]), identity[:])
            part = row(name + "_part")
            rest = row(name + "_rest")
            in_order = spread_rows[:].rearrange("p (j n) -> p n j", j=PACK)
            nc.scalar.activation(part.rearrange("p (n j) -> p n j", j=PACK), in_order, ACT.Copy, scale=-1.0)
            nc.scalar.activation(rest.rearrange("p (n j) -> p n j", j=PACK), in_order, ACT.Copy, bias=-1.0)
            for c in range(CHUNKS):
                cols = slice(c * P, (c + 1) * P)
                nc.tensor.transpose(turned_rows[:, cols], part[:, cols], identity[:])
            turned = row(name + "_turned")
            nc.scalar.copy(turned, turned_rows[:])
            return part, rest, turned

        part1, rest1, turned_part1 = spread(0, "frac1", bank("work_a"), bank("work_c"))
        part2, rest2, turned_part2 = spread(1, "frac2", bank("work_b"), bank("diff3"))
        turned_part = [turned_part1, turned_part2]

        x_codes = [[] for o in range(PASSES)]
        for o, pieces in enumerate(((2, 2), (1, 1, 2))):
            for blocks in pieces:
                first = len(x_codes[o])
                picked = held([P, blocks * P], U32, "x_codes%d_%d" % (o, first))
                cols = slice(first * P // 16, (first + blocks) * P // 16)
                nc.vector.tensor_copy(picked[:], x_table[o][:].indirect(offs_t[:, cols]))
                x_codes[o].extend(picked[:, i * P : (i + 1) * P] for i in range(blocks))

        def interleave(raw, grouped, engine_copy):
            engine_copy(
                grouped.rearrange("p (c i j) -> p c j i", i=PACK, j=PACK),
                raw.rearrange("p j (c i) -> p c j i", i=PACK),
            )

        def hidden_pass(b, o, acc):
            for t in range(PACK):
                nc.tensor.matmul_mx(
                    out=acc[:, t * P : (t + 1) * P],
                    lhsT=w1_q[o][0][:, t * P : (t + 1) * P].bitcast(FP8X4),
                    lhsT_scale=w1_q[o][1][:, t * P : (t + 1) * P],
                    rhs=x_codes[o][b].bitcast(FP8X4),
                    rhs_scale=x_scale[:, o, b * P : (b + 1) * P],
                    start=(o == 0 and t == 0),
                    stop=(o == PASSES - 1 and t == PACK - 1),
                )

        def hidden_block(b, acc):
            hidden_pass(b, PASSES - 1, acc)
            hidden = held([P, PACK * P], BF16, "hidden%d" % b)
            nc.scalar.activation(
                hidden[:].rearrange("p (n t) -> p n t", t=PACK), acc[:].rearrange("p (t n) -> p n t", t=PACK), ACT.Relu
            )
            return hidden

        def product(stationary, moving, acc):
            width = acc.shape[1]
            nc.tensor.matmul_mx(
                out=acc,
                lhsT=stationary[0][:].bitcast(FP8X4),
                lhsT_scale=stationary[1][:],
                rhs=moving[0][:, :width].bitcast(FP8X4),
                rhs_scale=moving[1][:, :width],
                start=True,
                stop=True,
            )

        def half_product(b, acc, half):
            cols = HALVES[half]
            nc.tensor.matmul_mx(
                out=acc[:, cols],
                lhsT=h_q[b][0][:].bitcast(FP8X4),
                lhsT_scale=h_q[b][1][:],
                rhs=kn2_q[0][:, cols].bitcast(FP8X4),
                rhs_scale=kn2_q[1][:, cols],
                start=(half == 0),
                stop=(half == 1),
            )

        def quantize_half(half):
            cols = HALVES[half]
            nc.vector.quantize_mx(
                out=kn2_q[0][:, cols].bitcast(FP8X4), scales=kn2_q[1][:, cols], in_=kn2_grouped[half][:]
            )

        def warm_up(acc):
            product(h_q[0], w1_q[0], acc)

        def knots_out(acc, window):
            nc.scalar.copy(window[:, : acc.shape[1]], acc)

        def knots(b, kn_q, window, acc):
            product(h_q[b], kn_q, acc)
            knots_out(acc, window)

        def add_turned(total, term, start=False, stop=False):
            for c in range(CHUNKS):
                cols = slice(c * P, (c + 1) * P)
                nc.tensor.matmul(
                    total[:, cols], term[:, cols], identity[:], is_transpose=True,
                    start=(start and c == 0), stop=(stop and c == CHUNKS - 1),
                )

        def part_of(lst, cols):
            return lst[:, cols.start // 16 : cols.stop // 16]

        def weighted(window, lst, weight, term):
            nc.vector.tensor_tensor(term, window[:].indirect(lst), weight, ALU.mult)
            return term

        def fetched(window, lst, plain, sign):
            nc.scalar.activation(plain, window[:].indirect(lst), ACT.Copy, scale=sign)
            return plain

        def leave(dst, src, func):
            if func == ACT.Copy:
                nc.scalar.copy(dst, src)
            else:
                nc.scalar.activation(dst, src, func)

        def turn_out(total, func, name):
            turned = row(name)
            leave(turned, total[:], func)
            return turned

        def scaled(diff, rate, name):
            step = row(name)
            nc.vector.tensor_tensor(step, diff[:], turned_part[rate], ALU.mult)
            return step

        def scaled_out(diff, rate, name):
            step = row(name)
            for c in range(CHUNKS):
                cols = slice(c * P, (c + 1) * P)
                weight = turned_part[rate][:, c * P : c * P + 1]
                nc.scalar.activation(step[:, cols], diff[:, cols], ACT.Copy, scale=weight)
            return step

        def turn_in(turned, back):
            for c in range(CHUNKS):
                cols = slice(c * P, (c + 1) * P)
                nc.tensor.transpose(back[:, cols], turned[:, cols], identity[:])
            return back

        def store(b, back, func):
            result = row("result%d" % b)
            leave(result, back[:], func)
            nc.sync.dma_start(out[b * P : (b + 1) * P, :], result)

        kn1_grouped = held([P, PACK * G], BF16, "kn1_grouped")
        interleave(kn1_raw[:], kn1_grouped[:], nc.vector.tensor_copy)
        before_relu = [bank("sum%d" % b) for b in range(BLOCKS)]
        for b in range(BLOCKS):
            hidden_pass(b, 0, before_relu[b])
        hidden = [hidden_block(b, before_relu[b]) for b in range(BLOCKS)]
        h_q = [quantize(hidden[0], P, "h0")]
        kn1_q = quantize(kn1_grouped, G, "kn1")
        h_q.append(quantize(hidden[1], P, "h1"))
        knots(0, kn1_q, knots1[0], bank("work_a")[:, :G])
        knots(1, kn1_q, knots1[1], bank("work_b")[:, :G])
        kn2_grouped = [held([P, PACK * KN2_SHARE], BF16, "kn2_grouped")]
        h_q.append(quantize(hidden[2], P, "h2"))
        knots(2, kn1_q, knots1[2], bank("work_c")[:, :G])
        interleave(kn2_first[:], kn2_grouped[0][:], nc.vector.tensor_copy)
        h_q.append(quantize(hidden[3], P, "h3"))
        kn2_q = held([P, W], U32, "kn2_codes"), held([P, W], U8, "kn2_scales")
        quantize_half(0)
        right1_0 = weighted(knots1[0], right1_t[:], part1, row("x_table0"))
        kn2_grouped.append(held([P, PACK * KN2_SHARE], BF16, "kn2_grouped1"))
        interleave(kn2_raw[:], kn2_grouped[1][:], lambda dst, src: nc.scalar.activation(dst, src, ACT.Copy))
        knots(3, kn1_q, knots1[3], bank("diff3")[:, :G])
        out2_1 = bank("work_a")
        half_product(1, out2_1, 0)
        product(h_q[3], kn2_q, bank("sum0")[:, :G])
        sums = [bank("sum%d" % b) for b in range(BLOCKS)]
        add_turned(sums[0], true_t[0], start=True)
        add_turned(sums[0], right1_0)
        add_turned(sums[1], true_t[1], start=True)
        warm_up(bank("diff3")[:, :256])
        out2_0 = bank("diff3")
        half_product(0, out2_0, 0)
        add_turned(sums[2], true_t[2], start=True)
        left1_0 = weighted(knots1[0], left1_t[:], rest1, row("left1_0"))
        add_turned(sums[0], left1_0)
        quantize_half(1)
        after_kn2 = held([P, 6, R], F32, "kn2_raw")
        right1_1 = weighted(knots1[1], right1_t[:], part1, after_kn2[:, 5, :])
        left1_2 = fetched(knots1[2], left1_t[:], after_kn2[:, 3, :], -1.0)
        right1_2 = fetched(knots1[2], right1_t[:], after_kn2[:, 4, :], 1.0)
        half_product(1, out2_1, 1)
        knots_out(out2_1[:], knots2[1])
        half_product(0, out2_0, 1)
        knots_out(out2_0[:], knots2[0])
        add_turned(sums[3], true_t[3], start=True)
        diff2 = bank("work_c")
        add_turned(diff2, left1_2, start=True)
        left2_1 = fetched(knots2[1], left2_t[:], row("left2_1"), -1.0)
        add_turned(diff2, right1_2, stop=True)
        add_turned(sums[2], left1_2)
        add_turned(sums[1], right1_1)
        step2 = scaled_out(diff2, 0, "step2")
        add_turned(sums[1], weighted(knots1[1], left1_t[:], rest1, after_kn2[:, 0, :]))
        right1_3 = weighted(knots1[3], right1_t[:], part1, after_kn2[:, 1, :])
        left1_3 = weighted(knots1[3], left1_t[:], rest1, after_kn2[:, 2, :])
        knots(2, kn2_q, knots2[2], bank("work_b")[:])
        right2_1 = fetched(knots2[1], right2_t[:], row("h2_codes"), 1.0)
        add_turned(sums[3], right1_3)
        diff1 = bank("work_a")
        add_turned(diff1, left2_1, start=True)
        add_turned(sums[1], left2_1, stop=True)
        knots(3, kn2_q, knots2[3], bank("diff3")[:])
        left2_2 = fetched(knots2[2], left2_t[:], row("h3_codes"), -1.0)
        add_turned(sums[3], left1_3)
        turned1 = turn_out(sums[1], ACT.Copy, "kn2_raw")
        partial = bank("work_c")
        add_turned(partial, step2, start=True)
        add_turned(sums[0], weighted(knots2[0], left2_t[:], rest2, row("left2_0")))
        right2_0 = weighted(knots2[0], right2_t[:], part2, row("right2_0"))
        spare = bank("work_b")
        warm_up(spare[:, :512])
        add_turned(diff1, right2_1, stop=True)
        add_turned(sums[0], right2_0, stop=True)
        turned0 = turn_out(sums[0], ACT.Abs, "turned0")
        left2_3 = weighted(knots2[3], left2_t[:], rest2, row("left2_3"))
        right2_3 = weighted(knots2[3], right2_t[:], part2, row("right2_3"))
        spare = bank("work_b")
        warm_up(spare[:, :256])
        add_turned(sums[2], left2_2, stop=True)
        turned2 = turn_out(sums[2], ACT.Copy, "turned2")
        spare = bank("diff3")
        warm_up(spare[:, :512])
        add_turned(sums[3], left2_3)
        step1 = scaled(diff1, 1, "left2_3")
        store(0, turn_in(turned0, bank("sum0")), ACT.Copy)
        back1 = bank("work_b")
        add_turned(back1, turned1, start=True)
        add_turned(sums[3], right2_3, stop=True)
        turned3 = turn_out(sums[3], ACT.Abs, "turned3")
        add_turned(partial, turned2, stop=True)
        add_turned(back1, step1, stop=True)
        store(1, back1, ACT.Abs)
        store(3, turn_in(turned3, bank("sum3")), ACT.Copy)

        gaps = row("kn2_raw")
        steps = row("steps")
        for cols in HALVES:
            window = knots2[2][:].indirect(part_of(right2_t, cols))
            nc.vector.tensor_tensor(gaps[:, cols], window, left2_2[:, cols], ALU.add)
        for cols in HALVES:
            nc.vector.tensor_tensor(steps[:, cols], gaps[:, cols], part2[:, cols], ALU.mult)
        result = row("turned3")
        for i, cols in enumerate(HALVES):
            total = held([P, R // 2], F32, "total%d" % i)
            nc.vector.tensor_tensor(total[:], partial[:, cols], steps[:, cols], ALU.add)
            nc.scalar.activation(result[:, cols], total[:], ACT.Abs)
            nc.sync.dma_start(out[2 * P : 3 * P, cols], result[:, cols])
